import numpy as np, ml_dtypes
CORES = [24,25,26,27,28,29,30,31]
N = 8
BF = ml_dtypes.bfloat16
W, NB, L, E, T, LIM, HOP, STR = 4096, 512, 512, 1024, 4, 2, 3, 8
def among(rng, m, *s):
    i = rng.integers(0, m.shape[1], (N, 8) + s)
    return m[np.arange(8).reshape((1, 8) + (1,) * len(s)), i]
def parts(rng):
    rate = np.array([0.3, 0.6, 0.8, 0.93])[(np.arange(W) >> 4) & 3]
    rec = np.where(rng.random((N, 8, 16, W)) < rate, 9, rng.integers(0, 4, (N, 8, 16, W)))
    ver = rng.integers(0, W // 64, (N, 8, 16, NB)) * 64 + rng.integers(0, 3, (N, 8, 1, NB)) * 16 + rng.integers(0, 16, (N, 8, 16, NB))
    hot = rng.integers(0, W // 64, (8, 24)) * 64 + 48 + rng.integers(0, 16, (8, 24)); hb = rng.integers(0, NB, (8, 48)); s = (N, 8, 16, NB)
    known = np.where(rng.random(s) < 0.5, among(rng, hot, 16, NB), rng.integers(0, W // 64, s) * 64 + 48 + rng.integers(0, 16, s))
    stub = W + np.where(rng.random(s) < 0.5, among(rng, hb, 16, NB), rng.integers(0, NB, s))
    edge = np.where(rng.random(s) < 0.4, known, stub)
    eff = rng.integers(0, 4, (N, 8, 16, E)) * rng.integers(0, 2, (N, 8, 16, E)); x = rng.integers(0, 4, (N, 8, 16, L))
    v = np.where(rng.random((N, 8, L)) < 0.5, among(rng, hot, L), rng.integers(0, W, (N, 8, L)))
    return rec, ver, edge, eff, x, v
def own(rng, a, g, dd, lo=0):
    rec, ver, edge, eff, x, v = a; i = np.arange(L)
    v[:, g] = i; edge[:, g, :, :L] = W + i
    ver[:, g, :, :L] = STR * i + (np.arange(16)[:, None] + rng.integers(0, STR)) % STR
    far = np.argsort(rng.random((N, 16 - lo, L, STR)), axis=1) < dd.reshape(N, 1, L, -1); xx = x[:, g][:, :, :, None]
    far = np.concatenate([np.zeros((N, lo, L, STR), bool), far], axis=1)
    rec[:, g] = np.where(far, (xx + rng.integers(1, 4, far.shape)) & 3, xx).reshape(N, 16, W)
def two(a, g):
    rec, ver, edge, eff, x, v = a
    x[:, g] = 0; x[1::2, g, :LIM + 1] = 1; eff[:, g] = 0
def pack(a):
    rec, ver, edge, eff, x, v = [np.ascontiguousarray(z) for z in a]
    return {"rec0": rec.reshape(N, 128, W).astype(BF), "ver0": ver.reshape(N, 128, NB).astype(np.int32), "edge0": edge.reshape(N, 128, NB).astype(np.int32),
            "eff": eff.reshape(N, 128, E).astype(BF), "x0": x.reshape(N, 128, L).astype(BF), "v0": v.astype(np.int32)}
def setup_inputs(rng):
    return pack(parts(rng))
def skew(rng, hi, *s):
    e = rng.choice(np.array([1.0, 3.0, 8.0]), (N, 8) + (1,) * len(s))
    return np.minimum(((hi + 1) * rng.random((N, 8) + s) ** e).astype(np.int64), hi)
def setup_inputs_spread(rng):
    ex = rng.choice(np.array([0.5, 1.0, 2.0, 4.0]), (1, 8, 16, 1))
    val = np.minimum((4 * rng.random((N, 8, 16, W)) ** ex).astype(np.int64), 3)
    rec = np.where(rng.random((N, 8, 16, W)) < 0.75 * rng.random((N, 8, 1, W)), 9, val)
    x = np.minimum((4 * rng.random((N, 8, 16, L)) ** ex).astype(np.int64), 3)
    edge = np.where(rng.random((N, 8, 16, NB)) < rng.choice(np.array([0.1, 0.4, 0.7]), (N, 8, 1, 1)), skew(rng, W - 1, 16, NB), W + skew(rng, NB - 1, 16, NB))
    return pack((rec, skew(rng, W - 1, 16, NB), edge, skew(rng, 3, 16, E), x, skew(rng, W - 1, L)))
def end(rng, lo, hi, *s):
    return np.where(rng.random((N, 8) + s) < 0.5, lo, hi)
def setup_inputs_ends(rng):
    rec = end(rng, 0, 9, 16, W); ver = end(rng, 0, W - 1, 16, NB); edge = end(rng, 0, W + NB - 1, 16, NB); eff = end(rng, 0, 3, 16, E); x = end(rng, 0, 3, 16, L); v = end(rng, 0, W - 1, L)
    for g in (1, 3, 5):
        ver[:, g] = np.where(rng.random((N, 16, NB)) < 0.3, rng.integers(0, W, (N, 16, NB)), ver[:, g])
        edge[:, g] = np.where(rng.random((N, 16, NB)) < 0.3, rng.integers(0, W + NB, (N, 16, NB)), edge[:, g])
        v[:, g] = np.where(rng.random((N, L)) < 0.3, rng.integers(0, W, (N, L)), v[:, g])
    for g in (0, 7):
        rec[:, g, :, 0] = 0; rec[:, g, :, W - 1] = 0
        m = rng.random((N, 1, L)); x[:, g] = np.where(m < 0.25, 3, np.where(m < 0.5, 0, x[:, g]))
        x[:, g, :, L - 1] = 3; v[:, g, L - 1] = W - 1
    edge[:, 7, :, NB - 1] = W + NB - 1; edge[:, 7, :, 0] = 0
    x[N - 1, 7] = 0; x[N - 1, 7, :, L - 1] = 3
    return pack((rec, ver, edge, eff, x, v))
def setup_inputs_corners(rng):
    a = parts(rng); rec, ver, edge, eff, x, v = a
    ver[:, 0] = 0; ver[:, 1] = W - 1; rec[:, 1, :, W - 1] = rng.integers(0, 4, (N, 16))
    v[:, 2] = rng.integers(0, NB, (N, L)); edge[:, 2] = np.arange(NB); rec[:, 2, :, ::2] = 9
    edge[:, 3] = W + rng.integers(0, NB, (N, 16, NB)); ver[:, 3] = ver[:, 3] // STR * STR + rng.integers(0, T, (N, 16, NB)) * rng.integers(0, 2, (N, 16, NB))
    v[:, 3] = STR * np.argsort(rng.random((N, L)), axis=1) + rng.integers(0, 2, (N, L)) * rng.integers(0, T, (N, L))
    dd = np.repeat(rng.choice(np.array([0, 1, LIM, LIM + 1, LIM + 2, 16]), (N, L, 1)), STR, axis=2)
    dd[:, 3::4] = 16; dd[:, 3::4, STR - 1] = 15
    own(rng, a, 4, dd)
    i = np.arange(3, L, 4); kk = np.arange(16)[:, None]; p = np.where(rng.random((N, 1, len(i))) < 0.5, 15, rng.integers(0, 16, (N, 1, len(i))))
    ver[:, 4, :, 3:L:4] = np.where(kk == p, STR * i + STR - 1, STR * i + kk % (STR - 1))
    edge[:, 5] = W + rng.choice(np.array([0, NB - 1]), (N, 16, NB)); rec[:, 5, :, 0] = 9
    two(a, 6); own(rng, a, 6, rng.integers(0, LIM + 1, (N, L)), LIM + 1)
    fit = np.where((rng.random((N, 16, L + 1)) < 0.3) & (kk > LIM), 9, x[:, 6, :, :1])
    rec[:, 6, :, ::STR] = fit[:, :, :L]; rec[:, 6, :, W - 1] = fit[:, :, L]
    edge[:, 6] = np.where(rng.random((N, 16, NB)) < 0.5, rng.choice(np.array([0, W - 1]), (N, 16, NB)), STR * rng.integers(0, L, (N, 16, NB)))
    edge[1::2, 6, :, L - 1] = W + L - 1
    rec[:, 7] = rng.integers(0, 4, (N, 16, W))
    return pack(a)
def setup_inputs_crowd(rng):
    a = parts(rng); rec, ver, edge, eff, x, v = a; full = np.full((N, L), 16); less = full.copy(); less[:, L - 1] = 0
    soft = rng.integers(1, LIM + 1, (N, L)); soft[1::2, L - 1] = 0
    rec[:, 2:7] = np.where(rng.random((N, 5, 16, W)) < 0.5, 9, rng.integers(0, 4, (N, 5, 16, W)))
    two(a, 0); two(a, 1); two(a, 7)
    own(rng, a, 0, soft, LIM + 1); own(rng, a, 1, less); own(rng, a, 7, full)
    edge[:, 2:4] = W + rng.integers(0, NB, (N, 2, 16, NB))
    x[:, 2] = x[:, 2, :, :1].copy(); v[:, 2] = v[:, 2, :1].copy()
    x[:, 3, :, :L - 1] = x[:, 3, :, :1].copy(); v[:, 3, :L - 1] = v[:, 3, :1].copy()
    v[:, 4] = v[:, 4, :1].copy(); edge[:, 4] = W + rng.integers(0, NB, (N, 1, 1))
    edge[:, 5] = W + NB - 1; v[:, 5] = np.argsort(rng.random((N, W)), axis=1)[:, :L]
    v[:, 6] = np.arange(L); edge[:, 6, :, :L] = W + np.arange(L); ver[:, 6] = W - 1; ver[:, 6, :, L - 1] = 5
    return pack(a)
def check_inputs(d):
    bad = []
    for k, lo, hi in (("rec0", 0, 9), ("ver0", 0, W - 1), ("edge0", 0, W + NB - 1), ("eff", 0, 3), ("x0", 0, 3), ("v0", 0, W - 1)):
        a = np.asarray(d[k]).astype(np.float64)
        if not (np.min(a) >= lo and np.max(a) <= hi and np.all(a == np.floor(a))): bad.append("range of " + k)
    a = np.asarray(d["rec0"]).astype(np.float64)
    if np.any((a > 3) & (a < 9)): bad.append("rec0 holds a number between 3 and 9")
    return bad
def reference(rec0, ver0, edge0, eff, x0, v0):
    R = np.asarray(rec0).astype(np.int32).reshape(N, 8, 16, W); V = np.asarray(ver0).astype(np.int32).reshape(N, 8, 16, NB)
    S = np.tile(np.asarray(edge0).astype(np.int32).reshape(N, 8, 16, NB), (1, 1, 1, W // NB)); ef = np.asarray(eff).astype(np.int32).reshape(N, 8, 16, E)
    x = np.asarray(x0).astype(np.int32).reshape(N, 8, 16, L); v = np.asarray(v0).astype(np.int32); A = np.zeros((N, 8), np.int32)
    lane = np.arange(L); low = lane[None, :] < lane[:, None]; wt = (2 * np.arange(16) + 1)[:, None]
    for t in range(T):
        for q in range(N):
            r = (q - HOP * t) % N
            for g in range(8):
                Rg, Vg, Sg, xx, vv = R[q, g], V[q, g], S[q, g], x[r, g], v[r, g].copy()
                j = np.sum(wt * xx, axis=0) & 15; w = Sg[j, vv]; rw = Rg[:, w & (W - 1)]
                known = (w < W) & ~np.any((rw != xx) & (rw != 9), axis=0)
                b = w & (NB - 1); ver = Vg[:, b]; old = Rg[:, ver]
                mis = np.sum((old != xx[:, None, :]) & (old != 9), axis=0); k = np.argmin(mis, axis=0)
                d = mis[k, lane]; c = ver[k, lane]
                want = ~known & (d > 0)
                clash = low & want[None, :] & ((b[:, None] == b[None, :]) | (c[:, None] == c[None, :]))
                may = want & ~np.any(clash, axis=1)
                gen = may & (d <= LIM + (A[q, g] & 1)); cl = may & ~gen
                rc = Rg[:, c]; new = np.where(rc == xx, rc, 9); n = STR * lane + t
                eat = np.all((new[:, None, :] == 9) | (old == new[:, None, :]), axis=0)
                vn = np.where(known, w, np.where(cl, n, c)); sc = W + (Sg[:, c] & (NB - 1))
                Rg[:, c[gen]] = new[:, gen]; Rg[:, n[cl]] = xx[:, cl]
                Vg[:, b[gen]] = np.where(eat, c[None, :], ver)[:, gen]; Vg[(lane[cl] + t) & 15, b[cl]] = n[cl]
                Sg[:, n[cl]] = sc[:, cl]
                first = ~np.any(low & (vv[:, None] == vv[None, :]), axis=1)
                Sg[j[first], vv[first]] = vn[first]
                x[r, g] = (xx + ef[q, g][:, vn & (E - 1)]) & 3; v[r, g] = vn; A[q, g] = np.count_nonzero(cl)
    return {"yr": R.reshape(N, 128, W).astype(np.float32).astype(BF), "yl": V.reshape(N, 128, NB).astype(np.float32), "ys": np.sum(S, axis=2).astype(np.float32),
            "yx": x.reshape(N, 128, L).astype(np.float32).astype(BF), "yv": v.astype(np.float32)}

@@ -1,0 +1,712 @@
+from concourse.mybir import AluOpType as ALU, AxisListType as AX, ActivationFunctionType as AF
+
+SCRATCH = {}
+
+
+def _decl(where, dtype, spec):
+    for item in spec.split():
+        name, cols = item.split(":")
+        SCRATCH[name] = (where, [128, int(cols)], dtype)
+
+
+_decl("psum", "float32", "B0:512 B1:512 B2:512 B3:512 B4:512 B5:512 B6:512 B7:512")
+_decl("sbuf", "bfloat16", "EF:4096 G:8192 EQ:8192 MK:784 onesw:144 ones960:144 jw:144 jw4:144 hn:512 yu:512 hu:512 bk:1024 "
+      "idb:128 neg2:128 blk:128 ones:128 wexp:512 we:24 wg:8 seld:2048 x0b:512 x1b:512 x2b:512 x3b:512 x4b:512 "
+      "xo0:512 xo1:512 xo2:512 xo3:512 mask0:512 mask1:512 nmask:512 gw:512 eqw:512 eqd:512 eqv:256 tvf:512 tcf:512 tbf:512 rc:512 "
+      "eqc:512 z:512 efg:512 sg:512 ntg:32 cl:32")
+_decl("sbuf", "float32", "R:4608 SU:4608 VL:1024 TT:5632 TV:4608 IOTA:4096 cv:1024 gk:512 am:256 oneswf:144 ow2:144 idf:128 ids:128 lw:240 "
+      "sc0:128 col:32 sm:1280 base5:160 del5:160 prod5:160 sum5:160 mn2:64 dum2:64 sel:512 verf:512 keyl:512 scan:512 expd:256 val:512 "
+      "x32:512 scf:512 dv:512 dm:512 vm:512 pg:512 tmpf:128")
+_decl("sbuf", "int32", "smi:256 coli:32 di:512 ei:1024 sci:512")
+_decl("sbuf", "uint16", "v0u:64 v1u:64 v2u:64 v3u:64 v4u:64 of0:160 of1:160 of2:160 of3:160 smu:224 veru:512 ofcb:64 ofb:64 ofv:64 exu:16")
+_decl("sbuf", "float16", "dif:1024 idh:128 key2:64 keyv:32 w8:144 v0h:512")
+
+DMASEMS = ["dx", "dv0", "de", "dver", "dr0", "dr1", "dr2", "dr3", "deff", "dsu", "dtt", "dtv", "out"]
+SEMAPHORES = ["pe", "act", "dve", "pool", "sent"] + DMASEMS + ["ax%d" % t for t in range(1, 5)] + ["av%d" % t for t in range(1, 5)]
+NSTEP, HOP, BIGW = 4, 3, 262144.0
+CYC, PEC, GATH, SCAT, FIX, WAKE = 0.00083, 0.0006, 1.56, 3.8, 0.05, 0.06
+ORDER = {}
+OPT = {"split": False, "nv1": 20, "nv2": 10, "rounds": 4, "halves": (), "xc": 0, "gw": 0,
+       "between": ("", "hn", "", "snc"), "tail": "tc tv sn ef sg mask xo rg rn"}
+
+
+def schedule(ops):
+    n = len(ops)
+    pred = [[] for _ in range(n)]
+    succ = [[] for _ in range(n)]
+    for k, o in enumerate(ops):
+        for i in o["all"]:
+            p = ops[i]
+            free = i not in o["need"] or (p["e"] == "pe" and o["e"] == "pe")
+            gap = 0.0 if free else p["lat"] + WAKE
+            pred[k].append((i, gap))
+            succ[i].append((k, gap))
+    left = [len(p) for p in pred]
+    topo_order = [i for i in range(n) if not left[i]]
+    for i in topo_order:
+        for k, _ in succ[i]:
+            left[k] -= 1
+            if not left[k]:
+                topo_order.append(k)
+    assert len(topo_order) == n
+
+    def place(seq, before, back):
+        busy, start = {}, [0.0] * n
+        for i in seq:
+            c, e = ops[i]["cost"], ops[i]["e"]
+            t = max([start[j] + ops[j]["cost"] + gp for j, gp in before[i]] + [ops[i]["lat"] if back else 0.0])
+            if e is not None:
+                lst = busy.setdefault(e, [])
+                lo, hi = 0, len(lst)
+                while lo < hi:
+                    mid = (lo + hi) // 2
+                    if lst[mid][1] <= t + 1e-9:
+                        lo = mid + 1
+                    else:
+                        hi = mid
+                while lo < len(lst) and lst[lo][0] < t + c - 1e-9:
+                    t = max(t, lst[lo][1])
+                    lo += 1
+                lst.insert(lo, (t, t + c))
+            start[i] = t
+        return start
+
+    prio = [0.0] * n
+    for i in reversed(topo_order):
+        prio[i] = ops[i]["cost"] + max([prio[k] + gp for k, gp in succ[i]] + [ops[i]["lat"]])
+    load = [bool(o["dma"]) and not o["rd"] and not o["ext"] for o in ops]
+    rank_in = {i: m for m, i in enumerate(topo_order)}
+    seq = sorted(range(n), key=lambda i: (not load[i], i if load[i] else -prio[i], rank_in[i]))
+    best = None
+    for _ in range(OPT["rounds"]):
+        st = place(seq, pred, False)
+        span = max(st[i] + ops[i]["cost"] + ops[i]["lat"] for i in range(n))
+        rank_in = {i: m for m, i in enumerate(seq)}
+        if best is None or span < best[0]:
+            best = (span, sorted(range(n), key=lambda i: (st[i], rank_in[i])))
+        back = sorted(range(n), key=lambda i: (-(st[i] + ops[i]["cost"]), -rank_in[i]))
+        sb = place(back, succ, True)
+        rank_in = {i: m for m, i in enumerate(back)}
+        seq = sorted(range(n), key=lambda i: (not load[i], i if load[i] else -(sb[i] + ops[i]["cost"]), -rank_in[i]))
+    ORDER["span"] = best[0]
+    return best[1]
+
+
+def rank_program(g, core, T, topo):
+    rank = T.rank_of(core)
+    if rank is None:
+        return
+    n_r = len(T.cores)
+    ops, tags = [], {}
+    Q = {"pe": g.tensor, "act": g.scalar, "dve": g.vector, "pool": g, "sp": g.sync}
+
+    def A(name, a=None, b=None, s=None, key=None, p=None):
+        keys = [name] if key is None else [name + "#" + str(k) for k in (key if isinstance(key, list) else [key])]
+        n = len(range(SCRATCH[name][1][1])[slice(a, b, s)])
+        return (T[name][slice(None) if p is None else p, slice(a, b, s)], keys, [], n, name, False)
+
+    def IN(win, off):
+        return (win[0].indirect(off[0]), win[1], off[1], 16 * off[3], win[4], True)
+
+    def op(e, fn, outs, ins, cost, dma=None, ext=None, lat=0.0, after=()):
+        rd, wr = [], []
+        for o in outs:
+            wr += o[1]
+            rd += o[2]
+        for i in ins:
+            if isinstance(i, tuple):
+                rd += i[1] + i[2]
+        ops.append({"e": e, "fn": fn, "rd": rd, "wr": wr, "dma": dma, "ext": ext, "inc": False, "cost": cost, "lat": lat, "after": list(after), "n": 16})
+
+    def tag(name):
+        tags.setdefault(name, []).append(len(ops) - 1)
+
+    def est(o, ins, two=False, fast=True):
+        n = max(o[3], ins[0][3]) if ins else o[3]
+        if o[5]:
+            return FIX + n * SCAT * CYC
+        if ins and ins[0][5]:
+            return FIX + n * GATH * CYC
+        r = 2 if two else 0.5 if fast and all(SCRATCH[x[4]][2].endswith("16") for x in [o] + ins) else 1
+        return FIX / 2 + max(64, n * r) * CYC
+
+    def u(x):
+        return x[0] if isinstance(x, tuple) else x
+
+    def cp(o, i):
+        op("dve", lambda: g.vector.tensor_copy(o[0], i[0]), [o], [i], est(o, [i]))
+
+    def tt(o, a, b, alu):
+        two = SCRATCH[a[4]][0] == SCRATCH[b[4]][0]
+        op("dve", lambda: g.vector.tensor_tensor(o[0], a[0], b[0], alu), [o], [a, b], est(o, [a, b], two, False))
+
+    def ts(o, a, s1, op0, s2=None, op1=None):
+        if op1 is None:
+            op("dve", lambda: g.vector.tensor_scalar(o[0], a[0], u(s1), None, op0), [o], [a, s1], est(o, [a]))
+        else:
+            op("dve", lambda: g.vector.tensor_scalar(o[0], a[0], u(s1), u(s2), op0, op1), [o], [a, s1, s2], est(o, [a]))
+
+    def ms(o, c):
+        op("dve", lambda: g.vector.memset(o[0], c), [o], [], est(o, []))
+
+    def scan(o, a, b, init, op0, op1):
+        op("dve", lambda: g.vector.tensor_tensor_scan(o[0], a[0], b[0], init, op0, op1), [o], [a, b], est(o, [a]))
+
+    def red(o, a):
+        op("dve", lambda: g.vector.tensor_reduce(o[0], a[0], AX.X, ALU.add), [o], [a], est(o, [a]))
+
+    def act(name, o, i, f, bias=None, scale=None):
+        kw = {}
+        if bias is not None:
+            kw["bias"] = u(bias)
+        if scale is not None:
+            kw["scale"] = scale
+        op("act", lambda: g.scalar.activation(o[0], i[0], f, **kw), [o], [i, bias], 0.015 + est(o, [i], fast=False))
+        tag(name)
+
+    def mm(o, l, r, start, stop):
+        c = max(64, r[3]) * (4 if SCRATCH[l[4]][2] == "float32" else 1) * PEC
+        op("pe", lambda: g.tensor.matmul(o[0], l[0], r[0], start, stop), [o], [l, r], c)
+
+    def iota(o, pat, base=0, cm=0, flt=True, after=()):
+        c = 0.13 + 2 * o[3] * CYC
+        if flt:
+            op("pool", lambda: g.iota(o[0], pat, base, cm, allow_small_or_imprecise_dtypes=True), [o], [], c, after=after)
+        else:
+            op("pool", lambda: g.iota(o[0], pat, base, cm), [o], [], c)
+
+    def asel(o, i, pat, cmp, fill, base, cm):
+        op("pool", lambda: g.affine_select(o[0], i[0], pat, cmp, fill, base, cm), [o], [i], 0.17 + 2 * o[3] * CYC)
+
+    queue_tail = {}
+
+    def dma(e, o, i, sem, lat=3.0):
+        op(e, lambda: Q[e].dma_start(o[0], i[0]), [o], [i], 0.1, dma=sem, lat=lat, after=queue_tail.get(e, ()))
+        queue_tail[e] = (len(ops) - 1,)
+
+    def send(src, dname, dst, sem, lat):
+        rid, pid, _ = topo.addr(dst)
+        m = topo.mask(core, dst)
+        op("pool", lambda: g.remote_dma(T[dname][:], src[0], T.sem[sem], T.sem["sent"], pid, rid, m), [], [src], 0.5, ext="send")
+        ops[-1]["n"] = len(topo.engines(core, dst))
+        return (len(ops) - 1, lat)
+
+    def arrive(name, sem, src, sent):
+        op(None, None, [A(name)], [], 0.0, dma=sem, ext="arr", lat=sent[1], after=(sent[0],))
+        ops[-1]["n"] = len(topo.engines(src, core))
+
+    def f2w(o, wide, src, first=True, last=True, p=None):
+        for p0 in range(16):
+            mm(o, A(wide, 16 - p0, 144 - p0, p=p), A(src, p0, 512, 16, p=p), first and p0 == 0, last and p0 == 15)
+
+    H = lambda name: (T[name][:], [], [])
+    C = lambda j: A("col", j, j + 1, key=j)
+    S = lambda j: A("sm", 32 * j, 32 * j + 32, key=j)
+    SI = lambda j: A("smi", 32 * j, 32 * j + 32, key=j)
+    SUU = lambda j: A("smu", 32 * j, 32 * j + 32, key=j)
+    P5 = lambda nm, q: A(nm, 32 * q, 32 * q + 32, key=q)
+    TM = lambda j: A("tmpf", 8 * j, 8 * j + 8, key=j)
+    RQ = lambda q: A("EQ", 1024 * q, 1024 * q + 1024, key="r%d" % q)
+    eq, ne, ge, lt = ALU.is_equal, ALU.not_equal, ALU.is_ge, ALU.is_lt
+    add, sub, mul, mx, mn, band = ALU.add, ALU.subtract, ALU.mult, ALU.max, ALU.min, ALU.bitwise_and
+    PART, P16, G16, G16P, TWOF, LIM, PLO, PHI, B31N, B5N, B35, B2N, B36, T1, T2, T3, T4, T5, ACNT, MLO, MHI = range(21)
+    LANE, DUMR, DUMV, OWN2, OWN1, WF, BF_, THR, KN, MNV, CF, SENT, THR2, MAY, NT, NDC, CNT, SN = range(18)
+    fresh = [0]
+
+    def tmp():
+        fresh[0] += 1
+        return S(18 + fresh[0] % 22)
+
+    io = lambda n: A("IOTA", 0, n, key=0)
+    r8 = slice(0, 8)
+
+    dma("sp", A("x0b"), H("x0"), "dx", 2.5)
+    dma("sp", A("sci", p=r8), H("v0"), "dv0", 2.5)
+    dma("sp", A("ei", 0, 512, key=[0, 1]), H("edge0"), "de")
+    dma("act", A("ei", 512, 1024, key=[2, 3]), H("ver0"), "dver")
+    for q in range(4):
+        dma("sp", RQ(q), (T["rec0"][:, 1024 * q:1024 * q + 1024], [], []), "dr%d" % q, 4.0 + q)
+    for q in range(4):
+        dma("sp", A("EF", 1024 * q, 1024 * q + 1024, key=q), H("eff"), "deff", 10.0)
+    iota(A("coli", 0, 1, key=0), [[0, 1]], 0, 1, flt=False)
+    iota(io(256), [[1, 256]], after=(len(ops) - 1,))
+    iota(A("MK"), [[0, 49], [1, 16]], after=(len(ops) - 1,))
+    iota(S(LANE), [[16, 32]], after=(len(ops) - 1,))
+    iota(A("gk"), [[0, 4], [16, 8], [0, 16]], after=(len(ops) - 1,))
+    iota(A("am"), [[0, 32], [16, 8]], after=(len(ops) - 1,))
+    iota(A("tmpf", 0, 16, key=[0, 1]), [[16, 4], [64, 2], [256, 2]], 15, after=(len(ops) - 1,))
+    iota(A("cv"), [[1, 32], [0, 32]], 32, after=(len(ops) - 1,))
+    for j, c in ((B31N, -31.0), (B5N, -5.0), (B35, -3.5), (B2N, -2.0), (B36, 36.0), (LIM, 196608.0)):
+        ms(C(j), c)
+    cp(C(PART), A("coli", 0, 1, key=0))
+    ts(A("coli", 1, 2, key=1), A("coli", 0, 1, key=0), 15, band)
+    cp(C(P16), A("coli", 1, 2, key=1))
+    tt(C(G16), C(PART), C(P16), sub)
+    ts(C(G16P), C(G16), 16.0, add)
+    ts(C(TWOF), C(P16), 2.0, mul, 1.0, add)
+    ts(C(T1), C(PART), 16.0, mul, 16.0, add)
+    ts(C(T3), C(G16), 24.0, add)
+    ts(C(MLO), C(P16), 8.0, lt)
+    ts(C(MHI), C(P16), 8.0, ge)
+    ts(A("jw"), io(144), C(G16P), eq, C(TWOF), mul)
+    ts(A("jw4"), A("jw"), -4.0, mul)
+    ts(A("w8"), io(144), C(T1), eq)
+    ts(A("oneswf"), io(144), C(G16P), eq)
+    ts(A("ow2"), io(144), C(T3), eq)
+    tt(A("ow2"), A("ow2"), A("oneswf"), add)
+    ts(A("MK"), A("MK"), C(P16), eq)
+    ts(A("v0h", p=r8), A("sci", p=r8), -2048.0, add)
+    f2w(A("B6", 0, 32), "w8", "v0h", p=r8)
+    ts(SI(0), A("B6", 0, 32), 2048.0, add)
+    cp(A("v0u", 32, 64, key=1), SI(0))
+    ts(SI(1), SI(0), 511, band)
+    cp(SUU(4), SI(1))
+    f2w(A("B5", 0, 32), "jw", "x0b")
+    cp(A("v0u", 0, 32, key=0), A("B5", 0, 32))
+    cp(A("SU", 0, 512, key=0), A("ei", 0, 512, key=[0, 1]))
+    for q in range(4):
+        act("rin%d" % q, A("R", 1024 * q, 1024 * q + 1024, key=q), RQ(q), AF.Relu, C(B36), -4.0)
+    cp(A("VL", 0, 512), A("ei", 512, 1024, key=[2, 3]))
+    cp(A("onesw"), A("oneswf"))
+    ts(A("ones960"), A("oneswf"), 960.0, mul)
+    ts(A("idf"), io(128), C(PART), eq)
+    ts(A("ids"), A("idf"), 2.0 ** -16, mul)
+    ms(A("ones"), 1.0)
+    ms(TM(5), 4.0)
+    ms(TM(6), 1.0)
+    scan(TM(7), TM(5), TM(6), 0.25, mul, mul)
+    for j, sh, a in ((PLO, 0.0, 8), (PHI, 8.0, 12)):
+        ts(TM(a), io(8), sh, add, C(P16), eq)
+        tt(TM(a + 1), TM(a), TM(7), mul)
+        red(C(j), TM(a + 1))
+    ms(A("wexp"), 0.0)
+    ts(A("wexp", 128, 256), A("gk", 0, 128), C(G16), eq, C(PLO), mul)
+    ts(A("wexp", 256, 384), A("gk", 0, 128), C(G16), eq, C(PHI), mul)
+    ts(A("blk"), A("gk", 0, 128), C(G16), eq)
+    cp(A("wg"), A("blk", 0, 128, 16))
+    ts(A("we", 0, 8), A("wg"), 960.0, mul)
+    ts(A("we", 8, 24), A("wexp", 128, 384, 16), -1.0, mul)
+    ts(S(LANE), S(LANE), C(P16), add)
+    ts(S(DUMR), S(LANE), 4096.0, add)
+    ts(S(DUMV), S(LANE), 512.0, add)
+    ts(A("dum2", 0, 32), S(LANE), 2048.0, add)
+    ts(A("dum2", 32, 64), S(LANE), 512.0, add)
+    cp(P5("base5", 2), S(DUMR))
+    cp(P5("base5", 3), S(DUMR))
+    cp(P5("base5", 4), S(DUMV))
+    ts(S(OWN2), io(32), 32.0, mul, 1016.0, add)
+    ts(S(OWN1), io(32), 16.0, mul, 504.0, add)
+    cp(A("idh"), A("idf"))
+    cp(A("idb"), A("idf"))
+    ts(A("neg2"), A("idf"), -2.0, mul)
+    c2, c3 = A("coli", 8, 16, key=2), A("coli", 16, 24, key=3)
+    ts(c2, io(8), -1.0, mul, C(P16), add)
+    ts(c2, c2, 15.0, add)
+    ts(c2, c2, 15, band)
+    ts(TM(10), c2, C(G16), add)
+    ts(c3, io(8), 1.0, add, C(P16), add)
+    ts(c3, c3, 15, band)
+    ts(TM(11), c3, C(P16), mx, C(G16), add)
+    for d in range(8):
+        ts(A("rc", 128 * (d % 4), 128 * (d % 4) + 128, key=d % 4), io(128), A("tmpf", 80 + d, 81 + d, key=10), eq)
+        tt(A("dif", 128 * d, 128 * d + 128, key=d), A("rc", 128 * (d % 4), 128 * (d % 4) + 128, key=d % 4), A("idb"), sub)
+        ts(A("bk", 128 * d, 128 * d + 128, key=d), io(128), A("tmpf", 88 + d, 89 + d, key=11), eq, 8192.0, mul)
+    ms(A("sc0"), -1.0 / 16)
+    ms(A("sc0", 0, 128, 16), 1.0e6)
+    ts(A("am"), A("am"), C(G16), eq)
+    ts(C(T2), C(MHI), 128.0, mul)
+    ts(A("exu"), A("tmpf", 0, 16, key=[0, 1]), C(T2), add)
+    ts(C(T4), C(P16), 112.0, add)
+    ts(C(T5), C(P16), 176.0, add)
+    ts(A("lw"), io(240), C(T4), eq, 65536.0, mul)
+    ts(A("expd", 0, 240), io(240), C(T5), eq, 65536.0, mul)
+    tt(A("lw"), A("lw"), A("expd", 0, 240), add)
+
+    def seld(t, after=()):
+        pat = [[-1, 16], [0, 8], [1, 16]]
+        iota(A("seld"), [[0, 2048]], int(BIGW), after=after)
+        asel(A("seld"), A("seld"), pat, ne, -BIGW, -t, 0)
+        if t:
+            asel(A("seld"), A("seld"), pat, ne, -BIGW, 16 - t, 0)
+        asel(A("seld"), A("seld"), [[-1, 16], [-16, 8], [0, 16]], eq, 0.0, 0, 1)
+
+    seld(0)
+    iota(A("IOTA", 256, 4096, key=1), [[1, 3840]], 256)
+    for q in range(8):
+        dma("sp", A("TV", 512 * q, 512 * q + 512, key=q), A("SU", 0, 512, key=0), "dtv", 8.0)
+    for q in (0, 1, 2, 3, 4, 5, 6, 7, 9):
+        dma("sp", A("TT", 512 * q, 512 * q + 512, key="c" if q < 9 else "b"), A("SU", 0, 512, key=0), "dtt", 12.0)
+    for q in range(1, 8):
+        dma("sp", A("SU", 512 * q, 512 * q + 512, key=q), A("SU", 0, 512, key=0), "dsu", 16.0)
+
+    Rw, SUw = A("R", 0, 4096), A("SU", 0, 4096)
+
+    def edge(t):
+        act("mask%d" % t, A("mask%d" % (t % 2)), IN(A("MK"), A("v%du" % t, 0, 32, key=0 if t == 0 else None)), AF.Copy)
+        if t == 0:
+            tt(A("sel"), IN(A("SU", 0, 512, key=0), SUU(4)), A("mask0"), mul)
+        else:
+            tt(A("sel"), IN(SUw, A("v%du" % t, 32, 64)), A("mask%d" % (t % 2)), mul)
+        for p0 in range(8):
+            mm(A("B5", 32, 96), A("ow2", 16 - p0, 144 - p0), A("sel", p0, 512, 8), p0 == 0, p0 == 7)
+        a, b = tmp(), tmp()
+        ts(a, A("B5", 32, 96, 2), C(MLO), mul)
+        ts(b, A("B5", 33, 96, 2), C(MHI), mul)
+        tt(SI(2), a, b, add)
+        ts(SI(3), SI(2), 511, band)
+        ts(SI(4), SI(2), 4095, band)
+        cp(SUU(0), SI(3))
+        cp(SUU(1), SI(4))
+        act("gw%d" % t, A("gw"), IN(Rw, SUU(1)), AF.Square, C(B31N))
+        for a, b in ((0, 1), (1, 4)):
+            cp(A("veru", 128 * a, 128 * b, key=list(range(a, b))), IN(A("VL", 0, 512), A("smu", 8 * a, 8 * b, key=0)))
+
+    def main(t):
+        x, vu = "x%db" % t, A("v%du" % t, 32, 64)
+        last = t == NSTEP - 1
+        act("xc%d" % t, A("B4"), A(x), AF.Square, C(B5N), 4.0)
+        parts = []
+        for ch in range(4):
+            parts += [(ch, 0, 64), (ch, 64, 128)] if ch in OPT["halves"] else [(ch, 0, 128)]
+        gkey = lambda ch, a: "%d_%d" % (ch, a)
+        for ch, a, b in parts:
+            act("G%d" % t, A("G", 2048 * ch + 16 * a, 2048 * ch + 16 * b, key=gkey(ch, a)),
+                IN(Rw, A("veru", 128 * ch + a, 128 * ch + b, key=ch)), AF.Square, C(B31N))
+        ts(A("nmask"), A("mask%d" % (t % 2)), -1.0, mul, 1.0, add)
+        ts(A("x32"), A(x), -4.0, mul, 36.0, add)
+        for ch in range(4):
+            mm(A("B%d" % ch), A("ones"), A("wexp"), True, False)
+        cp(A("verf"), A("veru"))
+        for ch in range(4):
+            mm(A("B%d" % ch, 384, 512), A("verf", 128 * ch, 128 * ch + 128), A("ids"), False, False)
+        ts(A("keyv"), vu, -2048.0, add)
+        for d in range(8):
+            mm(A("B6", 32 * d, 32 * d + 32), A("dif", 128 * d, 128 * d + 128, key=d), A("keyv"), True, True)
+        ts(A("eqv"), A("B6", 0, 256), 0.0, eq)
+        for d in range(8):
+            mm(A("B5", 96, 128), A("bk", 128 * d, 128 * d + 128, key=d), A("eqv", 32 * d, 32 * d + 32), d == 0, False)
+        mm(A("B5", 96, 128), A("idh"), A("keyv"), False, True)
+        tt(S(MNV), A("B5", 96, 128), A("dum2", 0, 32), mn)
+        ts(A("ofv", 0, 64, 2), S(MNV), 2048.0, add)
+        for c in range(31, -1, -1):
+            act("V%d" % t, IN(A("TV"), A("ofv", 2 * c, 2 * c + 1)), A("cv", 32 * c, 32 * c + 16), AF.Silu)
+        act("tv%d" % t, A("tvf"), IN(A("TV", 0, 4096), vu), AF.Copy)
+        if not last:
+            mm(A("B6"), A("idb"), A(x), True, False)
+            mm(A("B6"), A("idb"), A("EF", t, 4096, 8), False, True)
+            ts(A("hn"), A("B6"), 4.0, ge)
+            tag("hn%d" % t)
+            f2w(A("B6", 256, 288), "jw", x, last=False)
+            for p0 in range(16):
+                mm(A("B6", 256, 288), A("jw", 16 - p0, 144 - p0), A("EF", t + 8 * p0, 4096, 128), False, False)
+            f2w(A("B6", 256, 288), "jw4", "hn", first=False)
+            cp(S(SN), A("B6", 256, 288))
+            tag("snc%d" % t)
+        for ch in range(4):
+            mine = [q for q in parts if q[0] == ch]
+            old = ["r%d" % (2 * ch), "r%d" % (2 * ch + 1)] if ch < 2 and t in (0, NSTEP - 1) else []
+            for k in range(16):
+                base = 2048 * ch + 128 * k
+                for _, a, b in mine:
+                    tt(A("EQ", base + a, base + b, key=["%d_%d_%d" % (ch, k, a)] + ([old[k // 8]] if old and t == 0 and k % 8 == 0 else [])),
+                       A("G", 2048 * ch + 16 * a + k, 2048 * ch + 16 * b, 16, key=gkey(ch, a)), A("B4", 128 * ch + a, 128 * ch + b), eq)
+                    tag("E%d_%d_%d" % (t, ch, a))
+                mm(A("B%d" % ch, k, 128, 16), A("G", 2048 * ch + k, 2048 * ch + 2048, 16, key=[gkey(ch, q[1]) for q in mine]), A("wg"), False, False)
+            for k in range(16):
+                base = 2048 * ch + 128 * k
+                mm(A("B%d" % ch, k, 128, 16), A("EQ", base, base + 128, key=["%d_%d_%d" % (ch, k, q[1]) for q in mine]), A("we", 0, 8), False, k == 15)
+            sl = lambda nm: A(nm, 128 * ch, 128 * ch + 128, key=ch)
+            ts(sl("di"), A("B%d" % ch, 0, 128), -1.0 / 960, mul, 16.41, add)
+            tt(sl("keyl"), sl("di"), A("B%d" % ch, 384, 512), add)
+            scan(sl("scan"), A("sc0"), sl("keyl"), 0.0, add, mn)
+            tag("S%d_%d" % (t, ch))
+            mm(A("B%d" % ch, 128, 384), A("ones"), A("wexp", 128, 384), True, False)
+            for k in range(16):
+                base = 2048 * ch + 128 * k
+                mm(A("B%d" % ch, 128 + k, 384, 16), A("EQ", base, base + 128, key=["%d_%d_%d" % (ch, k, q[1]) for q in mine] + (old if last else [])),
+                   A("we", 8, 24), False, False)
+        tt(A("eqw"), A("gw"), A("B4"), eq)
+        tag("eqw%d" % t)
+        f2w(A("B7", 0, 32), "onesw", "gw", last=False)
+        f2w(A("B7", 0, 32), "ones960", "eqw", first=False)
+        a, b = tmp(), tmp()
+        ts(a, A("B7", 0, 32), 15360.0, ge)
+        ts(b, SI(2), 4096.0, lt)
+        tt(S(KN), a, b, mul)
+        ts(S(THR), S(KN), 1.0e9, mul, 65536.0, add)
+        tag("thr%d" % t)
+        chain = []
+        for ch, a, b in parts:
+            if a == 0:
+                chain += tags["S%d_%d" % (t, ch - 2)] if ch >= 2 else []
+                for nm in OPT["between"][ch].split():
+                    chain += tags.get(nm + str(t), [])
+            chain += tags["E%d_%d_%d" % (t, ch, a)]
+        for a, b in zip(chain, chain[1:]):
+            ops[b]["after"].append(a)
+        cp(S(WF), SI(2))
+        cp(S(BF_), SI(3))
+        ts(S(NT), S(LANE), 8.0, mul, float(t), add)
+        tt(S(NDC), S(NT), S(DUMR), sub)
+        tt(P5("del5", 4), S(BF_), S(DUMV), sub)
+
+    def decide(t):
+        x, of = "x%db" % t, "of%d" % t
+        last = t == NSTEP - 1
+        tt(A("expd"), IN(A("scan"), A("exu")), A("am"), mul)
+        for gg in range(4):
+            mm(A("B5", 128, 192), A("lw", 112 - 16 * gg, 240 - 16 * gg), A("expd", 64 * gg, 64 * gg + 64), gg == 0, gg == 3)
+        ts(A("smi", 160, 192, key=5, p=slice(0, 64)), A("B5", 128, 160, p=slice(0, 64)), 61440.0, add)
+        ts(A("smi", 160, 192, key=7, p=slice(64, 128)), A("B5", 160, 192, p=slice(64, 128)), 61440.0, add)
+        K = A("smi", 160, 192, key=[5, 7])
+        a, b = tmp(), tmp()
+        ts(SI(6), K, 4095, band)
+        tt(a, K, S(THR), lt)
+        ts(b, SI(6), -2048.0, add)
+        ts(S(SENT), a, 4096.0, mul, -2048.0, add)
+        cp(SUU(2), SI(6))
+        tt(A("key2", 0, 32, key=0), b, S(SENT), mx)
+        tt(A("key2", 32, 64, key=1), S(BF_), S(SENT), mx)
+        act("rc%d" % t, A("rc"), IN(Rw, SUU(2)), AF.Square, C(B31N))
+        for d in range(8):
+            mm(A("B6", 64 * d, 64 * d + 64), A("dif", 128 * d, 128 * d + 128, key=d), A("key2"), True, True)
+        ts(A("ntg"), K, C(LIM), ge)
+        ts(A("eqd"), A("B6"), 0.0, eq)
+        for d in range(8):
+            mm(A("B5", 192, 256), A("bk", 128 * d, 128 * d + 128, key=d), A("eqd", 64 * d, 64 * d + 64), d == 0, False)
+        mm(A("B5", 192, 256), A("idh"), A("key2"), False, True)
+        tt(A("mn2"), A("B5", 192, 256), A("dum2"), mn)
+        ts(A("ofcb", 0, 64, 2, key=0), A("mn2", 0, 32), 2048.0, add)
+        if OPT["split"]:
+            cp(A("ofb", 0, 64, 2), A("mn2", 32, 64))
+            for c in range(31, -1, -1):
+                act("CB%d" % t, IN(A("TT", 0, 4608, key="c"), A("ofcb", 2 * c, 2 * c + 1, key=0)), A("cv", 32 * c, 32 * c + 16), AF.Silu)
+                act("CB%d" % t, IN(A("TT", 4608, 5632, key="b"), A("ofb", 2 * c, 2 * c + 1)), A("cv", 32 * c, 32 * c + 16), AF.Silu)
+        else:
+            ts(A("ofcb", 1, 64, 2, key=1), A("mn2", 32, 64), 4608.0, add)
+            for c in range(31, -1, -1):
+                act("CB%d" % t, IN(A("TT"), A("ofcb", 2 * c, 2 * c + 2)), A("cv", 32 * c, 32 * c + 32), AF.Silu)
+        act("tc%d" % t, A("tcf"), IN(A("TT", 0, 4096), SUU(2)), AF.Copy)
+        act("tc%d" % t, A("tbf"), IN(A("TT", 4608, 5120), SUU(0)), AF.Copy)
+        tt(A("eqc"), A("rc"), A("B4"), eq)
+        for ch in range(4):
+            mm(A("B%d" % ch, 128, 384), A("eqc", 128 * ch, 128 * ch + 128), A("wexp", 128, 384), False, True)
+        mm(A("B7"), A("wexp", 0, 128), A("gw"), True, False)
+        for p0 in range(16):
+            mm(A("B7", p0, 512, 16), A("seld", 128 * p0, 128 * p0 + 128), A("ntg"), False, False)
+        cp(S(CF), SI(6))
+        a, b, c, d, e = tmp(), tmp(), tmp(), tmp(), tmp()
+        tt(a, S(WF), S(CF), sub)
+        tt(a, a, S(KN), mul)
+        tt(P5("base5", 1), a, S(CF), add)
+        tt(b, S(NT), S(CF), sub)
+        tt(P5("del5", 1), b, A("ntg"), mul)
+        tt(b, P5("del5", 1), S(CF), add)
+        cp(SUU(6), b)
+        ts(c, A("mn2", 32, 64), 4.0, mul)
+        tt(c, c, A("mn2", 0, 32), mx)
+        ts(c, c, 2048.0, ge, 1.0e6, mul)
+        tt(S(THR2), c, S(OWN2), add)
+        ts(d, K, C(LIM), lt)
+        tt(e, S(CF), S(DUMR), sub)
+        tt(P5("del5", 2), e, d, mul)
+        tt(P5("del5", 3), S(NDC), A("ntg"), mul)
+        if not last:
+            cp(SUU(5), P5("base5", 1))
+            tt(A("yu"), IN(A("EF"), SUU(5)), A(x), add)
+            ts(A("hu"), A("yu"), 4.0, ge)
+            f2w(A("B6", 0, 32), "jw", "yu", last=False)
+            f2w(A("B6", 0, 32), "jw4", "hu", first=False)
+            cp(P5("base5", 0), A("B6", 0, 32))
+            a = tmp()
+            tt(a, S(SN), P5("base5", 0), sub)
+            tt(P5("del5", 0), a, A("ntg"), mul)
+        cp(A("sci"), IN(SUw, SUU(2)))
+        ts(A("sci"), A("sci"), 511, band)
+        ts(A("scf"), A("sci"), 4096.0, add)
+        tt(A("val"), A("eqc"), A("x32"), mul)
+        for ch in range(4):
+            ek = A("ei", 256 * ch, 256 * ch + 256, key=ch)
+            cp(ek, A("B%d" % ch, 128, 384))
+            ts(ek, ek, 0xAAAA, band)
+            tt(A("z", 128 * ch, 128 * ch + 128, key=ch), A("ei", 256 * ch, 256 * ch + 128, key=ch), A("ei", 256 * ch + 128, 256 * ch + 256, key=ch), add)
+            mm(A("B7", 128 * ch, 128 * ch + 128), A("z", 128 * ch, 128 * ch + 128, key=ch), A("idb"), False, ch == 3)
+        tt(A("dv"), IN(A("IOTA"), SUU(6)), A("verf"), sub)
+        ts(A("B7"), A("B7"), 0.5, lt)
+        tt(A("dm"), A("dv"), A("B7"), mul)
+        f2w(A("B5", 256, 288), "onesw", "tcf", last=False)
+        f2w(A("B5", 256, 288), "onesw", "tbf", first=False)
+        tt(S(MAY), A("B5", 256, 288), S(THR2), ge)
+        for q in range(5):
+            tt(P5("prod5", q), P5("del5", q), S(MAY), mul)
+        for a, b in ((3, 4), (0, 2), (2, 3), (4, 5)):
+            ks = list(range(a, b))
+            tt(A("sum5", 32 * a, 32 * b, key=ks), A("prod5", 32 * a, 32 * b, key=ks), A("base5", 32 * a, 32 * b, key=ks), add)
+            cp(A(of, 32 * a, 32 * b, key=ks), A("sum5", 32 * a, 32 * b, key=ks))
+        f2w(A("B5", 288, 320), "onesw", "tvf")
+        a = tmp()
+        tt(a, A("B5", 288, 320), S(OWN1), lt)
+        ts(a, a, 8192.0, mul)
+        tt(a, a, S(MNV), add)
+        tt(a, a, A("dum2", 0, 32), mn)
+        ts(SUU(3), a, 2048.0, add)
+
+    def writes(t):
+        x, vu, of = "x%db" % t, A("v%du" % t, 32, 64), "of%d" % t
+        last = t == NSTEP - 1
+        hop = HOP if not last else -HOP * t
+        dst, src = T.cores[(rank + hop) % n_r], T.cores[(rank - hop) % n_r]
+        O = lambda q: P5(of, q)
+        sv = send(A(of, 0, 64, key=[0, 1]), "v%du" % (t + 1), dst, "av%d" % (t + 1), 2.5)
+        act("ef%d" % t, A("efg"), IN(A("EF"), O(1)), AF.Copy)
+        for bank in ("B4", "B6"):
+            mm(A(bank), A("idb"), A(x), True, False)
+        mm(A("B4"), A("idb"), A("efg"), False, True)
+        mm(A("B6"), A("idb"), A("efg"), False, False)
+        act("sg%d" % t, A("sg"), A("B4"), AF.Sign, C(B35))
+        mm(A("B6"), A("neg2"), A("sg"), False, True)
+        act("xo%d" % t, A("xo%d" % t), A("B6"), AF.Identity, C(B2N))
+        sx = send(A("xo%d" % t), "x%db" % (t + 1), dst, "ax%d" % (t + 1), 3.2)
+        act("rg%d" % t, IN(A("R"), O(2)), A("val"), AF.Silu)
+        act("rn%d" % t, IN(A("R"), O(3)), A("x32"), AF.Silu)
+        act("sn%d" % t, IN(A("SU"), O(3)), A("scf"), AF.Silu)
+        tt(A("vm"), IN(A("IOTA"), O(1)), A("mask%d" % (t % 2)), mul)
+        tt(A("pg"), IN(SUw, vu), A("nmask"), mul)
+        tt(IN(A("SU"), SUU(3)), A("pg"), A("vm"), add)
+        tt(IN(A("VL"), O(4)), A("verf"), A("dm"), add)
+        arrive("v%du" % (t + 1), "av%d" % (t + 1), src, sv)
+        arrive("x%db" % (t + 1), "ax%d" % (t + 1), src, sx)
+        if not last:
+            seld(t + 1, (sx[0],))
+            tt(A("cl"), S(MAY), A("ntg"), mul)
+            mm(A("B6", 0, 32), A("blk"), A("cl"), True, True)
+            red(C(ACNT), A("B6", 0, 32))
+            cp(A("coli", 2, 3, key=4), C(ACNT))
+            ts(A("coli", 3, 4, key=5), A("coli", 2, 3, key=4), 1, band)
+            ts(C(LIM), A("coli", 3, 4, key=5), 65536.0, mul, 196608.0, add)
+
+    for t in range(NSTEP):
+        edge(t)
+        main(t)
+        decide(t)
+        writes(t)
+    for ch in range(32):
+        mm(A("B0", ch, 256, 32), A("SU", 128 * ch, 128 * ch + 128), A("oneswf", 16, 144, 16), True, True)
+    cp(A("keyl", 0, 256), A("B0", 0, 256))
+    for h in range(2):
+        mm(A("B1", 128 * h, 128 * h + 128), A("keyl", 128 * h, 128 * h + 128), A("idf"), True, True)
+    cp(A("di", 0, 256), A("B1", 0, 256))
+    cp(A("scan", 0, 256), A("di", 0, 256))
+    for q in range(4):
+        if q < 3:
+            act("rout", RQ(q), A("R", 1024 * q, 1024 * q + 1024), AF.Copy)
+        else:
+            cp(RQ(q), A("R", 1024 * q, 1024 * q + 1024))
+        ts(RQ(q), RQ(q), -0.25, mul, 9.0, add)
+    act("yv", A("sel"), IN(A("IOTA"), A("v4u", 32, 64)), AF.Copy)
+    dma("act", H("yv"), A("sel", p=slice(0, 128, 16)), "out")
+    dma("sp", H("yl"), A("VL", 0, 512), "out")
+    dma("sp", H("yx"), A("x4b"), "out")
+    for q in (0, 3, 1, 2):
+        dma("sp", (T["yr"][:, 1024 * q:1024 * q + 1024], [], []), RQ(q), "out")
+    for h in range(2):
+        dma("sp", (T["ys"][4 * h:4 * h + 4, :], [], []), A("scan", 128 * h, 128 * h + 128), "out")
+
+    seq = tags["xc0"] + tags["rin0"] + tags["mask0"] + tags["rin1"] + tags["rin2"] + tags["rin3"]
+    for t in range(NSTEP):
+        tg = lambda nm: tags.get(nm + str(t), [])
+        gs, vs, cb = tg("G"), tg("V"), tg("CB")
+        n1, n2 = OPT["nv1"], OPT["nv1"] + OPT["nv2"]
+        xa, ga = OPT["xc"], OPT["gw"]
+        seq += (tg("gw") if ga else []) + gs[:xa] + (tg("xc") if t else []) + gs[xa:] + ([] if ga else tg("gw")) + vs[:n1] + tg("rc") + vs[n1:n2]
+        rest = vs[n2:]
+        for m, i in enumerate(cb):
+            seq += [i] + rest[m:m + 1]
+        for nm in OPT["tail"].split():
+            seq += tags.get("mask%d" % (t + 1), []) if nm == "mask" else tg(nm)
+    seq += tags["rout"][:1] + tags["yv"] + tags["rout"][1:]
+    for a, b in zip(seq, seq[1:]):
+        ops[b]["after"].append(a)
+
+    def hit(a, b):
+        return a == b or a.split("#")[0] == b or b.split("#")[0] == a
+
+    lastw, readers, group = {}, {}, {}
+    for i, o in enumerate(ops):
+        if o["dma"]:
+            group.setdefault(o["dma"], []).append(i)
+    for i, o in enumerate(ops):
+        deps = set()
+        for k in o["rd"]:
+            base = k.split("#")[0]
+            deps.update(j for k2, j in lastw.get(base, {}).items() if hit(k, k2))
+            if SCRATCH[base][0] == "psum":
+                deps.update(j for j in readers.get(base, {}).get(base, []) if ops[j]["e"] != o["e"])
+        for k in o["wr"]:
+            base = k.split("#")[0]
+            deps.update(j for k2, j in lastw.get(base, {}).items() if hit(k, k2))
+            for k2, js in readers.get(base, {}).items():
+                if hit(k, k2):
+                    deps.update(js)
+        if o["ext"] == "arr" or (o["dma"] and o["dma"] == "dtt"):
+            deps = set(j for j in deps if o["ext"] is None and ops[j]["dma"] != o["dma"])
+        deps.discard(i)
+        for j in list(deps):
+            if ops[j]["dma"]:
+                deps.update(group[ops[j]["dma"]])
+        o["sync"] = [j for j in deps if ops[j]["ext"] != "send" and not (ops[j]["e"] == "pe" and o["e"] == "pe")]
+        o["need"] = deps
+        o["all"] = sorted(deps.union(o["after"]))
+        for k in o["wr"]:
+            base = k.split("#")[0]
+            d = lastw.setdefault(base, {})
+            r = readers.setdefault(base, {})
+            if k == base:
+                d.clear()
+                r.clear()
+            r.pop(k, None)
+            d[k] = i
+        for k in o["rd"]:
+            readers.setdefault(k.split("#")[0], {}).setdefault(k, []).append(i)
+    if "order" not in ORDER:
+        ORDER["order"] = schedule(ops)
+    order = ORDER["order"]
+    pos = {i: n for n, i in enumerate(order)}
+    seen = {e: {} for e in Q}
+    for i in order:
+        o = ops[i]
+        if o["e"] is None:
+            continue
+        keep = {}
+        for j in o["sync"]:
+            s = ops[j]["dma"] or ops[j]["e"]
+            if s not in keep or pos[j] > pos[keep[s]]:
+                keep[s] = j
+        sn = seen[o["e"]]
+        o["deps"] = {s: j for s, j in keep.items() if sn.get(s, -1) < pos[j]}
+        for s, j in o["deps"].items():
+            sn[s] = len(ops) if ops[j]["dma"] else pos[j]
+            ops[j]["inc"] = True
+    total = {}
+    for i in order:
+        o = ops[i]
+        if o["dma"]:
+            total[o["dma"]] = total.get(o["dma"], 0) + o["n"]
+        elif o["ext"] == "send":
+            total["sent"] = total.get("sent", 0) + o["n"]
+        elif o["inc"]:
+            total[o["e"]] = total.get(o["e"], 0) + 1
+            o["cnt"] = total[o["e"]]
+    for i in order:
+        o = ops[i]
+        if o["e"] is None:
+            continue
+        for s, j in o["deps"].items():
+            Q[o["e"]].wait_ge(T.sem[s], total[s] if ops[j]["dma"] else ops[j]["cnt"])
+        ins = o["fn"]()
+        if o["dma"]:
+            ins.then_inc(T.sem[o["dma"]], 16)
+        elif o["inc"]:
+            ins.then_inc(T.sem[o["e"]], 1)
+    for s, n in total.items():
+        g.wait_ge(T.sem[s], n)

@@ -13,8 +13,8 @@ _decl("psum", "float32", "B0:512 B1:512 B2:512 B3:512 B4:512 B5:512 B6:512 B7:51
 _decl("sbuf", "bfloat16", "EF:4096 G:8192 EQ:8192 MK:784 onesw:144 ones960:144 jw:144 jw4:144 hn:512 yu:512 hu:512 bk:1024 "
       "idb:128 neg2:128 blk:128 ones:128 wexp:512 we:24 wg:8 seld:2048 x0b:512 x1b:512 x2b:512 x3b:512 x4b:512 "
       "xo0:512 xo1:512 xo2:512 xo3:512 mask0:512 mask1:512 nmask:512 gw:512 eqw:512 eqd:512 eqv:256 tvf:512 tcf:512 tbf:512 rc:512 "
-      "eqc:512 z:512 efg:512 sg:512 ntg:32 cl:32")
-_decl("sbuf", "float32", "R:4608 SU:4608 VL:1024 TT:5632 TV:4608 IOTA:4096 cv:1024 gk:512 am:256 oneswf:144 ow2:144 idf:128 ids:128 lw:240 "
+      "iob:128 neg4:128 onesn:144 c36:512 eqc:512 z:512 efg:512 sg:512 ntg:32 cl:32")
+_decl("sbuf", "float32", "R:4608 SU:4608 VL:1024 TT:5632 TV:4608 IOTA:4096 cv:1024 gk:512 am:256 oneswf:144 ow2:144 idf:128 ids:128 lw:256 "
       "sc0:128 col:32 sm:1280 base5:160 del5:160 prod5:160 sum5:160 mn2:64 dum2:64 sel:512 verf:512 keyl:512 scan:512 expd:256 val:512 "
       "x32:512 scf:512 dv:512 dm:512 vm:512 pg:512 tmpf:128")
 _decl("sbuf", "int32", "smi:256 coli:32 di:512 ei:1024 sci:512")
@@ -27,7 +27,8 @@ NSTEP, HOP, BIGW = 4, 3, 262144.0
 CYC, PEC, GATH, SCAT, FIX, WAKE = 0.00083, 0.0006, 1.56, 3.8, 0.05, 0.06
 ORDER = {}
 OPT = {"split": False, "nv1": 20, "nv2": 10, "rounds": 4, "halves": (), "xc": 0, "gw": 0,
-       "between": ("", "hn", "", "snc"), "tail": "tc tv sn ef sg mask xo rg rn"}
+       "between": ("", "hn", "", "snc"), "tail": "tc tv x32 sn ef sg mask xo rg rn",
+       "end": "tc tv x32 sn ef rg sg rn xo", "x32": 1, "snd": 0, "nact": 2, "ofs": ((3, 4), (0, 2), (2, 3), (4, 5))}
 
 
 def schedule(ops):
@@ -235,6 +236,8 @@ def rank_program(g, core, T, topo):
     iota(A("gk"), [[0, 4], [16, 8], [0, 16]], after=(len(ops) - 1,))
     iota(A("am"), [[0, 32], [16, 8]], after=(len(ops) - 1,))
     iota(A("tmpf", 0, 16, key=[0, 1]), [[16, 4], [64, 2], [256, 2]], 15, after=(len(ops) - 1,))
+    iota(A("lw"), [[0, 4], [1, 64]], -48, after=(len(ops) - 1,))
+    iota(A("c36"), [[0, 512]], 36, after=(len(ops) - 1,))
     iota(A("cv"), [[1, 32], [0, 32]], 32, after=(len(ops) - 1,))
     for j, c in ((B31N, -31.0), (B5N, -5.0), (B35, -3.5), (B2N, -2.0), (B36, 36.0), (LIM, 196608.0)):
         ms(C(j), c)
@@ -249,7 +252,7 @@ def rank_program(g, core, T, topo):
     ts(C(MLO), C(P16), 8.0, lt)
     ts(C(MHI), C(P16), 8.0, ge)
     ts(A("jw"), io(144), C(G16P), eq, C(TWOF), mul)
-    ts(A("jw4"), A("jw"), -4.0, mul)
+    act("k0", A("jw4"), A("jw"), AF.Copy, None, -4.0)
     ts(A("w8"), io(144), C(T1), eq)
     ts(A("oneswf"), io(144), C(G16P), eq)
     ts(A("ow2"), io(144), C(T3), eq)
@@ -267,10 +270,8 @@ def rank_program(g, core, T, topo):
     for q in range(4):
         act("rin%d" % q, A("R", 1024 * q, 1024 * q + 1024, key=q), RQ(q), AF.Relu, C(B36), -4.0)
     cp(A("VL", 0, 512), A("ei", 512, 1024, key=[2, 3]))
-    cp(A("onesw"), A("oneswf"))
-    ts(A("ones960"), A("oneswf"), 960.0, mul)
-    ts(A("idf"), io(128), C(PART), eq)
-    ts(A("ids"), A("idf"), 2.0 ** -16, mul)
+    act("k0", A("onesw"), A("oneswf"), AF.Copy)
+    act("k0", A("ones960"), A("oneswf"), AF.Copy, None, 960.0)
     ms(A("ones"), 1.0)
     ms(TM(5), 4.0)
     ms(TM(6), 1.0)
@@ -295,10 +296,14 @@ def rank_program(g, core, T, topo):
     cp(P5("base5", 3), S(DUMR))
     cp(P5("base5", 4), S(DUMV))
     ts(S(OWN2), io(32), 32.0, mul, 1016.0, add)
-    ts(S(OWN1), io(32), 16.0, mul, 504.0, add)
-    cp(A("idh"), A("idf"))
-    cp(A("idb"), A("idf"))
-    ts(A("neg2"), A("idf"), -2.0, mul)
+    ts(S(OWN1), io(32), 8192.0, mul, 262144.0, add)
+    cp(A("iob"), io(128))
+    ts(A("idb"), A("iob"), C(PART), eq)
+    cp(A("idh"), A("idb"))
+    mm(A("B7", 0, 128), A("idb"), A("idb"), True, True)
+    act("k1", A("neg2"), A("idb"), AF.Copy, None, -2.0)
+    act("k1", A("idf"), A("idb"), AF.Copy)
+    act("k1", A("ids"), A("idb"), AF.Copy, None, 2.0 ** -16)
     c2, c3 = A("coli", 8, 16, key=2), A("coli", 16, 24, key=3)
     ts(c2, io(8), -1.0, mul, C(P16), add)
     ts(c2, c2, 15.0, add)
@@ -308,19 +313,17 @@ def rank_program(g, core, T, topo):
     ts(c3, c3, 15, band)
     ts(TM(11), c3, C(P16), mx, C(G16), add)
     for d in range(8):
-        ts(A("rc", 128 * (d % 4), 128 * (d % 4) + 128, key=d % 4), io(128), A("tmpf", 80 + d, 81 + d, key=10), eq)
-        tt(A("dif", 128 * d, 128 * d + 128, key=d), A("rc", 128 * (d % 4), 128 * (d % 4) + 128, key=d % 4), A("idb"), sub)
-        ts(A("bk", 128 * d, 128 * d + 128, key=d), io(128), A("tmpf", 88 + d, 89 + d, key=11), eq, 8192.0, mul)
+        ts(A("rc", 128 * (d % 4), 128 * (d % 4) + 128, key=d % 4), A("iob"), A("tmpf", 80 + d, 81 + d, key=10), eq)
+        tt(A("dif", 128 * d, 128 * d + 128, key=d), A("rc", 128 * (d % 4), 128 * (d % 4) + 128, key=d % 4), A("B7", 0, 128), sub)
+        ts(A("bk", 128 * d, 128 * d + 128, key=d), A("iob"), A("tmpf", 88 + d, 89 + d, key=11), eq, 8192.0, mul)
+    act("k1", A("neg4"), A("idb"), AF.Copy, None, -4.0)
+    act("k0", A("onesn"), A("oneswf"), AF.Copy, None, -512.0)
     ms(A("sc0"), -1.0 / 16)
     ms(A("sc0", 0, 128, 16), 1.0e6)
     ts(A("am"), A("am"), C(G16), eq)
     ts(C(T2), C(MHI), 128.0, mul)
     ts(A("exu"), A("tmpf", 0, 16, key=[0, 1]), C(T2), add)
-    ts(C(T4), C(P16), 112.0, add)
-    ts(C(T5), C(P16), 176.0, add)
-    ts(A("lw"), io(240), C(T4), eq, 65536.0, mul)
-    ts(A("expd", 0, 240), io(240), C(T5), eq, 65536.0, mul)
-    tt(A("lw"), A("lw"), A("expd", 0, 240), add)
+    ts(A("lw"), A("lw"), C(P16), eq, 65536.0, mul)
 
     def seld(t, after=()):
         pat = [[-1, 16], [0, 8], [1, 16]]
@@ -373,7 +376,10 @@ def rank_program(g, core, T, topo):
             act("G%d" % t, A("G", 2048 * ch + 16 * a, 2048 * ch + 16 * b, key=gkey(ch, a)),
                 IN(Rw, A("veru", 128 * ch + a, 128 * ch + b, key=ch)), AF.Square, C(B31N))
         ts(A("nmask"), A("mask%d" % (t % 2)), -1.0, mul, 1.0, add)
-        ts(A("x32"), A(x), -4.0, mul, 36.0, add)
+        if OPT["x32"]:
+            act("x32%d" % t, A("x32"), A(x), AF.Identity, C(B36), -4.0)
+        else:
+            ts(A("x32"), A(x), -4.0, mul, 36.0, add)
         for ch in range(4):
             mm(A("B%d" % ch), A("ones"), A("wexp"), True, False)
         cp(A("verf"), A("veru"))
@@ -388,6 +394,7 @@ def rank_program(g, core, T, topo):
         mm(A("B5", 96, 128), A("idh"), A("keyv"), False, True)
         tt(S(MNV), A("B5", 96, 128), A("dum2", 0, 32), mn)
         ts(A("ofv", 0, 64, 2), S(MNV), 2048.0, add)
+        tt(S(MNV), S(MNV), S(OWN1), add)
         for c in range(31, -1, -1):
             act("V%d" % t, IN(A("TV"), A("ofv", 2 * c, 2 * c + 1)), A("cv", 32 * c, 32 * c + 16), AF.Silu)
         act("tv%d" % t, A("tvf"), IN(A("TV", 0, 4096), vu), AF.Copy)
@@ -444,11 +451,9 @@ def rank_program(g, core, T, topo):
             chain += tags["E%d_%d_%d" % (t, ch, a)]
         for a, b in zip(chain, chain[1:]):
             ops[b]["after"].append(a)
-        cp(S(WF), SI(2))
-        cp(S(BF_), SI(3))
         ts(S(NT), S(LANE), 8.0, mul, float(t), add)
         tt(S(NDC), S(NT), S(DUMR), sub)
-        tt(P5("del5", 4), S(BF_), S(DUMV), sub)
+        tt(P5("del5", 4), SI(3), S(DUMV), sub)
 
     def decide(t):
         x, of = "x%db" % t, "of%d" % t
@@ -466,7 +471,7 @@ def rank_program(g, core, T, topo):
         ts(S(SENT), a, 4096.0, mul, -2048.0, add)
         cp(SUU(2), SI(6))
         tt(A("key2", 0, 32, key=0), b, S(SENT), mx)
-        tt(A("key2", 32, 64, key=1), S(BF_), S(SENT), mx)
+        tt(A("key2", 32, 64, key=1), SI(3), S(SENT), mx)
         act("rc%d" % t, A("rc"), IN(Rw, SUU(2)), AF.Square, C(B31N))
         for d in range(8):
             mm(A("B6", 64 * d, 64 * d + 64), A("dif", 128 * d, 128 * d + 128, key=d), A("key2"), True, True)
@@ -489,26 +494,28 @@ def rank_program(g, core, T, topo):
         act("tc%d" % t, A("tcf"), IN(A("TT", 0, 4096), SUU(2)), AF.Copy)
         act("tc%d" % t, A("tbf"), IN(A("TT", 4608, 5120), SUU(0)), AF.Copy)
         tt(A("eqc"), A("rc"), A("B4"), eq)
+        mm(A("B6"), A("idb"), A("c36"), True, False)
+        mm(A("B6"), A("neg4"), A(x), False, True)
+        tt(A("val"), A("eqc"), A("B6"), mul)
         for ch in range(4):
             mm(A("B%d" % ch, 128, 384), A("eqc", 128 * ch, 128 * ch + 128), A("wexp", 128, 384), False, True)
         mm(A("B7"), A("wexp", 0, 128), A("gw"), True, False)
         for p0 in range(16):
             mm(A("B7", p0, 512, 16), A("seld", 128 * p0, 128 * p0 + 128), A("ntg"), False, False)
-        cp(S(CF), SI(6))
         a, b, c, d, e = tmp(), tmp(), tmp(), tmp(), tmp()
-        tt(a, S(WF), S(CF), sub)
+        tt(a, SI(2), SI(6), sub)
         tt(a, a, S(KN), mul)
-        tt(P5("base5", 1), a, S(CF), add)
-        tt(b, S(NT), S(CF), sub)
+        tt(P5("base5", 1), a, SI(6), add)
+        tt(b, S(NT), SI(6), sub)
         tt(P5("del5", 1), b, A("ntg"), mul)
-        tt(b, P5("del5", 1), S(CF), add)
+        tt(b, P5("del5", 1), SI(6), add)
         cp(SUU(6), b)
         ts(c, A("mn2", 32, 64), 4.0, mul)
         tt(c, c, A("mn2", 0, 32), mx)
         ts(c, c, 2048.0, ge, 1.0e6, mul)
         tt(S(THR2), c, S(OWN2), add)
         ts(d, K, C(LIM), lt)
-        tt(e, S(CF), S(DUMR), sub)
+        tt(e, SI(6), S(DUMR), sub)
         tt(P5("del5", 2), e, d, mul)
         tt(P5("del5", 3), S(NDC), A("ntg"), mul)
         if not last:
@@ -524,7 +531,6 @@ def rank_program(g, core, T, topo):
         cp(A("sci"), IN(SUw, SUU(2)))
         ts(A("sci"), A("sci"), 511, band)
         ts(A("scf"), A("sci"), 4096.0, add)
-        tt(A("val"), A("eqc"), A("x32"), mul)
         for ch in range(4):
             ek = A("ei", 256 * ch, 256 * ch + 256, key=ch)
             cp(ek, A("B%d" % ch, 128, 384))
@@ -537,17 +543,16 @@ def rank_program(g, core, T, topo):
         f2w(A("B5", 256, 288), "onesw", "tcf", last=False)
         f2w(A("B5", 256, 288), "onesw", "tbf", first=False)
         tt(S(MAY), A("B5", 256, 288), S(THR2), ge)
-        for q in range(5):
+        for q in range(1 if last else 0, 5):
             tt(P5("prod5", q), P5("del5", q), S(MAY), mul)
-        for a, b in ((3, 4), (0, 2), (2, 3), (4, 5)):
+        for a, b in OPT["ofs"]:
             ks = list(range(a, b))
             tt(A("sum5", 32 * a, 32 * b, key=ks), A("prod5", 32 * a, 32 * b, key=ks), A("base5", 32 * a, 32 * b, key=ks), add)
             cp(A(of, 32 * a, 32 * b, key=ks), A("sum5", 32 * a, 32 * b, key=ks))
-        f2w(A("B5", 288, 320), "onesw", "tvf")
+            tag("of%d" % t)
+        f2w(A("B5", 288, 320), "onesn", "tvf")
         a = tmp()
-        tt(a, A("B5", 288, 320), S(OWN1), lt)
-        ts(a, a, 8192.0, mul)
-        tt(a, a, S(MNV), add)
+        tt(a, A("B5", 288, 320), S(MNV), add)
         tt(a, a, A("dum2", 0, 32), mn)
         ts(SUU(3), a, 2048.0, add)
 
@@ -569,9 +574,13 @@ def rank_program(g, core, T, topo):
         sx = send(A("xo%d" % t), "x%db" % (t + 1), dst, "ax%d" % (t + 1), 3.2)
         act("rg%d" % t, IN(A("R"), O(2)), A("val"), AF.Silu)
         act("rn%d" % t, IN(A("R"), O(3)), A("x32"), AF.Silu)
-        act("sn%d" % t, IN(A("SU"), O(3)), A("scf"), AF.Silu)
+        if last and OPT["snd"]:
+            cp(IN(A("SU"), O(3)), A("scf"))
+        else:
+            act("sn%d" % t, IN(A("SU"), O(3)), A("scf"), AF.Silu)
         tt(A("vm"), IN(A("IOTA"), O(1)), A("mask%d" % (t % 2)), mul)
         tt(A("pg"), IN(SUw, vu), A("nmask"), mul)
+        ops[-1]["after"] += tags["of%d" % t]
         tt(IN(A("SU"), SUU(3)), A("pg"), A("vm"), add)
         tt(IN(A("VL"), O(4)), A("verf"), A("dm"), add)
         arrive("v%du" % (t + 1), "av%d" % (t + 1), src, sv)
@@ -598,7 +607,7 @@ def rank_program(g, core, T, topo):
     cp(A("di", 0, 256), A("B1", 0, 256))
     cp(A("scan", 0, 256), A("di", 0, 256))
     for q in range(4):
-        if q < 3:
+        if q < OPT["nact"]:
             act("rout", RQ(q), A("R", 1024 * q, 1024 * q + 1024), AF.Copy)
         else:
             cp(RQ(q), A("R", 1024 * q, 1024 * q + 1024))
@@ -606,13 +615,13 @@ def rank_program(g, core, T, topo):
     act("yv", A("sel"), IN(A("IOTA"), A("v4u", 32, 64)), AF.Copy)
     dma("act", H("yv"), A("sel", p=slice(0, 128, 16)), "out")
     dma("sp", H("yl"), A("VL", 0, 512), "out")
-    dma("sp", H("yx"), A("x4b"), "out")
-    for q in (0, 3, 1, 2):
+    for q in (2, 0, 3, 1):
         dma("sp", (T["yr"][:, 1024 * q:1024 * q + 1024], [], []), RQ(q), "out")
+    dma("act", H("yx"), A("x4b"), "out")
     for h in range(2):
         dma("sp", (T["ys"][4 * h:4 * h + 4, :], [], []), A("scan", 128 * h, 128 * h + 128), "out")
 
-    seq = tags["xc0"] + tags["rin0"] + tags["mask0"] + tags["rin1"] + tags["rin2"] + tags["rin3"]
+    seq = tags["k0"] + tags["k1"] + tags["xc0"] + tags["rin0"] + tags["mask0"] + tags["rin1"] + tags["rin2"] + tags["rin3"]
     for t in range(NSTEP):
         tg = lambda nm: tags.get(nm + str(t), [])
         gs, vs, cb = tg("G"), tg("V"), tg("CB")
@@ -622,9 +631,9 @@ def rank_program(g, core, T, topo):
         rest = vs[n2:]
         for m, i in enumerate(cb):
             seq += [i] + rest[m:m + 1]
-        for nm in OPT["tail"].split():
+        for nm in OPT["tail" if t < NSTEP - 1 else "end"].split():
             seq += tags.get("mask%d" % (t + 1), []) if nm == "mask" else tg(nm)
-    seq += tags["rout"][:1] + tags["yv"] + tags["rout"][1:]
+    seq += tags["rout"] + tags["yv"]
     for a, b in zip(seq, seq[1:]):
         ops[b]["after"].append(a)
 

@@ -14,8 +14,8 @@ _decl("sbuf", "bfloat16", "EF:4096 G:8192 EQ:8192 MK:784 onesw:144 ones960:144 j
       "idb:128 neg2:128 blk:128 ones:128 wexp:512 we:24 wg:8 seld:2048 x0b:512 x1b:512 x2b:512 x3b:512 x4b:512 "
       "xo0:512 xo1:512 xo2:512 xo3:512 mask0:512 mask1:512 nmask:512 gw:512 eqw:512 eqd:512 eqv:256 tvf:512 tcf:512 tbf:512 rc:512 "
       "iob:128 neg4:128 onesn:144 c36:512 eqc:512 z:512 efg:512 sg:512 ntg:32 cl:32")
-_decl("sbuf", "float32", "R:4608 SU:4608 VL:1024 TT:5632 TV:4608 IOTA:4096 cv:1024 gk:512 am:256 oneswf:144 ow2:144 idf:128 ids:128 lw:256 "
-      "sc0:128 col:32 sm:1280 base5:160 del5:160 prod5:160 sum5:160 mn2:64 dum2:64 sel:512 verf:512 keyl:512 scan:512 expd:256 val:512 "
+_decl("sbuf", "float32", "R:4608 SU:4608 VL:1024 TT:5632 TV:4608 IOTA:4128 cv:1024 gk:128 am:256 oneswf:144 ow2:144 idf:128 ids:128 lw:256 "
+      "sc0:128 col:32 sm:1280 base5:160 del5:160 prod5:160 sum5:160 mn2:64 kt:96 dum2:64 sel:512 verf:512 keyl:512 scan:512 expd:256 val:512 "
       "x32:512 scf:512 dv:512 dm:512 vm:512 pg:512 tmpf:128")
 _decl("sbuf", "int32", "smi:256 coli:32 di:512 ei:1024 sci:512")
 _decl("sbuf", "uint16", "v0u:64 v1u:64 v2u:64 v3u:64 v4u:64 of0:160 of1:160 of2:160 of3:160 smu:224 veru:512 ofcb:64 ofb:64 ofv:64 exu:16")
@@ -24,11 +24,12 @@ _decl("sbuf", "float16", "dif:1024 idh:128 key2:64 keyv:32 w8:144 v0h:512")
 DMASEMS = ["dx", "dv0", "de", "dver", "dr0", "dr1", "dr2", "dr3", "deff", "dsu", "dtt", "dtv", "out"]
 SEMAPHORES = ["pe", "act", "dve", "pool", "sent"] + DMASEMS + ["ax%d" % t for t in range(1, 5)] + ["av%d" % t for t in range(1, 5)]
 NSTEP, HOP, BIGW = 4, 3, 262144.0
-CYC, PEC, GATH, SCAT, FIX, WAKE = 0.00083, 0.0006, 1.56, 3.8, 0.05, 0.06
+CYC, PEC, GATH, SCAT, FIX, WAKE = 0.00083, 0.00066, 1.56, 3.8, 0.05, 0.06
 ORDER = {}
-OPT = {"split": False, "nv1": 20, "nv2": 10, "rounds": 4, "halves": (), "xc": 0, "gw": 0,
-       "between": ("", "hn", "", "snc"), "tail": "tc tv x32 sn ef sg mask xo rg rn",
-       "end": "tc tv x32 sn ef rg sg rn xo", "x32": 1, "snd": 0, "nact": 2, "ofs": ((3, 4), (0, 2), (2, 3), (4, 5))}
+OPT = {"split": False, "nv1": 4, "nv2": 4, "rounds": 4, "seed": 0, "xc": 0, "nm": 1, "eps": 1.0, "halves": (), "gw": 0, "lag": 1, "hup": 24, "yup": 18, "scp": 20, "sca": 0,
+       "between": ("eqw", "thr", "", ""), "tail": "tc tv x32 sn ef sg mask xo rg rn ma",
+       "end": "tc tv x32 sn ef rg sg rn xo ma", "ma": 0, "x32": 1, "snd": 0, "tbd": 0, "head": "k0 k1 xc0 mask0 rin0 k2 rin1 rin2 rin3",
+       "nact": 2, "ofs": ((3, 4), (0, 2), (2, 3), (4, 5))}
 
 
 def schedule(ops):
@@ -78,6 +79,21 @@ def schedule(ops):
     load = [bool(o["dma"]) and not o["rd"] and not o["ext"] for o in ops]
     rank_in = {i: m for m, i in enumerate(topo_order)}
     seq = sorted(range(n), key=lambda i: (not load[i], i if load[i] else -prio[i], rank_in[i]))
+    if OPT["seed"]:
+        z, key = OPT["seed"], []
+        for i in range(n):
+            z = (z * 1103515245 + 12345) % 2147483648
+            key.append(1.0e9 - i if load[i] else prio[i] + OPT["eps"] * z / 2147483648)
+        left = [len(p) for p in pred]
+        ready, seq = [i for i in range(n) if not left[i]], []
+        while ready:
+            i = max(ready, key=lambda m: key[m])
+            ready.remove(i)
+            seq.append(i)
+            for k, _ in succ[i]:
+                left[k] -= 1
+                if not left[k]:
+                    ready.append(k)
     best = None
     for _ in range(OPT["rounds"]):
         st = place(seq, pred, False)
@@ -203,8 +219,8 @@ def rank_program(g, core, T, topo):
     H = lambda name: (T[name][:], [], [])
     C = lambda j: A("col", j, j + 1, key=j)
     S = lambda j: A("sm", 32 * j, 32 * j + 32, key=j)
-    SI = lambda j: A("smi", 32 * j, 32 * j + 32, key=j)
-    SUU = lambda j: A("smu", 32 * j, 32 * j + 32, key=j)
+    SI = lambda j: A("smi", 32 * j, 32 * j + 32, key=["6_0", "6_1"] if j == 6 else j)
+    SUU = lambda j: A("smu", 32 * j, 32 * j + 32, key=["2_0", "2_1"] if j == 2 else j)
     P5 = lambda nm, q: A(nm, 32 * q, 32 * q + 32, key=q)
     TM = lambda j: A("tmpf", 8 * j, 8 * j + 8, key=j)
     RQ = lambda q: A("EQ", 1024 * q, 1024 * q + 1024, key="r%d" % q)
@@ -232,14 +248,21 @@ def rank_program(g, core, T, topo):
     iota(A("coli", 0, 1, key=0), [[0, 1]], 0, 1, flt=False)
     iota(io(256), [[1, 256]], after=(len(ops) - 1,))
     iota(A("MK"), [[0, 49], [1, 16]], after=(len(ops) - 1,))
+    iota(A("iob"), [[1, 128]], after=(len(ops) - 1,))
     iota(S(LANE), [[16, 32]], after=(len(ops) - 1,))
-    iota(A("gk"), [[0, 4], [16, 8], [0, 16]], after=(len(ops) - 1,))
+    iota(A("gk"), [[16, 8], [0, 16]], after=(len(ops) - 1,))
+    iota(TM(5), [[0, 8]], 4, after=(len(ops) - 1,))
+    iota(TM(6), [[0, 8]], 1, after=(len(ops) - 1,))
+    iota(A("wexp"), [[0, 512]], after=(len(ops) - 1,))
+    iota(A("ones"), [[0, 128]], 1, after=(len(ops) - 1,))
+    iota(S(OWN1), [[8192, 32]], 262144, after=(len(ops) - 1,))
+    iota(S(OWN2), [[32, 32]], 1016, after=(len(ops) - 1,))
     iota(A("am"), [[0, 32], [16, 8]], after=(len(ops) - 1,))
-    iota(A("tmpf", 0, 16, key=[0, 1]), [[16, 4], [64, 2], [256, 2]], 15, after=(len(ops) - 1,))
+    iota(A("tmpf", 0, 16, key=[0, 1]), [[0, 2], [16, 4], [64, 2]], 15, after=(len(ops) - 1,))
     iota(A("lw"), [[0, 4], [1, 64]], -48, after=(len(ops) - 1,))
     iota(A("c36"), [[0, 512]], 36, after=(len(ops) - 1,))
     iota(A("cv"), [[1, 32], [0, 32]], 32, after=(len(ops) - 1,))
-    for j, c in ((B31N, -31.0), (B5N, -5.0), (B35, -3.5), (B2N, -2.0), (B36, 36.0), (LIM, 196608.0)):
+    for j, c in ((B31N, -31.0), (B5N, -5.0), (B35, -3.5), (B2N, -2.0), (B36, 36.0), (T4, 1.0), (T5, 0.5), (LIM, 196608.0)):
         ms(C(j), c)
     cp(C(PART), A("coli", 0, 1, key=0))
     ts(A("coli", 1, 2, key=1), A("coli", 0, 1, key=0), 15, band)
@@ -252,7 +275,7 @@ def rank_program(g, core, T, topo):
     ts(C(MLO), C(P16), 8.0, lt)
     ts(C(MHI), C(P16), 8.0, ge)
     ts(A("jw"), io(144), C(G16P), eq, C(TWOF), mul)
-    act("k0", A("jw4"), A("jw"), AF.Copy, None, -4.0)
+    act("k0", A("jw4"), A("jw"), AF.Copy, None, -2.0)
     ts(A("w8"), io(144), C(T1), eq)
     ts(A("oneswf"), io(144), C(G16P), eq)
     ts(A("ow2"), io(144), C(T3), eq)
@@ -272,15 +295,11 @@ def rank_program(g, core, T, topo):
     cp(A("VL", 0, 512), A("ei", 512, 1024, key=[2, 3]))
     act("k0", A("onesw"), A("oneswf"), AF.Copy)
     act("k0", A("ones960"), A("oneswf"), AF.Copy, None, 960.0)
-    ms(A("ones"), 1.0)
-    ms(TM(5), 4.0)
-    ms(TM(6), 1.0)
     scan(TM(7), TM(5), TM(6), 0.25, mul, mul)
     for j, sh, a in ((PLO, 0.0, 8), (PHI, 8.0, 12)):
         ts(TM(a), io(8), sh, add, C(P16), eq)
         tt(TM(a + 1), TM(a), TM(7), mul)
         red(C(j), TM(a + 1))
-    ms(A("wexp"), 0.0)
     ts(A("wexp", 128, 256), A("gk", 0, 128), C(G16), eq, C(PLO), mul)
     ts(A("wexp", 256, 384), A("gk", 0, 128), C(G16), eq, C(PHI), mul)
     ts(A("blk"), A("gk", 0, 128), C(G16), eq)
@@ -292,12 +311,9 @@ def rank_program(g, core, T, topo):
     ts(S(DUMV), S(LANE), 512.0, add)
     ts(A("dum2", 0, 32), S(LANE), 2048.0, add)
     ts(A("dum2", 32, 64), S(LANE), 512.0, add)
-    cp(P5("base5", 2), S(DUMR))
-    cp(P5("base5", 3), S(DUMR))
-    cp(P5("base5", 4), S(DUMV))
-    ts(S(OWN2), io(32), 32.0, mul, 1016.0, add)
-    ts(S(OWN1), io(32), 8192.0, mul, 262144.0, add)
-    cp(A("iob"), io(128))
+    act("k2", P5("base5", 2), S(DUMR), AF.Copy)
+    act("k2", P5("base5", 3), S(DUMR), AF.Copy)
+    act("k2", P5("base5", 4), S(DUMV), AF.Copy)
     ts(A("idb"), A("iob"), C(PART), eq)
     cp(A("idh"), A("idb"))
     mm(A("B7", 0, 128), A("idb"), A("idb"), True, True)
@@ -334,7 +350,7 @@ def rank_program(g, core, T, topo):
         asel(A("seld"), A("seld"), [[-1, 16], [-16, 8], [0, 16]], eq, 0.0, 0, 1)
 
     seld(0)
-    iota(A("IOTA", 256, 4096, key=1), [[1, 3840]], 256)
+    iota(A("IOTA", 256, 4128, key=1), [[1, 3872]], 256)
     for q in range(8):
         dma("sp", A("TV", 512 * q, 512 * q + 512, key=q), A("SU", 0, 512, key=0), "dtv", 8.0)
     for q in (0, 1, 2, 3, 4, 5, 6, 7, 9):
@@ -361,7 +377,7 @@ def rank_program(g, core, T, topo):
         cp(SUU(0), SI(3))
         cp(SUU(1), SI(4))
         act("gw%d" % t, A("gw"), IN(Rw, SUU(1)), AF.Square, C(B31N))
-        for a, b in ((0, 1), (1, 4)):
+        for a, b in ((3, 4), (0, 3)):
             cp(A("veru", 128 * a, 128 * b, key=list(range(a, b))), IN(A("VL", 0, 512), A("smu", 8 * a, 8 * b, key=0)))
 
     def main(t):
@@ -369,22 +385,25 @@ def rank_program(g, core, T, topo):
         last = t == NSTEP - 1
         act("xc%d" % t, A("B4"), A(x), AF.Square, C(B5N), 4.0)
         parts = []
-        for ch in range(4):
+        for ch in (3, 2, 1, 0):
             parts += [(ch, 0, 64), (ch, 64, 128)] if ch in OPT["halves"] else [(ch, 0, 128)]
         gkey = lambda ch, a: "%d_%d" % (ch, a)
         for ch, a, b in parts:
             act("G%d" % t, A("G", 2048 * ch + 16 * a, 2048 * ch + 16 * b, key=gkey(ch, a)),
                 IN(Rw, A("veru", 128 * ch + a, 128 * ch + b, key=ch)), AF.Square, C(B31N))
-        ts(A("nmask"), A("mask%d" % (t % 2)), -1.0, mul, 1.0, add)
+        if OPT["nm"]:
+            act("nm%d" % t, A("nmask"), A("mask%d" % (t % 2)), AF.Identity, C(T4), -1.0)
+        else:
+            ts(A("nmask"), A("mask%d" % (t % 2)), -1.0, mul, 1.0, add)
         if OPT["x32"]:
             act("x32%d" % t, A("x32"), A(x), AF.Identity, C(B36), -4.0)
         else:
             ts(A("x32"), A(x), -4.0, mul, 36.0, add)
         for ch in range(4):
-            mm(A("B%d" % ch), A("ones"), A("wexp"), True, False)
+            mm(A("B%d" % ch, 0, 256), A("wexp", 0, 128), A("c36", 0, 256), True, False)
         cp(A("verf"), A("veru"))
         for ch in range(4):
-            mm(A("B%d" % ch, 384, 512), A("verf", 128 * ch, 128 * ch + 128), A("ids"), False, False)
+            mm(A("B%d" % ch, 128, 256), A("verf", 128 * ch, 128 * ch + 128), A("ids"), False, False)
         ts(A("keyv"), vu, -2048.0, add)
         for d in range(8):
             mm(A("B6", 32 * d, 32 * d + 32), A("dif", 128 * d, 128 * d + 128, key=d), A("keyv"), True, True)
@@ -398,17 +417,6 @@ def rank_program(g, core, T, topo):
         for c in range(31, -1, -1):
             act("V%d" % t, IN(A("TV"), A("ofv", 2 * c, 2 * c + 1)), A("cv", 32 * c, 32 * c + 16), AF.Silu)
         act("tv%d" % t, A("tvf"), IN(A("TV", 0, 4096), vu), AF.Copy)
-        if not last:
-            mm(A("B6"), A("idb"), A(x), True, False)
-            mm(A("B6"), A("idb"), A("EF", t, 4096, 8), False, True)
-            ts(A("hn"), A("B6"), 4.0, ge)
-            tag("hn%d" % t)
-            f2w(A("B6", 256, 288), "jw", x, last=False)
-            for p0 in range(16):
-                mm(A("B6", 256, 288), A("jw", 16 - p0, 144 - p0), A("EF", t + 8 * p0, 4096, 128), False, False)
-            f2w(A("B6", 256, 288), "jw4", "hn", first=False)
-            cp(S(SN), A("B6", 256, 288))
-            tag("snc%d" % t)
         for ch in range(4):
             mine = [q for q in parts if q[0] == ch]
             old = ["r%d" % (2 * ch), "r%d" % (2 * ch + 1)] if ch < 2 and t in (0, NSTEP - 1) else []
@@ -424,7 +432,7 @@ def rank_program(g, core, T, topo):
                 mm(A("B%d" % ch, k, 128, 16), A("EQ", base, base + 128, key=["%d_%d_%d" % (ch, k, q[1]) for q in mine]), A("we", 0, 8), False, k == 15)
             sl = lambda nm: A(nm, 128 * ch, 128 * ch + 128, key=ch)
             ts(sl("di"), A("B%d" % ch, 0, 128), -1.0 / 960, mul, 16.41, add)
-            tt(sl("keyl"), sl("di"), A("B%d" % ch, 384, 512), add)
+            tt(sl("keyl"), sl("di"), A("B%d" % ch, 128, 256), add)
             scan(sl("scan"), A("sc0"), sl("keyl"), 0.0, add, mn)
             tag("S%d_%d" % (t, ch))
             mm(A("B%d" % ch, 128, 384), A("ones"), A("wexp", 128, 384), True, False)
@@ -442,11 +450,20 @@ def rank_program(g, core, T, topo):
         tt(S(KN), a, b, mul)
         ts(S(THR), S(KN), 1.0e9, mul, 65536.0, add)
         tag("thr%d" % t)
+        if not last:
+            mm(A("B7"), A("idb"), A(x), True, False)
+            mm(A("B7"), A("idb"), A("EF", t, 4096, 8), False, True)
+            act("hn%d" % t, A("hn"), A("B7"), AF.Sign, C(B35))
+            for p0 in range(16):
+                mm(A("B7", 256, 288), A("jw", 16 - p0, 144 - p0), A("EF", t + 8 * p0, 4096, 128), p0 == 0, False)
+            f2w(A("B7", 256, 288), "jw4", "hn", first=False)
+            ts(S(CNT), A("v%du" % t, 0, 32), -512.0, add)
+            tt(S(SN), A("B7", 256, 288), S(CNT), add)
         chain = []
         for ch, a, b in parts:
             if a == 0:
-                chain += tags["S%d_%d" % (t, ch - 2)] if ch >= 2 else []
-                for nm in OPT["between"][ch].split():
+                chain += tags["S%d_%d" % (t, ch + OPT["lag"])] if ch + OPT["lag"] < 4 else []
+                for nm in OPT["between"][3 - ch].split():
                     chain += tags.get(nm + str(t), [])
             chain += tags["E%d_%d_%d" % (t, ch, a)]
         for a, b in zip(chain, chain[1:]):
@@ -458,41 +475,46 @@ def rank_program(g, core, T, topo):
     def decide(t):
         x, of = "x%db" % t, "of%d" % t
         last = t == NSTEP - 1
-        tt(A("expd"), IN(A("scan"), A("exu")), A("am"), mul)
-        for gg in range(4):
-            mm(A("B5", 128, 192), A("lw", 112 - 16 * gg, 240 - 16 * gg), A("expd", 64 * gg, 64 * gg + 64), gg == 0, gg == 3)
-        ts(A("smi", 160, 192, key=5, p=slice(0, 64)), A("B5", 128, 160, p=slice(0, 64)), 61440.0, add)
-        ts(A("smi", 160, 192, key=7, p=slice(64, 128)), A("B5", 160, 192, p=slice(64, 128)), 61440.0, add)
-        K = A("smi", 160, 192, key=[5, 7])
-        a, b = tmp(), tmp()
-        ts(SI(6), K, 4095, band)
-        tt(a, K, S(THR), lt)
-        ts(b, SI(6), -2048.0, add)
-        ts(S(SENT), a, 4096.0, mul, -2048.0, add)
-        cp(SUU(2), SI(6))
-        tt(A("key2", 0, 32, key=0), b, S(SENT), mx)
-        tt(A("key2", 32, 64, key=1), SI(3), S(SENT), mx)
+        for pt in (1, 0):
+            c0 = 16 * pt
+            part = lambda ap, key: A(ap[0], ap[1] + c0, ap[1] + c0 + 16, key=key)
+            ex = A("expd", 128 * pt, 128 * pt + 128, key=pt)
+            tt(ex, IN(A("scan", 256 * pt, 256 * pt + 256, key=[2 * pt, 2 * pt + 1]), A("exu", 0, 8)), A("am", 0, 128), mul)
+            for gg in range(4):
+                mm(A("B5", 128, 160), A("lw", 112 - 16 * gg, 240 - 16 * gg), A("expd", 128 * pt + 32 * gg, 128 * pt + 32 * gg + 32, key=pt), gg == 0, gg == 3)
+            for h in range(2):
+                rows = slice(64 * h, 64 * h + 64)
+                ts(A("smi", 160 + c0, 176 + c0, key="5_%d_%d" % (pt, h), p=rows), A("B5", 128 + 16 * h, 144 + 16 * h, p=rows), 61440.0, add)
+            kp, cc = part(("smi", 160), ["5_%d_0" % pt, "5_%d_1" % pt]), part(("smi", 192), "6_%d" % pt)
+            a, b, sent = part(("kt", 0), "a%d" % pt), part(("kt", 32), "b%d" % pt), part(("kt", 64), "s%d" % pt)
+            ts(cc, kp, 4095, band)
+            tt(a, kp, part(("sm", 32 * THR), THR), lt)
+            ts(b, cc, -2048.0, add)
+            ts(sent, a, 4096.0, mul, -2048.0, add)
+            cp(part(("smu", 64), "2_%d" % pt), cc)
+            tt(A("key2", 32 * pt, 32 * pt + 16, key="c%d" % pt), b, sent, mx)
+            tt(A("key2", 32 * pt + 16, 32 * pt + 32, key="b%d" % pt), part(("smi", 96), 3), sent, mx)
+            k2 = A("key2", 32 * pt, 32 * pt + 32, key=["c%d" % pt, "b%d" % pt])
+            for d in range(8):
+                mm(A("B6", 32 * d, 32 * d + 32), A("dif", 128 * d, 128 * d + 128, key=d), k2, True, True)
+            ts(A("eqd", 256 * pt, 256 * pt + 256, key=pt), A("B6", 0, 256), 0.0, eq)
+            for d in range(8):
+                mm(A("B5", 192, 224), A("bk", 128 * d, 128 * d + 128, key=d), A("eqd", 256 * pt + 32 * d, 256 * pt + 32 * d + 32, key=pt), d == 0, False)
+            mm(A("B5", 192, 224), A("idh"), k2, False, True)
+            for h, lift in ((0, 2048.0), (1, 4608.0)):
+                m2 = part(("mn2", 32 * h), "%d_%d" % (h, pt))
+                tt(m2, A("B5", 192 + 16 * h, 208 + 16 * h), part(("dum2", 32 * h), None), mn)
+                ts(A("ofcb", 2 * c0 + h, 2 * c0 + 32, 2, key="%d_%d" % (h, pt)), m2, lift, add)
+            for c in range(c0 + 15, c0 - 1, -1):
+                act("CB%d" % t, IN(A("TT"), A("ofcb", 2 * c, 2 * c + 2, key=["0_%d" % pt, "1_%d" % pt])), A("cv", 32 * c, 32 * c + 32), AF.Silu)
+        K = A("smi", 160, 192, key=["5_0_0", "5_0_1", "5_1_0", "5_1_1"])
         act("rc%d" % t, A("rc"), IN(Rw, SUU(2)), AF.Square, C(B31N))
-        for d in range(8):
-            mm(A("B6", 64 * d, 64 * d + 64), A("dif", 128 * d, 128 * d + 128, key=d), A("key2"), True, True)
         ts(A("ntg"), K, C(LIM), ge)
-        ts(A("eqd"), A("B6"), 0.0, eq)
-        for d in range(8):
-            mm(A("B5", 192, 256), A("bk", 128 * d, 128 * d + 128, key=d), A("eqd", 64 * d, 64 * d + 64), d == 0, False)
-        mm(A("B5", 192, 256), A("idh"), A("key2"), False, True)
-        tt(A("mn2"), A("B5", 192, 256), A("dum2"), mn)
-        ts(A("ofcb", 0, 64, 2, key=0), A("mn2", 0, 32), 2048.0, add)
-        if OPT["split"]:
-            cp(A("ofb", 0, 64, 2), A("mn2", 32, 64))
-            for c in range(31, -1, -1):
-                act("CB%d" % t, IN(A("TT", 0, 4608, key="c"), A("ofcb", 2 * c, 2 * c + 1, key=0)), A("cv", 32 * c, 32 * c + 16), AF.Silu)
-                act("CB%d" % t, IN(A("TT", 4608, 5632, key="b"), A("ofb", 2 * c, 2 * c + 1)), A("cv", 32 * c, 32 * c + 16), AF.Silu)
-        else:
-            ts(A("ofcb", 1, 64, 2, key=1), A("mn2", 32, 64), 4608.0, add)
-            for c in range(31, -1, -1):
-                act("CB%d" % t, IN(A("TT"), A("ofcb", 2 * c, 2 * c + 2)), A("cv", 32 * c, 32 * c + 32), AF.Silu)
         act("tc%d" % t, A("tcf"), IN(A("TT", 0, 4096), SUU(2)), AF.Copy)
-        act("tc%d" % t, A("tbf"), IN(A("TT", 4608, 5120), SUU(0)), AF.Copy)
+        if OPT["tbd"]:
+            cp(A("tbf"), IN(A("TT", 4608, 5120), SUU(0)))
+        else:
+            act("tc%d" % t, A("tbf"), IN(A("TT", 4608, 5120), SUU(0)), AF.Copy)
         tt(A("eqc"), A("rc"), A("B4"), eq)
         mm(A("B6"), A("idb"), A("c36"), True, False)
         mm(A("B6"), A("neg4"), A(x), False, True)
@@ -520,15 +542,21 @@ def rank_program(g, core, T, topo):
         tt(P5("del5", 3), S(NDC), A("ntg"), mul)
         if not last:
             cp(SUU(5), P5("base5", 1))
-            tt(A("yu"), IN(A("EF"), SUU(5)), A(x), add)
-            ts(A("hu"), A("yu"), 4.0, ge)
+            act("yu%d" % t, A("yu"), IN(A("EF"), SUU(5)), AF.Copy)
+            mm(A("B6"), A("idb"), A(x), True, False)
+            mm(A("B6"), A("idb"), A("yu"), False, True)
+            act("hu%d" % t, A("hu"), A("B6"), AF.Sign, C(B35))
             f2w(A("B6", 0, 32), "jw", "yu", last=False)
             f2w(A("B6", 0, 32), "jw4", "hu", first=False)
-            cp(P5("base5", 0), A("B6", 0, 32))
+            tt(P5("base5", 0), A("B6", 0, 32), S(CNT), add)
             a = tmp()
             tt(a, S(SN), P5("base5", 0), sub)
             tt(P5("del5", 0), a, A("ntg"), mul)
-        cp(A("sci"), IN(SUw, SUU(2)))
+        if OPT["sca"]:
+            act("sc%d" % t, A("scf"), IN(SUw, SUU(2)), AF.Copy)
+            cp(A("sci"), A("scf"))
+        else:
+            cp(A("sci"), IN(SUw, SUU(2)))
         ts(A("sci"), A("sci"), 511, band)
         ts(A("scf"), A("sci"), 4096.0, add)
         for ch in range(4):
@@ -538,7 +566,11 @@ def rank_program(g, core, T, topo):
             tt(A("z", 128 * ch, 128 * ch + 128, key=ch), A("ei", 256 * ch, 256 * ch + 128, key=ch), A("ei", 256 * ch + 128, 256 * ch + 256, key=ch), add)
             mm(A("B7", 128 * ch, 128 * ch + 128), A("z", 128 * ch, 128 * ch + 128, key=ch), A("idb"), False, ch == 3)
         tt(A("dv"), IN(A("IOTA"), SUU(6)), A("verf"), sub)
-        ts(A("B7"), A("B7"), 0.5, lt)
+        if OPT["ma"]:
+            act("ma%d" % t, A("B7"), A("B7"), AF.Sign, C(T5), -1.0)
+            act("ma%d" % t, A("B7"), A("B7"), AF.Relu)
+        else:
+            ts(A("B7"), A("B7"), 0.5, lt)
         tt(A("dm"), A("dv"), A("B7"), mul)
         f2w(A("B5", 256, 288), "onesw", "tcf", last=False)
         f2w(A("B5", 256, 288), "onesw", "tbf", first=False)
@@ -621,18 +653,29 @@ def rank_program(g, core, T, topo):
     for h in range(2):
         dma("sp", (T["ys"][4 * h:4 * h + 4, :], [], []), A("scan", 128 * h, 128 * h + 128), "out")
 
-    seq = tags["k0"] + tags["k1"] + tags["xc0"] + tags["rin0"] + tags["mask0"] + tags["rin1"] + tags["rin2"] + tags["rin3"]
+    seq = []
+    for nm in OPT["head"].split():
+        seq += tags[nm]
     for t in range(NSTEP):
         tg = lambda nm: tags.get(nm + str(t), [])
         gs, vs, cb = tg("G"), tg("V"), tg("CB")
-        n1, n2 = OPT["nv1"], OPT["nv1"] + OPT["nv2"]
-        xa, ga = OPT["xc"], OPT["gw"]
-        seq += (tg("gw") if ga else []) + gs[:xa] + (tg("xc") if t else []) + gs[xa:] + ([] if ga else tg("gw")) + vs[:n1] + tg("rc") + vs[n1:n2]
-        rest = vs[n2:]
+        n1, n2, ga = OPT["nv1"], OPT["nv2"], OPT["gw"]
+        if OPT["xc"] and t:
+            gs = gs[:1] + tg("xc") + gs[1:]
+        seq += (tg("xc") if t and not OPT["xc"] else []) + gs[:ga] + tg("gw") + gs[ga:] + tg("hn") + tg("nm") + (tg("x32") if OPT["x32"] == 2 else []) + vs[:n1]
+        rest = vs[n1:]
         for m, i in enumerate(cb):
-            seq += [i] + rest[m:m + 1]
+            if m == 16:
+                seq += rest[:n2] + tg("rc")
+                rest = rest[n2:]
+            for nm in ("yu", "sc", "hu"):
+                if m == OPT[nm + "p"]:
+                    seq += tg(nm)
+            seq += [i] + rest[:1]
+            rest = rest[1:]
+        seq += rest
         for nm in OPT["tail" if t < NSTEP - 1 else "end"].split():
-            seq += tags.get("mask%d" % (t + 1), []) if nm == "mask" else tg(nm)
+            seq += tags.get("mask%d" % (t + 1), []) if nm == "mask" else [] if nm == "x32" and OPT["x32"] == 2 else tg(nm)
     seq += tags["rout"] + tags["yv"]
     for a, b in zip(seq, seq[1:]):
         ops[b]["after"].append(a)

@@ -10,26 +10,28 @@ def _decl(where, dtype, spec):
 
 
 _decl("psum", "float32", "B0:512 B1:512 B2:512 B3:512 B4:512 B5:512 B6:512 B7:512")
-_decl("sbuf", "bfloat16", "EF:4096 G:8192 EQ:8192 MK:784 onesw:144 ones960:144 jw:144 jw4:144 hn:512 yu:512 hu:512 bk:1024 "
-      "idb:128 neg2:128 blk:128 ones:128 wexp:512 we:24 wg:8 seld:2048 x0b:512 x1b:512 x2b:512 x3b:512 x4b:512 "
-      "xo0:512 xo1:512 xo2:512 xo3:512 mask0:512 mask1:512 nmask:512 gw:512 eqw:512 eqd:512 eqv:256 tvf:512 tcf:512 tbf:512 rc:512 "
-      "iob:128 neg4:128 onesn:144 c36:512 eqc:512 z:512 efg:512 sg:512 ntg:32 cl:32")
-_decl("sbuf", "float32", "R:4608 SU:4608 VL:1024 TT:5632 TV:4608 IOTA:4128 cv:1024 gk:128 am:256 oneswf:144 ow2:144 idf:128 ids:128 lw:256 "
-      "sc0:128 col:32 sm:1280 base5:160 del5:160 prod5:160 sum5:160 mn2:64 kt:96 dum2:64 sel:512 verf:512 keyl:512 scan:512 expd:256 val:512 "
-      "x32:512 scf:512 dv:512 dm:512 vm:512 pg:512 tmpf:128")
-_decl("sbuf", "int32", "smi:256 coli:32 di:512 ei:1024 sci:512")
-_decl("sbuf", "uint16", "v0u:64 v1u:64 v2u:64 v3u:64 v4u:64 of0:160 of1:160 of2:160 of3:160 smu:224 veru:512 ofcb:64 ofb:64 ofv:64 exu:16")
-_decl("sbuf", "float16", "dif:1024 idh:128 key2:64 keyv:32 w8:144 v0h:512")
+_decl("sbuf", "bfloat16", "EF:4096 G:8192 EQ:8192 MK:784 wide:576 bk:1024 idm:768 blk:128 wexp:256 we:24 wg:8 wsel:2048 seld:2048 "
+      "x0r:512 x0b:512 x1b:512 x2b:512 x3b:512 x4b:512 xo0:512 xo1:512 xo2:512 xo3:512 mask0:512 mask1:512 gw:512 eqw:512 eqd:512 eqv:256 "
+      "tcb:1024 tvf:512 yu:512 hu:512 hn:512 rc:512 eqc:512 z:512 efg:512 sg:512 eat:512 iob:128 cst:416 c2112:512 cneg:512 smb:192")
+_decl("sbuf", "float32", "R:5120 SU:4608 VL:1024 TT:5632 ENC:4096 io:256 cv:1024 gk:128 ow2:144 oneswf:144 idf:384 lw:256 sc0:128 col:32 "
+      "TV:4112 sm:640 ev:64 eD:64 d0:128 d1:128 vs:128 dum3:96 a3:96 sel:512 verf:512 scan:576 expd:256 val:512 vm:512 pg:512 "
+      "nv1:512 nv2:512 keyl:512 tmpf:128")
+_decl("sbuf", "int32", "smi:160 coli:32 ei:1024 sci:512")
+_decl("sbuf", "uint16", "v0u:64 v1u:64 v2u:64 v3u:64 v4u:64 of0:64 of1:64 of2:64 of3:64 og:96 smu:128 veru:512 ofcb:64 ofv:64 ofp:32 exu:16")
+_decl("sbuf", "float16", "dif:1024 idh:512 wselh:2048 key2:64 smh:96 w8:144 v0h:512 verh:512 sch:512")
 
 DMASEMS = ["dx", "dv0", "de", "dver", "dr0", "dr1", "dr2", "dr3", "deff", "dsu", "dtt", "dtv", "out"]
 SEMAPHORES = ["pe", "act", "dve", "pool", "sent"] + DMASEMS + ["ax%d" % t for t in range(1, 5)] + ["av%d" % t for t in range(1, 5)]
-NSTEP, HOP, BIGW = 4, 3, 262144.0
-CYC, PEC, GATH, SCAT, FIX, WAKE = 0.00083, 0.00066, 1.56, 3.8, 0.05, 0.06
+NSTEP, HOP = 4, 3
+D1, FAR = 262144.0, 524288.0
+GUESS = ((0.00087, 1.56, 3.8, 0.00046, 0.12), (0.00095, 1.15, 2.0, 0.0006, 0.14), (0.00105, 1.95, 5.2, 0.0005, 0.08))
 ORDER = {}
-OPT = {"split": False, "nv1": 4, "nv2": 4, "rounds": 4, "seed": 0, "xc": 0, "nm": 1, "eps": 1.0, "halves": (), "gw": 0, "lag": 1, "hup": 24, "yup": 18, "scp": 20, "sca": 0,
-       "between": ("eqw", "thr", "", ""), "tail": "tc tv x32 sn ef sg mask xo rg rn ma",
-       "end": "tc tv x32 sn ef rg sg rn xo ma", "ma": 0, "x32": 1, "snd": 0, "tbd": 0, "head": "k0 k1 xc0 mask0 rin0 k2 rin1 rin2 rin3",
-       "nact": 2, "ofs": ((3, 4), (0, 2), (2, 3), (4, 5))}
+OPT = {"rounds": 3, "tries": 4, "noise": 0.4, "look": 1.0, "gain": 10.0, "slip": 0.05, "parts": ((3, 2), (1,), (0,)),
+       "gp": ((32, 96), (128,), (128,), (64, 64)), "gdve": 0, "ep": (1, 1, 1, 2), "expd": "dve", "tb": "dve", "gw": "dve", "rc": "dve",
+       "vw": "dve", "vl": "dve", "val": "act", "rclone": "act", "nact": 2, "tv": "act", "yu": "dve", "tvinit": "act",
+       "head": ("G.0-5 hn TV.0-3 TT.0-7~TV.4-7", "TV.0-3 G.0-1 hn G.2-5 TT.0-7~TV.4-7"),
+       "body": "TT.8-15~TV.8-15 TT.16-23~TV.16-23 TT.24-27~TV.24-27 hu TT.28-31~TV.28-31 tcb tvf val",
+       "tail": ("efg R.0 sg xo +mask R.1 VL", "R.0 efg sg VL xo")}
 
 
 def schedule(ops):
@@ -39,73 +41,88 @@ def schedule(ops):
     for k, o in enumerate(ops):
         for i in o["all"]:
             p = ops[i]
-            free = i not in o["need"] or (p["e"] == "pe" and o["e"] == "pe")
-            gap = 0.0 if free else p["lat"] + WAKE
-            pred[k].append((i, gap))
-            succ[i].append((k, gap))
-    left = [len(p) for p in pred]
-    topo_order = [i for i in range(n) if not left[i]]
-    for i in topo_order:
-        for k, _ in succ[i]:
-            left[k] -= 1
-            if not left[k]:
-                topo_order.append(k)
-    assert len(topo_order) == n
+            sync = i in o["need"] and not (p["e"] == "pe" and o["e"] == "pe")
+            pred[k].append((i, p["lat"] if sync else 0.0, sync))
+            succ[i].append((k, p["lat"] if sync else 0.0, sync))
+    costs = [[c[0] + cy * (c[1] + ga * c[2] + sc * c[3]) + pe * c[4] for c in (o["cost"] for o in ops)] for cy, ga, sc, pe, _ in GUESS]
+    eng = [o["e"] for o in ops]
+    lat = [o["lat"] for o in ops]
 
-    def place(seq, before, back):
-        busy, start = {}, [0.0] * n
-        for i in seq:
-            c, e = ops[i]["cost"], ops[i]["e"]
-            t = max([start[j] + ops[j]["cost"] + gp for j, gp in before[i]] + [ops[i]["lat"] if back else 0.0])
-            if e is not None:
-                lst = busy.setdefault(e, [])
-                lo, hi = 0, len(lst)
-                while lo < hi:
-                    mid = (lo + hi) // 2
-                    if lst[mid][1] <= t + 1e-9:
-                        lo = mid + 1
-                    else:
-                        hi = mid
-                while lo < len(lst) and lst[lo][0] < t + c - 1e-9:
-                    t = max(t, lst[lo][1])
-                    lo += 1
-                lst.insert(lo, (t, t + c))
-            start[i] = t
-        return start
+    def run(before, after, prio, back):
+        cost, wake = costs[0], GUESS[0][4]
+        left = [len(p) for p in before]
+        rel = list(lat) if back else [0.0] * n
+        ready, free, end, seq = {}, {}, [0.0] * n, []
+        todo = [i for i in range(n) if not left[i]]
 
-    prio = [0.0] * n
-    for i in reversed(topo_order):
-        prio[i] = ops[i]["cost"] + max([prio[k] + gp for k, gp in succ[i]] + [ops[i]["lat"]])
-    load = [bool(o["dma"]) and not o["rd"] and not o["ext"] for o in ops]
-    rank_in = {i: m for m, i in enumerate(topo_order)}
-    seq = sorted(range(n), key=lambda i: (not load[i], i if load[i] else -prio[i], rank_in[i]))
-    if OPT["seed"]:
-        z, key = OPT["seed"], []
-        for i in range(n):
-            z = (z * 1103515245 + 12345) % 2147483648
-            key.append(1.0e9 - i if load[i] else prio[i] + OPT["eps"] * z / 2147483648)
-        left = [len(p) for p in pred]
-        ready, seq = [i for i in range(n) if not left[i]], []
-        while ready:
-            i = max(ready, key=lambda m: key[m])
-            ready.remove(i)
+        def done(i):
             seq.append(i)
-            for k, _ in succ[i]:
+            for k, gp, sync in after[i]:
+                rel[k] = max(rel[k], end[i] + gp + (wake if sync else 0.0))
                 left[k] -= 1
                 if not left[k]:
-                    ready.append(k)
-    best = None
-    for _ in range(OPT["rounds"]):
-        st = place(seq, pred, False)
-        span = max(st[i] + ops[i]["cost"] + ops[i]["lat"] for i in range(n))
-        rank_in = {i: m for m, i in enumerate(seq)}
-        if best is None or span < best[0]:
-            best = (span, sorted(range(n), key=lambda i: (st[i], rank_in[i])))
-        back = sorted(range(n), key=lambda i: (-(st[i] + ops[i]["cost"]), -rank_in[i]))
-        sb = place(back, succ, True)
-        rank_in = {i: m for m, i in enumerate(back)}
-        seq = sorted(range(n), key=lambda i: (not load[i], i if load[i] else -(sb[i] + ops[i]["cost"]), -rank_in[i]))
-    ORDER["span"] = best[0]
+                    todo.append(k)
+
+        while True:
+            while todo:
+                i = todo.pop()
+                if eng[i] is None:
+                    end[i] = rel[i]
+                    done(i)
+                else:
+                    ready.setdefault(eng[i], []).append(i)
+            first = None
+            for e, lst in ready.items():
+                if lst:
+                    t = max(free.get(e, 0.0), min(rel[i] for i in lst))
+                    if first is None or t < first[0]:
+                        first = (t, e)
+            if first is None:
+                return seq, end
+            t, e = first
+            lst = ready[e]
+            i = max((i for i in lst if rel[i] <= t + 1e-9), key=lambda m: prio[m])
+            wait = [m for m in lst if t < rel[m] < t + OPT["look"] * cost[i] and prio[m] > prio[i] + OPT["gain"] * (rel[m] - t)]
+            if wait:
+                m = min(wait, key=lambda m: rel[m])
+                fit = [j for j in lst if max(rel[j], t) + cost[j] <= rel[m] + OPT["slip"]]
+                i = max(fit, key=lambda j: prio[j]) if fit else m
+            lst.remove(i)
+            end[i] = max(t, rel[i]) + cost[i]
+            free[e] = end[i]
+            done(i)
+
+    def span(seq, m):
+        cost, wake, end, free = costs[m], GUESS[m][4], [0.0] * n, {}
+        for i in seq:
+            t = free.get(eng[i], 0.0)
+            for j, gp, sync in pred[i]:
+                t = max(t, end[j] + gp + (wake if sync else 0.0))
+            end[i] = t + cost[i]
+            if eng[i] is not None:
+                free[eng[i]] = end[i]
+        return max(end[i] + lat[i] for i in range(n))
+
+    seq, _ = run(pred, succ, [0.0] * n, False)
+    base = [0.0] * n
+    for i in reversed(seq):
+        base[i] = costs[0][i] + max([base[k] + gp + (GUESS[0][4] if sync else 0.0) for k, gp, sync in succ[i]] + [lat[i]])
+    load = [bool(o["dma"]) and not o["rd"] and not o["ext"] for o in ops]
+    best, z, keep = None, 12345, base
+    for tr in range(OPT["tries"]):
+        prio = []
+        for i in range(n):
+            z = (z * 1103515245 + 12345) % 2147483648
+            prio.append(keep[i] + (OPT["noise"] * z / 2147483648 if tr else 0.0))
+        for r in range(OPT["rounds"]):
+            prio = [1.0e6 - i if load[i] else prio[i] for i in range(n)]
+            seq, end = run(pred, succ, prio, False)
+            spans = [span(seq, m) for m in range(len(GUESS))]
+            score = sum(s / GUESS[m][0] for m, s in enumerate(spans))
+            if best is None or score < best[0]:
+                best, keep = (score, seq, spans), prio
+            prio = run(succ, pred, end, True)[1]
+    ORDER["span"] = [round(s, 1) for s in best[2]]
     return best[1]
 
 
@@ -114,7 +131,7 @@ def rank_program(g, core, T, topo):
     if rank is None:
         return
     n_r = len(T.cores)
-    ops, tags = [], {}
+    ops, tags, step = [], {}, [-1]
     Q = {"pe": g.tensor, "act": g.scalar, "dve": g.vector, "pool": g, "sp": g.sync}
 
     def A(name, a=None, b=None, s=None, key=None, p=None):
@@ -135,17 +152,14 @@ def rank_program(g, core, T, topo):
                 rd += i[1] + i[2]
         ops.append({"e": e, "fn": fn, "rd": rd, "wr": wr, "dma": dma, "ext": ext, "inc": False, "cost": cost, "lat": lat, "after": list(after), "n": 16})
 
-    def tag(name):
-        tags.setdefault(name, []).append(len(ops) - 1)
-
-    def est(o, ins, two=False, fast=True):
+    def est(o, ins, two=False, fast=True, fix=0.0):
         n = max(o[3], ins[0][3]) if ins else o[3]
         if o[5]:
-            return FIX + n * SCAT * CYC
+            return (fix + 0.05, 0, 0, n, 0)
         if ins and ins[0][5]:
-            return FIX + n * GATH * CYC
+            return (fix + 0.05, 0, n, 0, 0)
         r = 2 if two else 0.5 if fast and all(SCRATCH[x[4]][2].endswith("16") for x in [o] + ins) else 1
-        return FIX / 2 + max(64, n * r) * CYC
+        return (fix + 0.012, max(64, n * r), 0, 0, 0)
 
     def u(x):
         return x[0] if isinstance(x, tuple) else x
@@ -172,97 +186,140 @@ def rank_program(g, core, T, topo):
     def red(o, a):
         op("dve", lambda: g.vector.tensor_reduce(o[0], a[0], AX.X, ALU.add), [o], [a], est(o, [a]))
 
-    def act(name, o, i, f, bias=None, scale=None):
+    def act(o, i, f, bias=None, scale=None):
         kw = {}
         if bias is not None:
             kw["bias"] = u(bias)
         if scale is not None:
             kw["scale"] = scale
-        op("act", lambda: g.scalar.activation(o[0], i[0], f, **kw), [o], [i, bias], 0.015 + est(o, [i], fast=False))
-        tag(name)
+        op("act", lambda: g.scalar.activation(o[0], i[0], f, **kw), [o], [i, bias], est(o, [i], fast=False, fix=0.015))
+        tags.setdefault((step[0], o[4].rstrip("0123")), []).append(len(ops) - 1)
 
-    def mm(o, l, r, start, stop):
-        c = max(64, r[3]) * (4 if SCRATCH[l[4]][2] == "float32" else 1) * PEC
-        op("pe", lambda: g.tensor.matmul(o[0], l[0], r[0], start, stop), [o], [l, r], c)
-
-    def iota(o, pat, base=0, cm=0, flt=True, after=()):
-        c = 0.13 + 2 * o[3] * CYC
-        if flt:
-            op("pool", lambda: g.iota(o[0], pat, base, cm, allow_small_or_imprecise_dtypes=True), [o], [], c, after=after)
+    def copy(e, o, i):
+        if e == "act":
+            act(o, i, AF.Copy)
         else:
-            op("pool", lambda: g.iota(o[0], pat, base, cm), [o], [], c)
+            cp(o, i)
 
-    def asel(o, i, pat, cmp, fill, base, cm):
-        op("pool", lambda: g.affine_select(o[0], i[0], pat, cmp, fill, base, cm), [o], [i], 0.17 + 2 * o[3] * CYC)
+    def mm(o, l, r, start=False):
+        c = max(min(64, l[3]), r[3]) * (4 if SCRATCH[l[4]][2] == "float32" else 1)
+        flag = [start, False]
+        op("pe", lambda: g.tensor.matmul(o[0], l[0], r[0], flag[0], flag[1]), [o], [l, r], (0.0, 0, 0, 0, c))
+        ops[-1]["flag"] = flag
+
+    pool_tail = []
+
+    def pool(fn, outs, ins, cost, chain):
+        op("pool", fn, outs, ins, cost, after=pool_tail[-1:] if chain else ())
+        if chain:
+            pool_tail.append(len(ops) - 1)
+
+    def iota(o, pat, base=0, cm=0, flt=True, chain=True):
+        c = (0.13, 2 * o[3], 0, 0, 0)
+        if flt:
+            pool(lambda: g.iota(o[0], pat, base, cm, allow_small_or_imprecise_dtypes=True), [o], [], c, chain)
+        else:
+            pool(lambda: g.iota(o[0], pat, base, cm), [o], [], c, chain)
+
+    def asel(o, i, pat, cmp, fill, base, cm, chain=True):
+        pool(lambda: g.affine_select(o[0], i[0], pat, cmp, fill, base, cm), [o], [i], (0.17, 2 * o[3], 0, 0, 0), chain)
 
     queue_tail = {}
 
     def dma(e, o, i, sem, lat=3.0):
-        op(e, lambda: Q[e].dma_start(o[0], i[0]), [o], [i], 0.1, dma=sem, lat=lat, after=queue_tail.get(e, ()))
+        op(e, lambda: Q[e].dma_start(o[0], i[0]), [o], [i], (0.1, 0, 0, 0, 0), dma=sem, lat=lat, after=queue_tail.get(e, ()))
         queue_tail[e] = (len(ops) - 1,)
 
     def send(src, dname, dst, sem, lat):
         rid, pid, _ = topo.addr(dst)
         m = topo.mask(core, dst)
-        op("pool", lambda: g.remote_dma(T[dname][:], src[0], T.sem[sem], T.sem["sent"], pid, rid, m), [], [src], 0.5, ext="send")
+        op("pool", lambda: g.remote_dma(T[dname][:], src[0], T.sem[sem], T.sem["sent"], pid, rid, m), [], [src], (0.5, 0, 0, 0, 0), ext="send")
         ops[-1]["n"] = len(topo.engines(core, dst))
         return (len(ops) - 1, lat)
 
     def arrive(name, sem, src, sent):
-        op(None, None, [A(name)], [], 0.0, dma=sem, ext="arr", lat=sent[1], after=(sent[0],))
+        op(None, None, [A(name)], [], (0.0, 0, 0, 0, 0), dma=sem, ext="arr", lat=sent[1], after=(sent[0],))
         ops[-1]["n"] = len(topo.engines(src, core))
 
-    def f2w(o, wide, src, first=True, last=True, p=None):
+    def f2w(o, wide, src, first=True, p=None):
         for p0 in range(16):
-            mm(o, A(wide, 16 - p0, 144 - p0, p=p), A(src, p0, 512, 16, p=p), first and p0 == 0, last and p0 == 15)
+            mm(o, wide(16 - p0, 144 - p0), A(src[0], src[1] + p0, src[1] + 512, 16, key=src[2], p=p), first and p0 == 0)
+
+    def w2f(bank, sel, src, first=False, cols=128):
+        for p0 in range(16):
+            mm(A(bank, p0, 512, 16, p=slice(0, 8) if cols == 8 else None), A(sel, 128 * p0, 128 * p0 + 128, 128 // cols), src, first and p0 == 0)
 
     H = lambda name: (T[name][:], [], [])
-    C = lambda j: A("col", j, j + 1, key=j)
+    C = lambda j, p=None: A("col", j, j + 1, key=j, p=p)
+    PARTKEYS = ["p%d" % q for q in range(4)]
     S = lambda j: A("sm", 32 * j, 32 * j + 32, key=j)
-    SI = lambda j: A("smi", 32 * j, 32 * j + 32, key=["6_0", "6_1"] if j == 6 else j)
-    SUU = lambda j: A("smu", 32 * j, 32 * j + 32, key=["2_0", "2_1"] if j == 2 else j)
-    P5 = lambda nm, q: A(nm, 32 * q, 32 * q + 32, key=q)
+    SI = lambda j: A("smi", 32 * j, 32 * j + 32, key=j)
+    SB = lambda j: A("smb", 32 * j, 32 * j + 32, key=j)
+    SH = lambda j: A("smh", 32 * j, 32 * j + 32, key=j)
+    SUU = lambda j: A("smu", 32 * j, 32 * j + 32, key=j)
     TM = lambda j: A("tmpf", 8 * j, 8 * j + 8, key=j)
+    ID = lambda j: A("idm", 128 * j, 128 * j + 128, key=j)
+    IH = lambda j: A("idh", 128 * j, 128 * j + 128, key=j)
+    IF = lambda j: A("idf", 128 * j, 128 * j + 128, key=j)
+    WD = lambda j: (lambda a, b: A("wide", 144 * j + a, 144 * j + b, key=j))
+    CS = lambda j: A("cst", 32 * j, 32 * j + 32, key=j)
     RQ = lambda q: A("EQ", 1024 * q, 1024 * q + 1024, key="r%d" % q)
     eq, ne, ge, lt = ALU.is_equal, ALU.not_equal, ALU.is_ge, ALU.is_lt
-    add, sub, mul, mx, mn, band = ALU.add, ALU.subtract, ALU.mult, ALU.max, ALU.min, ALU.bitwise_and
-    PART, P16, G16, G16P, TWOF, LIM, PLO, PHI, B31N, B5N, B35, B2N, B36, T1, T2, T3, T4, T5, ACNT, MLO, MHI = range(21)
-    LANE, DUMR, DUMV, OWN2, OWN1, WF, BF_, THR, KN, MNV, CF, SENT, THR2, MAY, NT, NDC, CNT, SN = range(18)
-    fresh = [0]
-
-    def tmp():
-        fresh[0] += 1
-        return S(18 + fresh[0] % 22)
-
-    io = lambda n: A("IOTA", 0, n, key=0)
+    add, sub, mul, mx, mn, band, shr = ALU.add, ALU.subtract, ALU.mult, ALU.max, ALU.min, ALU.bitwise_and, ALU.arith_shift_right
+    PART, P16, G16, G16P, TWOF, LIM, PLO, PHI, B256, B1, BSG, B2, B254, B247, B2048, T1, T2, T3, ACNT, MLO, MHI, B256N, T4, DC, DB = range(25)
+    LANE, DUMR, BF_, THR, CAND, MNV, NT, NC, CG, LQ, NG, JN, JD = range(13)
+    ONE, NEG, TWO, K4, N8K, K256 = range(6)
+    ONESW, JW, JW2, ONESN = range(4)
+    CK, CW, LIFT, LIFTV, CZ, OWN, OWNH = 0, 1, 2, 3, 4, 5, 12
+    CE, CKEY = A("cst", 192, 256, key="e"), A("cst", 256, 384, key="k")
+    NTG, NTN, CL, SW = range(4)
+    KEYV, TGT, JUH = range(3)
+    io = lambda n: A("io", 0, n)
     r8 = slice(0, 8)
 
-    dma("sp", A("x0b"), H("x0"), "dx", 2.5)
-    dma("sp", A("sci", p=r8), H("v0"), "dv0", 2.5)
-    dma("sp", A("ei", 0, 512, key=[0, 1]), H("edge0"), "de")
-    dma("act", A("ei", 512, 1024, key=[2, 3]), H("ver0"), "dver")
+    dma("sp", A("x0r"), H("x0"), "dx", 2.5)
+    dma("act", A("sci", p=r8), H("v0"), "dv0", 2.5)
     for q in range(4):
-        dma("sp", RQ(q), (T["rec0"][:, 1024 * q:1024 * q + 1024], [], []), "dr%d" % q, 4.0 + q)
+        dma("sp", RQ(q), (T["rec0"][:, 1024 * q:1024 * q + 1024], [], []), "dr%d" % q, 3.5 + q)
+        if q == 0:
+            dma("act", A("ei", 0, 512, key=[0, 1]), H("edge0"), "de")
+            dma("act", A("ei", 512, 1024, key=[2, 3]), H("ver0"), "dver", 3.5)
     for q in range(4):
         dma("sp", A("EF", 1024 * q, 1024 * q + 1024, key=q), H("eff"), "deff", 10.0)
     iota(A("coli", 0, 1, key=0), [[0, 1]], 0, 1, flt=False)
-    iota(io(256), [[1, 256]], after=(len(ops) - 1,))
-    iota(A("MK"), [[0, 49], [1, 16]], after=(len(ops) - 1,))
-    iota(A("iob"), [[1, 128]], after=(len(ops) - 1,))
-    iota(S(LANE), [[16, 32]], after=(len(ops) - 1,))
-    iota(A("gk"), [[16, 8], [0, 16]], after=(len(ops) - 1,))
-    iota(TM(5), [[0, 8]], 4, after=(len(ops) - 1,))
-    iota(TM(6), [[0, 8]], 1, after=(len(ops) - 1,))
-    iota(A("wexp"), [[0, 512]], after=(len(ops) - 1,))
-    iota(A("ones"), [[0, 128]], 1, after=(len(ops) - 1,))
-    iota(S(OWN1), [[8192, 32]], 262144, after=(len(ops) - 1,))
-    iota(S(OWN2), [[32, 32]], 1016, after=(len(ops) - 1,))
-    iota(A("am"), [[0, 32], [16, 8]], after=(len(ops) - 1,))
-    iota(A("tmpf", 0, 16, key=[0, 1]), [[0, 2], [16, 4], [64, 2]], 15, after=(len(ops) - 1,))
-    iota(A("lw"), [[0, 4], [1, 64]], -48, after=(len(ops) - 1,))
-    iota(A("c36"), [[0, 512]], 36, after=(len(ops) - 1,))
-    iota(A("cv"), [[1, 32], [0, 32]], 32, after=(len(ops) - 1,))
-    for j, c in ((B31N, -31.0), (B5N, -5.0), (B35, -3.5), (B2N, -2.0), (B36, 36.0), (T4, 1.0), (T5, 0.5), (LIM, 196608.0)):
+    iota(io(256), [[1, 256]])
+    iota(A("iob"), [[1, 128]])
+    iota(A("MK"), [[0, 49], [1, 16]])
+    iota(CE, [[0, 64]], -15 * int(D1))
+    iota(S(LANE), [[16, 32]])
+    iota(A("gk"), [[16, 8], [0, 16]])
+    iota(CS(CW), [[0, 32]], -4096)
+    iota(TM(5), [[0, 8]], 4)
+    iota(TM(6), [[0, 8]], 1)
+    iota(A("R", 4096, 4608, key=8), [[0, 512]], 200)
+    iota(CS(CK), [[0, 32]], 256000)
+    iota(CS(LIFT), [[0, 16], [2560, 2]], 2048)
+    iota(A("tmpf", 0, 16, key=[0, 1]), [[0, 2], [16, 4], [64, 2]], 15)
+    iota(A("tmpf", 16, 24, key=2), [[0, 2], [16, 4]], 15)
+    iota(A("lw"), [[0, 4], [1, 64]], -48)
+    for ch in range(4):
+        iota(A("cv", 256 * ch, 256 * ch + 256, key=ch), [[16 << ch, 8], [0, 2], [1 << ch, 16]], 128 << ch)
+    iota(CS(LIFTV), [[0, 32]], 2048)
+    iota(CS(CZ), [[0, 32]], 20480)
+    iota(S(LQ), [[0, 4], [16, 8]], 128)
+    iota(A("c2112"), [[0, 512]], 2112)
+    iota(A("ENC"), [[-1, 8], [256, 512]], 8)
+
+    def seld(t, chain):
+        pat = [[-1001, 16], [-16, 8], [1000, 16]]
+        asel(A("seld"), A("wsel"), pat, ne, 0.0, -1000 * t, 1, chain)
+        if t:
+            asel(A("seld"), A("seld"), pat, ne, 0.0, 1000 * (16 - t), 1, chain)
+
+    if OPT["rclone"] != "act":
+        iota(A("cneg"), [[0, 512]], -int(FAR))
+
+    for j, c in ((B256, 256.0), (B256N, -256.0), (B1, 1.0), (BSG, 252.5), (B2, 2.0), (B254, 254.0), (B247, -247.0), (B2048, 2048.0), (LIM, 3 * D1)):
         ms(C(j), c)
     cp(C(PART), A("coli", 0, 1, key=0))
     ts(A("coli", 1, 2, key=1), A("coli", 0, 1, key=0), 15, band)
@@ -272,54 +329,71 @@ def rank_program(g, core, T, topo):
     ts(C(TWOF), C(P16), 2.0, mul, 1.0, add)
     ts(C(T1), C(PART), 16.0, mul, 16.0, add)
     ts(C(T3), C(G16), 24.0, add)
-    ts(C(MLO), C(P16), 8.0, lt)
+    ts(C(MLO), C(P16), 8.0, lt, -8388608.0, mul)
     ts(C(MHI), C(P16), 8.0, ge)
-    ts(A("jw"), io(144), C(G16P), eq, C(TWOF), mul)
-    act("k0", A("jw4"), A("jw"), AF.Copy, None, -2.0)
+    ts(ID(ONE), A("iob"), C(PART), eq)
+    for j, c in ((NEG, -1.0), (TWO, 2.0), (K4, 4096.0), (N8K, -8192.0), (K256, 256.0)):
+        act(ID(j), ID(ONE), AF.Copy, None, c)
+    for j, c in ((0, 1.0), (1, -512.0), (2, 131072.0)):
+        act(IF(j), ID(ONE), AF.Copy, None, c)
+    for j, c in ((0, 1.0), (1, 2.0 ** -14), (2, 256.0), (3, -16.0)):
+        ts(IH(j), ID(ONE), c, mul)
+    ts(WD(JW)(0, 144), io(144), C(G16P), eq, C(TWOF), mul)
+    act(WD(JW2)(0, 144), WD(JW)(0, 144), AF.Copy, None, -2.0)
     ts(A("w8"), io(144), C(T1), eq)
     ts(A("oneswf"), io(144), C(G16P), eq)
     ts(A("ow2"), io(144), C(T3), eq)
     tt(A("ow2"), A("ow2"), A("oneswf"), add)
-    ts(A("MK"), A("MK"), C(P16), eq)
+    act(WD(ONESW)(0, 144), A("oneswf"), AF.Copy, None, 2.0)
+    act(WD(ONESN)(0, 144), A("oneswf"), AF.Copy, None, -512.0)
+    ts(A("MK"), A("MK"), C(P16), ne, D1, mul)
+    ts(A("cst", 193, 256, 2, key="e"), A("cst", 193, 256, 2, key="e"), C(MLO), add)
+    ms(A("eD"), -16777216.0)
+    ts(A("eD", 1, 64, 2), A("eD", 1, 64, 2), C(MHI), mul)
+    ms(A("d0"), 0.0)
+    ts(C(DC), C(P16), 4096.0, add)
+    ts(C(DB), C(P16), 5120.0, add)
+    ts(A("x0b"), A("x0r"), -1.0, mul, 256.0, add)
     ts(A("v0h", p=r8), A("sci", p=r8), -2048.0, add)
-    f2w(A("B6", 0, 32), "w8", "v0h", p=r8)
+    f2w(A("B6", 0, 32), lambda a, b: A("w8", a, b, p=r8), ("v0h", 0, None), p=r8)
     ts(SI(0), A("B6", 0, 32), 2048.0, add)
-    cp(A("v0u", 32, 64, key=1), SI(0))
+    cp(A("v0u", 0, 32, key=1), SI(0))
     ts(SI(1), SI(0), 511, band)
-    cp(SUU(4), SI(1))
-    f2w(A("B5", 0, 32), "jw", "x0b")
-    cp(A("v0u", 0, 32, key=0), A("B5", 0, 32))
-    cp(A("SU", 0, 512, key=0), A("ei", 0, 512, key=[0, 1]))
-    for q in range(4):
-        act("rin%d" % q, A("R", 1024 * q, 1024 * q + 1024, key=q), RQ(q), AF.Relu, C(B36), -4.0)
-    cp(A("VL", 0, 512), A("ei", 512, 1024, key=[2, 3]))
-    act("k0", A("onesw"), A("oneswf"), AF.Copy)
-    act("k0", A("ones960"), A("oneswf"), AF.Copy, None, 960.0)
+    cp(SUU(3), SI(1))
+    f2w(A("B5", 0, 32), WD(JW), ("x0r", 0, None))
+    cp(A("v0u", 32, 64, key=0), A("B5", 0, 32))
+    ts(A("sci"), A("ei", 0, 512, key=[0, 1]), 9, shr)
+    ts(A("B7"), A("sci"), -131073.0, mul, 8.0, add)
+    ts(A("nv1"), A("ei", 0, 512, key=[0, 1]), 256.0, mul)
+    tt(A("SU", 0, 512, key=0), A("nv1"), A("B7"), add)
+    ts(A("VL", 0, 512), A("ei", 512, 1024, key=[2, 3]), 64.0, add)
+    for q in range(8):
+        gq = A("G", 512 * q, 512 * q + 512, key="r%d" % q)
+        rq = A("EQ", 512 * q, 512 * q + 512, key="r%d" % (q // 2))
+        ts(gq, rq, 5.0, ge, -247.0, mul)
+        mm(A("B%d" % (q % 4)), ID(NEG), rq, True)
+        mm(A("B%d" % (q % 4)), ID(ONE), gq)
+        act(A("R", 512 * q, 512 * q + 512, key=q), A("B%d" % (q % 4)), AF.Identity, C(B256))
     scan(TM(7), TM(5), TM(6), 0.25, mul, mul)
     for j, sh, a in ((PLO, 0.0, 8), (PHI, 8.0, 12)):
         ts(TM(a), io(8), sh, add, C(P16), eq)
         tt(TM(a + 1), TM(a), TM(7), mul)
         red(C(j), TM(a + 1))
-    ts(A("wexp", 128, 256), A("gk", 0, 128), C(G16), eq, C(PLO), mul)
-    ts(A("wexp", 256, 384), A("gk", 0, 128), C(G16), eq, C(PHI), mul)
+    ts(A("wexp", 0, 128), A("gk", 0, 128), C(G16), eq, C(PLO), mul)
+    ts(A("wexp", 128, 256), A("gk", 0, 128), C(G16), eq, C(PHI), mul)
     ts(A("blk"), A("gk", 0, 128), C(G16), eq)
     cp(A("wg"), A("blk", 0, 128, 16))
-    ts(A("we", 0, 8), A("wg"), 960.0, mul)
-    ts(A("we", 8, 24), A("wexp", 128, 384, 16), -1.0, mul)
+    ts(A("we", 0, 8), A("wg"), -256.0, mul)
+    ts(A("we", 8, 24), A("wexp", 0, 256, 16), -1.0, mul)
     ts(S(LANE), S(LANE), C(P16), add)
     ts(S(DUMR), S(LANE), 4096.0, add)
-    ts(S(DUMV), S(LANE), 512.0, add)
-    ts(A("dum2", 0, 32), S(LANE), 2048.0, add)
-    ts(A("dum2", 32, 64), S(LANE), 512.0, add)
-    act("k2", P5("base5", 2), S(DUMR), AF.Copy)
-    act("k2", P5("base5", 3), S(DUMR), AF.Copy)
-    act("k2", P5("base5", 4), S(DUMV), AF.Copy)
-    ts(A("idb"), A("iob"), C(PART), eq)
-    cp(A("idh"), A("idb"))
-    mm(A("B7", 0, 128), A("idb"), A("idb"), True, True)
-    act("k1", A("neg2"), A("idb"), AF.Copy, None, -2.0)
-    act("k1", A("idf"), A("idb"), AF.Copy)
-    act("k1", A("ids"), A("idb"), AF.Copy, None, 2.0 ** -16)
+    ts(A("dum3", 0, 32), S(LANE), 4608.0, add)
+    ts(A("dum3", 32, 64), S(LANE), 512.0, add)
+    ts(A("dum3", 64, 96), S(LANE), 4608.0, add)
+    for ch in range(4):
+        ts(A("cst", 32 * OWN + 8 * ch, 32 * OWN + 8 * ch + 8, key=OWN), A("sm", 32 * LQ + 8 * ch, 32 * LQ + 8 * ch + 8, key=LQ), C(P16), add, float(4 << ch), mul)
+    ts(CS(OWNH), CS(OWN), 0.5, mul)
+    mm(A("B7", 0, 128), ID(ONE), ID(ONE), True)
     c2, c3 = A("coli", 8, 16, key=2), A("coli", 16, 24, key=3)
     ts(c2, io(8), -1.0, mul, C(P16), add)
     ts(c2, c2, 15.0, add)
@@ -329,360 +403,392 @@ def rank_program(g, core, T, topo):
     ts(c3, c3, 15, band)
     ts(TM(11), c3, C(P16), mx, C(G16), add)
     for d in range(8):
-        ts(A("rc", 128 * (d % 4), 128 * (d % 4) + 128, key=d % 4), A("iob"), A("tmpf", 80 + d, 81 + d, key=10), eq)
-        tt(A("dif", 128 * d, 128 * d + 128, key=d), A("rc", 128 * (d % 4), 128 * (d % 4) + 128, key=d % 4), A("B7", 0, 128), sub)
+        ts(A("rc", 128 * (d % 4), 128 * (d % 4) + 128, key="p%d" % (d % 4)), A("iob"), A("tmpf", 80 + d, 81 + d, key=10), eq)
+        tt(A("dif", 128 * d, 128 * d + 128, key=d), A("rc", 128 * (d % 4), 128 * (d % 4) + 128, key="p%d" % (d % 4)), A("B7", 0, 128), sub)
         ts(A("bk", 128 * d, 128 * d + 128, key=d), A("iob"), A("tmpf", 88 + d, 89 + d, key=11), eq, 8192.0, mul)
-    act("k1", A("neg4"), A("idb"), AF.Copy, None, -4.0)
-    act("k0", A("onesn"), A("oneswf"), AF.Copy, None, -512.0)
+    ts(A("tmpf", 112, 128, key=[14, 15]), io(16), C(P16), eq)
+    for p0 in range(16):
+        ts(A("wselh", 128 * p0, 128 * p0 + 128, key=p0), A("blk"), A("tmpf", 112 + p0, 113 + p0, key=[14, 15]), mul)
+    ts(A("wsel"), A("wselh"), FAR, mul)
+    seld(0, True)
     ms(A("sc0"), -1.0 / 16)
     ms(A("sc0", 0, 128, 16), 1.0e6)
-    ts(A("am"), A("am"), C(G16), eq)
-    ts(C(T2), C(MHI), 128.0, mul)
-    ts(A("exu"), A("tmpf", 0, 16, key=[0, 1]), C(T2), add)
-    ts(A("lw"), A("lw"), C(P16), eq, 65536.0, mul)
-
-    def seld(t, after=()):
-        pat = [[-1, 16], [0, 8], [1, 16]]
-        iota(A("seld"), [[0, 2048]], int(BIGW), after=after)
-        asel(A("seld"), A("seld"), pat, ne, -BIGW, -t, 0)
-        if t:
-            asel(A("seld"), A("seld"), pat, ne, -BIGW, 16 - t, 0)
-        asel(A("seld"), A("seld"), [[-1, 16], [-16, 8], [0, 16]], eq, 0.0, 0, 1)
-
-    seld(0)
-    iota(A("IOTA", 256, 4128, key=1), [[1, 3872]], 256)
+    for ch in range(4):
+        iota(A("scan", 144 * ch + 128, 144 * ch + 144, key=ch), [[0, 16]], 0, chain=False)
+    ts(A("lw"), A("lw"), C(P16), eq, D1, mul)
+    ts(A("coli", 24, 25, key=6), A("coli", 0, 1, key=0), 7, band)
+    ts(A("coli", 25, 26, key=7), A("coli", 0, 1, key=0), 4, shr)
+    tt(C(T4), A("coli", 24, 25, key=6), A("coli", 25, 26, key=7), eq)
+    ts(C(T2), C(MHI), 64.0, mul, -128.0, add)
+    ts(A("tmpf", 24, 28, key=3), A("tmpf", 16, 20, key=2), C(T2), add, C(T4), mul)
+    ts(A("exu", 0, 4), A("tmpf", 24, 28, key=3), 128.0, add)
+    ts(C(T2), C(MHI), 144.0, mul, -128.0, add)
+    ts(TM(3), TM(0), C(T2), add, C(T4), mul)
+    ts(A("exu", 4, 12), TM(3), 128.0, add)
     for q in range(8):
-        dma("sp", A("TV", 512 * q, 512 * q + 512, key=q), A("SU", 0, 512, key=0), "dtv", 8.0)
+        if OPT["tvinit"] == "act":
+            act(A("TV", 512 * q, 512 * q + 512, key=q), A("x0r"), AF.Copy)
+        else:
+            dma("sp", A("TV", 512 * q, 512 * q + 512, key=q), A("VL", 0, 512), "dtv", 8.0)
     for q in (0, 1, 2, 3, 4, 5, 6, 7, 9):
-        dma("sp", A("TT", 512 * q, 512 * q + 512, key="c" if q < 9 else "b"), A("SU", 0, 512, key=0), "dtt", 12.0)
+        dma("sp", A("TT", 512 * q, 512 * q + 512, key="c" if q < 9 else "b"), A("VL", 0, 512), "dtt", 12.0)
     for q in range(1, 8):
         dma("sp", A("SU", 512 * q, 512 * q + 512, key=q), A("SU", 0, 512, key=0), "dsu", 16.0)
 
     Rw, SUw = A("R", 0, 4096), A("SU", 0, 4096)
+    E = A("ev", 1, 64, 2)
 
     def edge(t):
-        act("mask%d" % t, A("mask%d" % (t % 2)), IN(A("MK"), A("v%du" % t, 0, 32, key=0 if t == 0 else None)), AF.Copy)
+        mask = A("mask%d" % (t % 2))
+        act(mask, IN(A("MK"), A("v%du" % t, 32, 64, key=0 if t == 0 else None)), AF.Copy)
         if t == 0:
-            tt(A("sel"), IN(A("SU", 0, 512, key=0), SUU(4)), A("mask0"), mul)
+            tt(A("sel"), IN(A("SU", 0, 512, key=0), SUU(3)), mask, mx)
         else:
-            tt(A("sel"), IN(SUw, A("v%du" % t, 32, 64)), A("mask%d" % (t % 2)), mul)
+            tt(A("sel"), IN(SUw, A("v%du" % t, 0, 32)), mask, mx)
+        mm(A("B5", 32, 96), ID(ONE), CE, True)
         for p0 in range(8):
-            mm(A("B5", 32, 96), A("ow2", 16 - p0, 144 - p0), A("sel", p0, 512, 8), p0 == 0, p0 == 7)
-        a, b = tmp(), tmp()
-        ts(a, A("B5", 32, 96, 2), C(MLO), mul)
-        ts(b, A("B5", 33, 96, 2), C(MHI), mul)
-        tt(SI(2), a, b, add)
-        ts(SI(3), SI(2), 511, band)
-        ts(SI(4), SI(2), 4095, band)
-        cp(SUU(0), SI(3))
-        cp(SUU(1), SI(4))
-        act("gw%d" % t, A("gw"), IN(Rw, SUU(1)), AF.Square, C(B31N))
+            mm(A("B5", 32, 96), A("ow2", 16 - p0, 144 - p0), A("sel", p0, 512, 8))
+        scan(A("ev"), A("eD"), A("B5", 32, 96), 0.0, add, mx)
+        ts(SUU(0), E, 1.0 / 256, mul, 0.25, add)
         for a, b in ((3, 4), (0, 3)):
-            cp(A("veru", 128 * a, 128 * b, key=list(range(a, b))), IN(A("VL", 0, 512), A("smu", 8 * a, 8 * b, key=0)))
+            ver, keys = IN(A("VL", 0, 512), A("smu", 8 * a, 8 * b, key=0)), list(range(a, b))
+            if OPT["vl"] == "act":
+                act(A("verf", 128 * a, 128 * b, key=keys), ver, AF.Copy)
+                ver = A("verf", 128 * a, 128 * b, key=keys)
+            ts(A("veru", 128 * a, 128 * b, key=keys), ver, -63.75, add)
+        ts(SI(2), E, 1.0 / 256, mul, 10240.0, add)
+        ts(S(BF_), SI(2), -10240.0, add)
+        mm(A("B5", 96, 128), ID(ONE), CS(CW), True)
+        mm(A("B5", 96, 128), IF(1), E)
+        mm(A("B5", 96, 128), IF(2), S(BF_))
+        mm(A("B5", 96, 128), IF(0), S(BF_))
+        ts(SUU(1), A("B5", 96, 128), 8192.25, add)
 
     def main(t):
-        x, vu = "x%db" % t, A("v%du" % t, 32, 64)
+        x = "x%db" % t
         last = t == NSTEP - 1
-        act("xc%d" % t, A("B4"), A(x), AF.Square, C(B5N), 4.0)
-        parts = []
-        for ch in (3, 2, 1, 0):
-            parts += [(ch, 0, 64), (ch, 64, 128)] if ch in OPT["halves"] else [(ch, 0, 128)]
-        gkey = lambda ch, a: "%d_%d" % (ch, a)
-        for ch, a, b in parts:
-            act("G%d" % t, A("G", 2048 * ch + 16 * a, 2048 * ch + 16 * b, key=gkey(ch, a)),
-                IN(Rw, A("veru", 128 * ch + a, 128 * ch + b, key=ch)), AF.Square, C(B31N))
-        if OPT["nm"]:
-            act("nm%d" % t, A("nmask"), A("mask%d" % (t % 2)), AF.Identity, C(T4), -1.0)
-        else:
-            ts(A("nmask"), A("mask%d" % (t % 2)), -1.0, mul, 1.0, add)
-        if OPT["x32"]:
-            act("x32%d" % t, A("x32"), A(x), AF.Identity, C(B36), -4.0)
-        else:
-            ts(A("x32"), A(x), -4.0, mul, 36.0, add)
-        for ch in range(4):
-            mm(A("B%d" % ch, 0, 256), A("wexp", 0, 128), A("c36", 0, 256), True, False)
-        cp(A("verf"), A("veru"))
-        for ch in range(4):
-            mm(A("B%d" % ch, 128, 256), A("verf", 128 * ch, 128 * ch + 128), A("ids"), False, False)
-        ts(A("keyv"), vu, -2048.0, add)
-        for d in range(8):
-            mm(A("B6", 32 * d, 32 * d + 32), A("dif", 128 * d, 128 * d + 128, key=d), A("keyv"), True, True)
-        ts(A("eqv"), A("B6", 0, 256), 0.0, eq)
-        for d in range(8):
-            mm(A("B5", 96, 128), A("bk", 128 * d, 128 * d + 128, key=d), A("eqv", 32 * d, 32 * d + 32), d == 0, False)
-        mm(A("B5", 96, 128), A("idh"), A("keyv"), False, True)
-        tt(S(MNV), A("B5", 96, 128), A("dum2", 0, 32), mn)
-        ts(A("ofv", 0, 64, 2), S(MNV), 2048.0, add)
-        tt(S(MNV), S(MNV), S(OWN1), add)
-        for c in range(31, -1, -1):
-            act("V%d" % t, IN(A("TV"), A("ofv", 2 * c, 2 * c + 1)), A("cv", 32 * c, 32 * c + 16), AF.Silu)
-        act("tv%d" % t, A("tvf"), IN(A("TV", 0, 4096), vu), AF.Copy)
-        for ch in range(4):
-            mine = [q for q in parts if q[0] == ch]
-            old = ["r%d" % (2 * ch), "r%d" % (2 * ch + 1)] if ch < 2 and t in (0, NSTEP - 1) else []
-            for k in range(16):
-                base = 2048 * ch + 128 * k
-                for _, a, b in mine:
-                    tt(A("EQ", base + a, base + b, key=["%d_%d_%d" % (ch, k, a)] + ([old[k // 8]] if old and t == 0 and k % 8 == 0 else [])),
-                       A("G", 2048 * ch + 16 * a + k, 2048 * ch + 16 * b, 16, key=gkey(ch, a)), A("B4", 128 * ch + a, 128 * ch + b), eq)
-                    tag("E%d_%d_%d" % (t, ch, a))
-                mm(A("B%d" % ch, k, 128, 16), A("G", 2048 * ch + k, 2048 * ch + 2048, 16, key=[gkey(ch, q[1]) for q in mine]), A("wg"), False, False)
-            for k in range(16):
-                base = 2048 * ch + 128 * k
-                mm(A("B%d" % ch, k, 128, 16), A("EQ", base, base + 128, key=["%d_%d_%d" % (ch, k, q[1]) for q in mine]), A("we", 0, 8), False, k == 15)
-            sl = lambda nm: A(nm, 128 * ch, 128 * ch + 128, key=ch)
-            ts(sl("di"), A("B%d" % ch, 0, 128), -1.0 / 960, mul, 16.41, add)
-            tt(sl("keyl"), sl("di"), A("B%d" % ch, 128, 256), add)
-            scan(sl("scan"), A("sc0"), sl("keyl"), 0.0, add, mn)
-            tag("S%d_%d" % (t, ch))
-            mm(A("B%d" % ch, 128, 384), A("ones"), A("wexp", 128, 384), True, False)
-            for k in range(16):
-                base = 2048 * ch + 128 * k
-                mm(A("B%d" % ch, 128 + k, 384, 16), A("EQ", base, base + 128, key=["%d_%d_%d" % (ch, k, q[1]) for q in mine] + (old if last else [])),
-                   A("we", 8, 24), False, False)
-        tt(A("eqw"), A("gw"), A("B4"), eq)
-        tag("eqw%d" % t)
-        f2w(A("B7", 0, 32), "onesw", "gw", last=False)
-        f2w(A("B7", 0, 32), "ones960", "eqw", first=False)
-        a, b = tmp(), tmp()
-        ts(a, A("B7", 0, 32), 15360.0, ge)
-        ts(b, SI(2), 4096.0, lt)
-        tt(S(KN), a, b, mul)
-        ts(S(THR), S(KN), 1.0e9, mul, 65536.0, add)
-        tag("thr%d" % t)
+        first_v(t)
+        mm(A("B4"), ID(ONE), A(x), True)
         if not last:
-            mm(A("B7"), A("idb"), A(x), True, False)
-            mm(A("B7"), A("idb"), A("EF", t, 4096, 8), False, True)
-            act("hn%d" % t, A("hn"), A("B7"), AF.Sign, C(B35))
-            for p0 in range(16):
-                mm(A("B7", 256, 288), A("jw", 16 - p0, 144 - p0), A("EF", t + 8 * p0, 4096, 128), p0 == 0, False)
-            f2w(A("B7", 256, 288), "jw4", "hn", first=False)
-            ts(S(CNT), A("v%du" % t, 0, 32), -512.0, add)
-            tt(S(SN), A("B7", 256, 288), S(CNT), add)
-        chain = []
-        for ch, a, b in parts:
-            if a == 0:
-                chain += tags["S%d_%d" % (t, ch + OPT["lag"])] if ch + OPT["lag"] < 4 else []
-                for nm in OPT["between"][3 - ch].split():
-                    chain += tags.get(nm + str(t), [])
-            chain += tags["E%d_%d_%d" % (t, ch, a)]
-        for a, b in zip(chain, chain[1:]):
-            ops[b]["after"].append(a)
-        ts(S(NT), S(LANE), 8.0, mul, float(t), add)
-        tt(S(NDC), S(NT), S(DUMR), sub)
-        tt(P5("del5", 4), SI(3), S(DUMV), sub)
+            ts(SH(JUH), A("v%du" % t, 32, 64), -512.0, add)
+            next_j(t, "n", lambda a, s: A("EF", t + 8 * a, 4096, 8 * s), "B1", "hn", A("B0", 0, 32))
+            cp(S(JN), A("B0", 0, 32))
+        gkey = lambda ch, a, b: ["%d_%d" % (ch, m) for m in range(a // 16, b // 16)]
+        old = ["r%d" % q for q in range(8)] if t == 0 else []
+        for ch in (3, 2, 1, 0):
+            b = 128
+            for m, ln in enumerate(OPT["gp"][3 - ch]):
+                copy("dve" if ch == 2 and m < OPT["gdve"] else "act", A("G", 2048 * ch + 16 * (b - ln), 2048 * ch + 16 * b, key=gkey(ch, b - ln, b) + (old if ch < 2 else [])),
+                     IN(Rw, A("veru", 128 * ch + b - ln, 128 * ch + b, key=ch)))
+                b -= ln
+        for a, b in ((3, 4), (0, 3)):
+            ts(A("verh", 128 * a, 128 * b, key=list(range(a, b))), A("veru", 128 * a, 128 * b, key=list(range(a, b))), -2048.0, add, 1.0 / 16, mul)
+        if OPT["vl"] == "dve":
+            ts(A("verf"), A("veru"), 64.0, add)
+        copy(OPT["gw"], A("gw"), IN(A("R", 0, 4608), SUU(1)))
+        tt(A("eqw"), A("gw"), A("B4"), eq)
+        f2w(A("B7", 0, 32), WD(ONESW), ("gw", 0, None))
+        f2w(A("B7", 0, 32), WD(ONESN), ("eqw", 0, None), False)
+        ts(S(THR), A("B7", 0, 32), 256.0, ge, 8388608.0, mul)
+        tt(S(CAND), S(THR), A("B5", 96, 128), add)
+        ts(S(NT), S(LANE), 8.0, mul, 8192.0 + t, add)
+        for ch in (3, 2, 1, 0):
+            bank = "B%d" % ch
+            olde = ["r%d" % (2 * ch), "r%d" % (2 * ch + 1)] if ch < 2 and t in (0, NSTEP - 1) else []
+            ne_ = OPT["ep"][3 - ch]
+            pieces = [(128 * m // ne_, 128 * (m + 1) // ne_) for m in range(ne_)]
+            eqk = lambda k: A("EQ", 2048 * ch + 128 * k, 2048 * ch + 128 * k + 128, key=["%d_%d_%d" % (ch, k, a) for a, _ in pieces] + (olde if last else []))
+            for k in range(16):
+                base = 2048 * ch + 128 * k
+                for a, b in reversed(pieces):
+                    tt(A("EQ", base + a, base + b, key=["%d_%d_%d" % (ch, k, a)] + ([olde[k // 8]] if olde and t == 0 and k % 8 == 0 else [])),
+                       A("G", 2048 * ch + 16 * a + k, 2048 * ch + 16 * b, 16, key=gkey(ch, a, b)), A("B4", 128 * ch + a, 128 * ch + b), eq)
+                mm(A(bank, k, 128, 16), A("G", 2048 * ch + k, 2048 * ch + 2048, 16, key=gkey(ch, 0, 128)), A("wg"), k == 0)
+                if k == 1:
+                    mm(A(bank, 128, 256), A("verh", 128 * ch, 128 * ch + 128, key=ch), IH(1))
+                mm(A(bank, k, 128, 16), eqk(k), A("we", 0, 8))
+            sl = lambda nm: A(nm, 128 * ch, 128 * ch + 128, key=ch)
+            ts(sl("sci"), A(bank, 0, 128), 1.0 / 256, mul, 0.09, add)
+            tt(sl("keyl"), sl("sci"), A(bank, 128, 256), add)
+            scan(A("scan", 144 * ch, 144 * ch + 128, key=ch), A("sc0"), sl("keyl"), 0.0, add, mn)
+            for k in range(16):
+                mm(A(bank, 128 + k, 384, 16), eqk(k), A("we", 8, 24), k == 0)
+
+    def first_v(t):
+        ts(SH(KEYV), A("v%du" % t, 0, 32), -2048.0, add)
+        for d in range(8):
+            mm(A("B4", 32 * d, 32 * d + 32), A("dif", 128 * d, 128 * d + 128, key=d), SH(KEYV), True)
+        ts(A("eqv", 0, 256), A("B4", 0, 256), 0.0, eq)
+        mm(A("B4", 256, 288), IH(0), SH(KEYV), True)
+        mm(A("B4", 256, 288), ID(ONE), CS(LIFTV))
+        for d in range(8):
+            mm(A("B4", 256, 288), A("bk", 128 * d, 128 * d + 128, key=d), A("eqv", 32 * d, 32 * d + 32))
+        ts(A("ofv", 0, 64, 2), A("B4", 256, 288), C(DC), mn)
+        for c in range(31, -1, -1):
+            act(IN(A("TV"), A("ofv", 2 * c, 2 * c + 1)), A("cv", 32 * c, 32 * c + 16, key=c // 8), AF.Silu)
+        copy(OPT["tv"], A("tvf"), IN(A("TV", 0, 4096), A("v%du" % t, 0, 32)))
+
+    def patchers():
+        zv = A("B7", 96, 128)
+        mm(zv, IH(0), SH(KEYV), True)
+        mm(zv, ID(ONE), CS(LIFTV))
+        mm(zv, ID(K4), CS(OWNH))
+        f2w(zv, WD(ONESN), ("tvf", 0, None), False)
+        tt(S(MNV), zv, S(DUMR), mn)
+        cp(A("ofp"), S(MNV))
+
+    def next_j(t, name, ef, bank, sign, out):
+        mm(A(bank), ID(ONE), A("x%db" % t), True)
+        mm(A(bank), ID(NEG), ef(0, 1))
+        act(A(sign), A(bank), AF.Sign, C(BSG), -1.0)
+        mm(out, IH(0), SH(JUH), True)
+        for p0 in range(16):
+            mm(out, WD(JW)(16 - p0, 144 - p0), ef(p0, 16))
+        f2w(out, WD(JW2), (sign, 0, None), False)
 
     def decide(t):
-        x, of = "x%db" % t, "of%d" % t
-        last = t == NSTEP - 1
-        for pt in (1, 0):
-            c0 = 16 * pt
-            part = lambda ap, key: A(ap[0], ap[1] + c0, ap[1] + c0 + 16, key=key)
-            ex = A("expd", 128 * pt, 128 * pt + 128, key=pt)
-            tt(ex, IN(A("scan", 256 * pt, 256 * pt + 256, key=[2 * pt, 2 * pt + 1]), A("exu", 0, 8)), A("am", 0, 128), mul)
+        of, last = "of%d" % t, t == NSTEP - 1
+        for part in OPT["parts"]:
+            nch, lo = len(part), min(part)
+            c0, w = 8 * lo, 8 * nch
+            keys = ["p%d" % q for q in part]
+            W_ = lambda nm, j: A(nm, 32 * j + c0, 32 * j + c0 + w, key=["%d%s" % (j, k) for k in keys])
+            ex = lambda a, b: A("expd", 64 * lo + a, 64 * lo + b, key=list(part))
+            copy(OPT["expd"], ex(0, 64 * nch), IN(A("scan", 144 * lo, 144 * (lo + nch), key=list(part)), A("exu", 4 * nch - 4, 8 * nch - 4)))
+            kb = A("B5", 128, 128 + 2 * w)
+            mm(kb, ID(ONE), A("cst", 32 * CK, 32 * CK + 2 * w, key=CK), True)
             for gg in range(4):
-                mm(A("B5", 128, 160), A("lw", 112 - 16 * gg, 240 - 16 * gg), A("expd", 128 * pt + 32 * gg, 128 * pt + 32 * gg + 32, key=pt), gg == 0, gg == 3)
+                mm(kb, A("lw", 112 - 16 * gg, 240 - 16 * gg), ex(2 * w * gg, 2 * w * gg + 2 * w))
             for h in range(2):
                 rows = slice(64 * h, 64 * h + 64)
-                ts(A("smi", 160 + c0, 176 + c0, key="5_%d_%d" % (pt, h), p=rows), A("B5", 128 + 16 * h, 144 + 16 * h, p=rows), 61440.0, add)
-            kp, cc = part(("smi", 160), ["5_%d_0" % pt, "5_%d_1" % pt]), part(("smi", 192), "6_%d" % pt)
-            a, b, sent = part(("kt", 0), "a%d" % pt), part(("kt", 32), "b%d" % pt), part(("kt", 64), "s%d" % pt)
-            ts(cc, kp, 4095, band)
-            tt(a, kp, part(("sm", 32 * THR), THR), lt)
-            ts(b, cc, -2048.0, add)
-            ts(sent, a, 4096.0, mul, -2048.0, add)
-            cp(part(("smu", 64), "2_%d" % pt), cc)
-            tt(A("key2", 32 * pt, 32 * pt + 16, key="c%d" % pt), b, sent, mx)
-            tt(A("key2", 32 * pt + 16, 32 * pt + 32, key="b%d" % pt), part(("smi", 96), 3), sent, mx)
-            k2 = A("key2", 32 * pt, 32 * pt + 32, key=["c%d" % pt, "b%d" % pt])
+                tt(A("smi", 96 + c0, 96 + c0 + w, key=["3p%d%s" % (ch, "ab"[h]) for ch in part], p=rows), A("B5", 128 + w * h, 128 + w * h + w, p=rows),
+                   A("sm", 32 * CAND + c0, 32 * CAND + c0 + w, key=CAND, p=rows), mn)
+            kp = A("smi", 96 + c0, 96 + c0 + w, key=["3p%d%s" % (ch, h) for ch in part for h in "ab"])
+            cc, sw = W_("smi", 4), W_("smb", SW)
+            ts(cc, kp, 0x2FFF, band)
+            ts(sw, kp, D1, ge, 10240.0, mul)
+            tt(A("key2", 2 * c0, 2 * c0 + 2 * w, 2, key=["c" + k for k in keys]), cc, sw, sub)
+            tt(A("key2", 2 * c0 + 1, 2 * c0 + 2 * w, 2, key=["b" + k for k in keys]), A("smi", 64 + c0, 64 + c0 + w, key=2), sw, sub)
+            ts(W_("smu", 2), cc, -8192.0, add)
+            copy(OPT["rc"], A("rc", 16 * c0, 16 * (c0 + w), key=keys), IN(Rw, W_("smu", 2)))
+            k2 = A("key2", 2 * c0, 2 * c0 + 2 * w, key=[y + k for k in keys for y in "cb"])
             for d in range(8):
-                mm(A("B6", 32 * d, 32 * d + 32), A("dif", 128 * d, 128 * d + 128, key=d), k2, True, True)
-            ts(A("eqd", 256 * pt, 256 * pt + 256, key=pt), A("B6", 0, 256), 0.0, eq)
+                mm(A("B6", 2 * w * d, 2 * w * d + 2 * w), A("dif", 128 * d, 128 * d + 128, key=d), k2, True)
+            ts(A("eqd", 16 * c0, 16 * c0 + 16 * w, key=keys), A("B6", 0, 16 * w), 0.0, eq)
+            back = A("B7", 64, 64 + 2 * w)
+            mm(back, IH(0), k2, True)
+            mm(back, ID(ONE), A("cst", 32 * LIFT, 32 * LIFT + 2 * w, key=LIFT))
             for d in range(8):
-                mm(A("B5", 192, 224), A("bk", 128 * d, 128 * d + 128, key=d), A("eqd", 256 * pt + 32 * d, 256 * pt + 32 * d + 32, key=pt), d == 0, False)
-            mm(A("B5", 192, 224), A("idh"), k2, False, True)
-            for h, lift in ((0, 2048.0), (1, 4608.0)):
-                m2 = part(("mn2", 32 * h), "%d_%d" % (h, pt))
-                tt(m2, A("B5", 192 + 16 * h, 208 + 16 * h), part(("dum2", 32 * h), None), mn)
-                ts(A("ofcb", 2 * c0 + h, 2 * c0 + 32, 2, key="%d_%d" % (h, pt)), m2, lift, add)
-            for c in range(c0 + 15, c0 - 1, -1):
-                act("CB%d" % t, IN(A("TT"), A("ofcb", 2 * c, 2 * c + 2, key=["0_%d" % pt, "1_%d" % pt])), A("cv", 32 * c, 32 * c + 32), AF.Silu)
-        K = A("smi", 160, 192, key=["5_0_0", "5_0_1", "5_1_0", "5_1_1"])
-        act("rc%d" % t, A("rc"), IN(Rw, SUU(2)), AF.Square, C(B31N))
-        ts(A("ntg"), K, C(LIM), ge)
-        act("tc%d" % t, A("tcf"), IN(A("TT", 0, 4096), SUU(2)), AF.Copy)
-        if OPT["tbd"]:
-            cp(A("tbf"), IN(A("TT", 4608, 5120), SUU(0)))
-        else:
-            act("tc%d" % t, A("tbf"), IN(A("TT", 4608, 5120), SUU(0)), AF.Copy)
-        tt(A("eqc"), A("rc"), A("B4"), eq)
-        mm(A("B6"), A("idb"), A("c36"), True, False)
-        mm(A("B6"), A("neg4"), A(x), False, True)
-        tt(A("val"), A("eqc"), A("B6"), mul)
-        for ch in range(4):
-            mm(A("B%d" % ch, 128, 384), A("eqc", 128 * ch, 128 * ch + 128), A("wexp", 128, 384), False, True)
-        mm(A("B7"), A("wexp", 0, 128), A("gw"), True, False)
-        for p0 in range(16):
-            mm(A("B7", p0, 512, 16), A("seld", 128 * p0, 128 * p0 + 128), A("ntg"), False, False)
-        a, b, c, d, e = tmp(), tmp(), tmp(), tmp(), tmp()
-        tt(a, SI(2), SI(6), sub)
-        tt(a, a, S(KN), mul)
-        tt(P5("base5", 1), a, SI(6), add)
-        tt(b, S(NT), SI(6), sub)
-        tt(P5("del5", 1), b, A("ntg"), mul)
-        tt(b, P5("del5", 1), SI(6), add)
-        cp(SUU(6), b)
-        ts(c, A("mn2", 32, 64), 4.0, mul)
-        tt(c, c, A("mn2", 0, 32), mx)
-        ts(c, c, 2048.0, ge, 1.0e6, mul)
-        tt(S(THR2), c, S(OWN2), add)
-        ts(d, K, C(LIM), lt)
-        tt(e, SI(6), S(DUMR), sub)
-        tt(P5("del5", 2), e, d, mul)
-        tt(P5("del5", 3), S(NDC), A("ntg"), mul)
+                mm(back, A("bk", 128 * d, 128 * d + 128, key=d), A("eqd", 16 * c0 + 2 * w * d, 16 * c0 + 2 * w * d + 2 * w, key=keys))
+            for y, dum in ((0, DC), (1, DB)):
+                ts(A("ofcb", 2 * c0 + y, 2 * c0 + 2 * w, 2, key=["cb"[y] + k for k in keys]), A("B7", 64 + y, 64 + 2 * w, 2), C(dum), mn)
+            for c in range(c0 + w - 1, c0 - 1, -1):
+                act(IN(A("TT"), A("ofcb", 2 * c, 2 * c + 2, key=[y + k for k in keys for y in "cb"])), A("cv", 32 * c, 32 * c + 32, key=c // 8), AF.Silu)
+            if not last:
+                copy(OPT["yu"], A("yu", 16 * c0, 16 * (c0 + w), key=keys), IN(A("EF"), W_("smu", 2)))
+        allp = lambda j: ["%d%s" % (j, k) for k in PARTKEYS]
+        K = A("smi", 96, 128, key=["3p%d%s" % (ch, h) for ch in range(4) for h in "ab"])
+        CC, CU, SWA = A("smi", 128, 160, key=allp(4)), A("smu", 64, 96, key=allp(2)), A("smb", 32 * SW, 32 * SW + 32, key=allp(SW))
+        cf, dl, may = A("d1", 1, 64, 2, key=1), A("d0", 1, 64, 2, key=1), A("d1", 0, 64, 2, key=0)
         if not last:
-            cp(SUU(5), P5("base5", 1))
-            act("yu%d" % t, A("yu"), IN(A("EF"), SUU(5)), AF.Copy)
-            mm(A("B6"), A("idb"), A(x), True, False)
-            mm(A("B6"), A("idb"), A("yu"), False, True)
-            act("hu%d" % t, A("hu"), A("B6"), AF.Sign, C(B35))
-            f2w(A("B6", 0, 32), "jw", "yu", last=False)
-            f2w(A("B6", 0, 32), "jw4", "hu", first=False)
-            tt(P5("base5", 0), A("B6", 0, 32), S(CNT), add)
-            a = tmp()
-            tt(a, S(SN), P5("base5", 0), sub)
-            tt(P5("del5", 0), a, A("ntg"), mul)
-        if OPT["sca"]:
-            act("sc%d" % t, A("scf"), IN(SUw, SUU(2)), AF.Copy)
-            cp(A("sci"), A("scf"))
+            ju = A("d1", 65, 128, 2, key=3)
+            next_j(t, "u", lambda a, s: A("yu", a, 512, s), "B7", "hu", A("B7", 0, 32))
+            cp(ju, A("B7", 0, 32))
+            tt(S(JD), S(JN), ju, sub)
+        patchers()
+        act(A("tcb", 0, 512, key=0), IN(A("TT", 0, 4096), CU), AF.Copy)
+        copy(OPT["tb"], A("tcb", 512, 1024, key=1), IN(A("TT", 4608, 5120), SUU(0)))
+        ts(SB(NTG), K, C(LIM), ge)
+        ts(SB(NTN), K, C(LIM), ge, -8192.0, mul)
+        ts(cf, CC, -8192.0, add)
+        tt(S(NC), S(NT), CC, sub)
+        tt(dl, S(NC), SB(NTG), mul)
+        if not last:
+            tt(A("d0", 65, 128, 2, key=3), S(JD), SB(NTG), mul)
+        tt(SH(TGT), A("key2", 0, 64, 2, key=["c" + k for k in PARTKEYS]), dl, add)
+        tt(S(CG), cf, SB(NTN), sub)
+        mm(A("B4"), ID(ONE), A("x%db" % t), True)
+        w2f("B4", "wsel", SB(NTG))
+        tt(A("eqc"), A("rc"), A("B4"), eq)
+        if OPT["val"] == "act":
+            mm(A("B4"), ID(ONE), A("x%db" % t), True)
+            mm(A("B4"), ID(K256), A("eqc"))
+            act(A("val"), A("B4"), AF.Relu, C(B256N))
         else:
-            cp(A("sci"), IN(SUw, SUU(2)))
-        ts(A("sci"), A("sci"), 511, band)
-        ts(A("scf"), A("sci"), 4096.0, add)
+            tt(A("val"), A("eqc"), A("B4"), mul)
+        for ch in range(4):
+            mm(A("B%d" % ch, 128, 384), A("eqc", 128 * ch, 128 * ch + 128), A("wexp"))
+        ts(A("sch"), IN(SUw, CU), 1.0 / 256, mul, -2048.0, add)
         for ch in range(4):
             ek = A("ei", 256 * ch, 256 * ch + 256, key=ch)
-            cp(ek, A("B%d" % ch, 128, 384))
+            ts(ek, A("B%d" % ch, 128, 384), 21845.0, add)
             ts(ek, ek, 0xAAAA, band)
             tt(A("z", 128 * ch, 128 * ch + 128, key=ch), A("ei", 256 * ch, 256 * ch + 128, key=ch), A("ei", 256 * ch + 128, 256 * ch + 256, key=ch), add)
-            mm(A("B7", 128 * ch, 128 * ch + 128), A("z", 128 * ch, 128 * ch + 128, key=ch), A("idb"), False, ch == 3)
-        tt(A("dv"), IN(A("IOTA"), SUU(6)), A("verf"), sub)
-        if OPT["ma"]:
-            act("ma%d" % t, A("B7"), A("B7"), AF.Sign, C(T5), -1.0)
-            act("ma%d" % t, A("B7"), A("B7"), AF.Relu)
+
+        def kept(bank, flag, ident, first):
+            w2f(bank, "seld", flag, first)
+            for ch in range(4):
+                mm(A(bank, 128 * ch, 128 * ch + 128), A("z", 128 * ch, 128 * ch + 128, key=ch), ident)
+
+        if OPT["vw"] == "act":
+            for bank, flag, ident in (("B6", SB(NTG), ID(K4)), ("B3", SB(NTN), ID(N8K))):
+                mm(A(bank), ID(ONE), A("c2112"), True)
+                w2f(bank, "wselh", SH(TGT))
+                kept(bank, flag, ident, False)
+            tt(A("nv1"), A("verf"), A("B6"), mn)
+            tt(A("nv2"), A("nv1"), A("B3"), mx)
         else:
-            ts(A("B7"), A("B7"), 0.5, lt)
-        tt(A("dm"), A("dv"), A("B7"), mul)
-        f2w(A("B5", 256, 288), "onesw", "tcf", last=False)
-        f2w(A("B5", 256, 288), "onesw", "tbf", first=False)
-        tt(S(MAY), A("B5", 256, 288), S(THR2), ge)
-        for q in range(1 if last else 0, 5):
-            tt(P5("prod5", q), P5("del5", q), S(MAY), mul)
-        for a, b in OPT["ofs"]:
-            ks = list(range(a, b))
-            tt(A("sum5", 32 * a, 32 * b, key=ks), A("prod5", 32 * a, 32 * b, key=ks), A("base5", 32 * a, 32 * b, key=ks), add)
-            cp(A(of, 32 * a, 32 * b, key=ks), A("sum5", 32 * a, 32 * b, key=ks))
-            tag("of%d" % t)
-        f2w(A("B5", 288, 320), "onesn", "tvf")
-        a = tmp()
-        tt(a, A("B5", 288, 320), S(MNV), add)
-        tt(a, a, A("dum2", 0, 32), mn)
-        ts(SUU(3), a, 2048.0, add)
+            kept("B6", SB(NTG), ID(K4), True)
+            act(A("eat"), A("B6"), AF.Relu, C(B1), -1.0)
+            mm(A("B3"), IH(3), A("verh"), True)
+            w2f("B3", "wselh", SH(TGT))
+            tt(A("nv2"), A("eat"), A("B3"), mul)
+        zn = A("B5", 256, 288)
+        mm(zn, ID(K4), CS(CZ), True)
+        mm(zn, ID(N8K), SWA)
+        mm(zn, ID(K4), CS(OWN))
+        f2w(zn, WD(ONESN), ("tcb", 0, 0), False)
+        f2w(zn, WD(ONESN), ("tcb", 512, 1), False)
+        ts(may, zn, 4096.0, lt)
+        if last:
+            scan(A("vs", 0, 64), A("d0", 0, 64, key=[0, 1]), A("d1", 0, 64, key=[0, 1]), 0.0, mul, add)
+            cp(A(of, 32, 64), A("vs", 1, 64, 2))
+            cp(A(of, 0, 32), A("vs", 1, 64, 2))
+        else:
+            ts(A("d1", 64, 128, 2, key=2), zn, 4096.0, lt)
+            scan(A("vs"), A("d0"), A("d1"), 0.0, mul, add)
+            cp(A(of, 0, 64), A("vs", 1, 128, 2))
+        tt(SB(CL), may, SB(NTG), mul)
+        tt(A("a3", 0, 32, key=0), zn, S(CG), add)
+        tt(A("a3", 32, 64, key=1), zn, S(BF_), add)
+        w = 64
+        if OPT["rclone"] == "act":
+            tt(S(NG), S(NT), SB(NTN), add)
+            tt(A("a3", 64, 96, key=2), zn, S(NG), add)
+            w = 96
+        tt(A("a3", 0, w), A("a3", 0, w), A("dum3", 0, w), mn)
+        cp(A("og", 0, w), A("a3", 0, w))
 
     def writes(t):
-        x, vu, of = "x%db" % t, A("v%du" % t, 32, 64), "of%d" % t
+        x, of = "x%db" % t, "of%d" % t
         last = t == NSTEP - 1
         hop = HOP if not last else -HOP * t
         dst, src = T.cores[(rank + hop) % n_r], T.cores[(rank - hop) % n_r]
-        O = lambda q: P5(of, q)
-        sv = send(A(of, 0, 64, key=[0, 1]), "v%du" % (t + 1), dst, "av%d" % (t + 1), 2.5)
-        act("ef%d" % t, A("efg"), IN(A("EF"), O(1)), AF.Copy)
-        for bank in ("B4", "B6"):
-            mm(A(bank), A("idb"), A(x), True, False)
-        mm(A("B4"), A("idb"), A("efg"), False, True)
-        mm(A("B6"), A("idb"), A("efg"), False, False)
-        act("sg%d" % t, A("sg"), A("B4"), AF.Sign, C(B35))
-        mm(A("B6"), A("neg2"), A("sg"), False, True)
-        act("xo%d" % t, A("xo%d" % t), A("B6"), AF.Identity, C(B2N))
-        sx = send(A("xo%d" % t), "x%db" % (t + 1), dst, "ax%d" % (t + 1), 3.2)
-        act("rg%d" % t, IN(A("R"), O(2)), A("val"), AF.Silu)
-        act("rn%d" % t, IN(A("R"), O(3)), A("x32"), AF.Silu)
-        if last and OPT["snd"]:
-            cp(IN(A("SU"), O(3)), A("scf"))
+        vn = A(of, 0, 32)
+        sv = send(A(of), "v%du" % (t + 1), dst, "av%d" % (t + 1), 1.8)
+        act(A("efg"), IN(A("EF"), vn), AF.Copy)
+        mm(A("B7"), ID(ONE), A(x), True)
+        mm(A("B7"), ID(NEG), A("efg"))
+        act(A("sg"), A("B7"), AF.Sign, C(BSG), -1.0)
+        mm(A("B6"), ID(ONE), A(x), True)
+        mm(A("B6"), ID(NEG), A("efg"))
+        mm(A("B6"), ID(TWO), A("sg"))
+        if last:
+            act(A("xo%d" % t), A("B6"), AF.Identity, C(B254), -1.0)
         else:
-            act("sn%d" % t, IN(A("SU"), O(3)), A("scf"), AF.Silu)
-        tt(A("vm"), IN(A("IOTA"), O(1)), A("mask%d" % (t % 2)), mul)
-        tt(A("pg"), IN(SUw, vu), A("nmask"), mul)
-        ops[-1]["after"] += tags["of%d" % t]
-        tt(IN(A("SU"), SUU(3)), A("pg"), A("vm"), add)
-        tt(IN(A("VL"), O(4)), A("verf"), A("dm"), add)
+            act(A("xo%d" % t), A("B6"), AF.Identity, C(B2))
+        sx = send(A("xo%d" % t), "x%db" % (t + 1), dst, "ax%d" % (t + 1), 2.3)
+        su_t = A("SU", t, 4096, 8)
+        mm(A("B1"), IH(2), A("sch"), True)
+        w2f("B0", "wsel", SB(CL), True)
+        tt(su_t, su_t, A("B0"), sub)
+        w2f("B1", "wsel", SB(CL))
+        tt(su_t, su_t, A("B1"), mx)
+        tt(A("vm"), IN(A("ENC"), vn), A("mask%d" % (t % 2)), sub)
+        tt(A("pg"), IN(SUw, A("v%du" % t, 0, 32)), A("mask%d" % (t % 2)), mn)
+        tt(IN(A("SU"), A("ofp")), A("pg"), A("vm"), mx)
+        act(IN(A("R"), A("og", 0, 32)), A("val"), AF.Silu)
+        if OPT["vw"] == "act":
+            act(IN(A("VL"), A("og", 32, 64)), A("nv2"), AF.Silu)
+        else:
+            tt(IN(A("VL"), A("og", 32, 64)), A("verf"), A("nv2"), add)
+        if OPT["rclone"] == "act":
+            act(A("keyl"), A(x), AF.Copy)
+            act(IN(A("R"), A("og", 64, 96)), A("keyl"), AF.Silu)
+        else:
+            r_t = A("R", t, 4096, 8)
+            mm(A("B2"), ID(ONE), A(x), True)
+            mm(A("B2"), ID(ONE), A("cneg"))
+            w2f("B2", "wsel", SB(CL))
+            tt(r_t, r_t, A("B0"), sub)
+            tt(r_t, r_t, A("B2"), mx)
         arrive("v%du" % (t + 1), "av%d" % (t + 1), src, sv)
         arrive("x%db" % (t + 1), "ax%d" % (t + 1), src, sx)
         if not last:
-            seld(t + 1, (sx[0],))
-            tt(A("cl"), S(MAY), A("ntg"), mul)
-            mm(A("B6", 0, 32), A("blk"), A("cl"), True, True)
-            red(C(ACNT), A("B6", 0, 32))
+            seld(t + 1, False)
+            for o in ops[-2:]:
+                o["after"].append(sx[0])
+            mm(A("B5", 320, 352), A("blk"), SB(CL), True)
+            red(C(ACNT), A("B5", 320, 352))
             cp(A("coli", 2, 3, key=4), C(ACNT))
             ts(A("coli", 3, 4, key=5), A("coli", 2, 3, key=4), 1, band)
-            ts(C(LIM), A("coli", 3, 4, key=5), 65536.0, mul, 196608.0, add)
+            ts(C(LIM), A("coli", 3, 4, key=5), D1, mul, 3 * D1, add)
 
     for t in range(NSTEP):
+        step[0] = t
         edge(t)
         main(t)
         decide(t)
         writes(t)
-    for ch in range(32):
-        mm(A("B0", ch, 256, 32), A("SU", 128 * ch, 128 * ch + 128), A("oneswf", 16, 144, 16), True, True)
-    cp(A("keyl", 0, 256), A("B0", 0, 256))
-    for h in range(2):
-        mm(A("B1", 128 * h, 128 * h + 128), A("keyl", 128 * h, 128 * h + 128), A("idf"), True, True)
-    cp(A("di", 0, 256), A("B1", 0, 256))
-    cp(A("scan", 0, 256), A("di", 0, 256))
-    for q in range(4):
-        if q < OPT["nact"]:
-            act("rout", RQ(q), A("R", 1024 * q, 1024 * q + 1024), AF.Copy)
-        else:
-            cp(RQ(q), A("R", 1024 * q, 1024 * q + 1024))
-        ts(RQ(q), RQ(q), -0.25, mul, 9.0, add)
-    act("yv", A("sel"), IN(A("IOTA"), A("v4u", 32, 64)), AF.Copy)
-    dma("act", H("yv"), A("sel", p=slice(0, 128, 16)), "out")
-    dma("sp", H("yl"), A("VL", 0, 512), "out")
-    for q in (2, 0, 3, 1):
-        dma("sp", (T["yr"][:, 1024 * q:1024 * q + 1024], [], []), RQ(q), "out")
-    dma("act", H("yx"), A("x4b"), "out")
-    for h in range(2):
-        dma("sp", (T["ys"][4 * h:4 * h + 4, :], [], []), A("scan", 128 * h, 128 * h + 128), "out")
+    step[0] = NSTEP
+
+    def named(t, word):
+        if "~" in word:
+            lists = [named(t, w) for w in word.split("~")]
+            return [l[m] for m in range(max(len(l) for l in lists)) for l in lists if m < len(l)]
+        if "," in word:
+            return [i for w in word.split(",") for i in named(t, w)]
+        name, _, rng = word.partition(".")
+        calls = tags.get((t + name.startswith("+"), name.lstrip("+")), [])
+        a, _, b = rng.partition("-")
+        return calls[int(a):int(b or a) + 1] if rng else calls
 
     seq = []
-    for nm in OPT["head"].split():
-        seq += tags[nm]
     for t in range(NSTEP):
-        tg = lambda nm: tags.get(nm + str(t), [])
-        gs, vs, cb = tg("G"), tg("V"), tg("CB")
-        n1, n2, ga = OPT["nv1"], OPT["nv2"], OPT["gw"]
-        if OPT["xc"] and t:
-            gs = gs[:1] + tg("xc") + gs[1:]
-        seq += (tg("xc") if t and not OPT["xc"] else []) + gs[:ga] + tg("gw") + gs[ga:] + tg("hn") + tg("nm") + (tg("x32") if OPT["x32"] == 2 else []) + vs[:n1]
-        rest = vs[n1:]
-        for m, i in enumerate(cb):
-            if m == 16:
-                seq += rest[:n2] + tg("rc")
-                rest = rest[n2:]
-            for nm in ("yu", "sc", "hu"):
-                if m == OPT[nm + "p"]:
-                    seq += tg(nm)
-            seq += [i] + rest[:1]
-            rest = rest[1:]
-        seq += rest
-        for nm in OPT["tail" if t < NSTEP - 1 else "end"].split():
-            seq += tags.get("mask%d" % (t + 1), []) if nm == "mask" else [] if nm == "x32" and OPT["x32"] == 2 else tg(nm)
-    seq += tags["rout"] + tags["yv"]
+        words = OPT["head"][min(t, 1)] + " " + OPT["body"] + " " + OPT["tail"][t == NSTEP - 1]
+        seq += [i for word in words.split() for i in named(t, word)]
     for a, b in zip(seq, seq[1:]):
         ops[b]["after"].append(a)
+    for ch in range(32):
+        mm(A("B2", ch, 256, 32), A("SU", 128 * ch, 128 * ch + 128), A("oneswf", 16, 144, 16), True)
+    cp(A("nv1", 0, 256, key=0), A("B2", 0, 256))
+    ts(A("ei", 0, 256), A("B2", 0, 256), 1.0 / 256, mul, -0.25, add)
+    cp(A("nv1", 256, 512, key=1), A("ei", 0, 256))
+    for h in range(2):
+        o = A("B3", 128 * h, 128 * h + 128)
+        mm(o, A("nv1", 128 * h, 128 * h + 128, key=0), IF(1), True)
+        mm(o, A("nv1", 256 + 128 * h, 384 + 128 * h, key=1), IF(2))
+        mm(o, A("nv1", 256 + 128 * h, 384 + 128 * h, key=1), IF(0))
+    ts(A("pg", 0, 256), A("B3", 0, 256), 65536.0, add)
+    for q in range(4):
+        if q < OPT["nact"]:
+            act(RQ(q), A("R", 1024 * q, 1024 * q + 1024), AF.Relu, C(B247))
+        else:
+            ts(RQ(q), A("R", 1024 * q, 1024 * q + 1024), -247.0, add, 0.0, mx)
+        ts(RQ(q), RQ(q), -1.0, mul, 9.0, add)
+    ts(A("sci"), A("VL", 0, 512), -64.0, add)
+    cp(A("verf"), A("sci"))
+    ts(SH(KEYV), A("v4u", 0, 32), -2048.0, add)
+    w2f("B4", "wselh", SH(KEYV), True, 8)
+    act(A("sel", p=r8), A("B4", p=r8), AF.Identity, C(B2048, r8))
+    dma("sp", H("yv"), A("sel", p=r8), "out", 2.0)
+    dma("sp", H("yx"), A("x4b"), "out", 2.5)
+    for m, q in enumerate((2, 0, 3, 1)):
+        dma("sp", (T["yr"][:, 1024 * q:1024 * q + 1024], [], []), RQ(q), "out", 5.2 - 0.8 * m)
+    dma("act", H("yl"), A("verf"), "out", 2.8)
+    for h in range(2):
+        dma("act", (T["ys"][4 * h:4 * h + 4, :], [], []), A("pg", 128 * h, 128 * h + 128), "out", 2.2)
 
     def hit(a, b):
         return a == b or a.split("#")[0] == b or b.split("#")[0] == a
 
+    opened = {}
+    for o in ops:
+        for k in o["rd"] + o["wr"]:
+            if k in opened and (o["e"] != "pe" or o["flag"][0]):
+                opened.pop(k)[1] = True
+        if o["e"] == "pe":
+            opened[o["wr"][0]] = o["flag"]
     lastw, readers, group = {}, {}, {}
     for i, o in enumerate(ops):
         if o["dma"]:

@@ -11,27 +11,28 @@ def _decl(where, dtype, spec):
 
 _decl("psum", "float32", "B0:512 B1:512 B2:512 B3:512 B4:512 B5:512 B6:512 B7:512")
 _decl("sbuf", "bfloat16", "EF:4096 G:8192 EQ:8192 MK:784 wide:576 bk:1024 idm:768 blk:128 wexp:256 we:24 wg:8 wsel:2048 seld:2048 "
-      "x0r:512 x0b:512 x1b:512 x2b:512 x3b:512 x4b:512 xo0:512 xo1:512 xo2:512 xo3:512 mask0:512 mask1:512 gw:512 eqw:512 eqd:512 eqv:256 "
+      "x0r:512 x0b:512 x1b:512 x2b:512 x3b:512 x4b:512 xo0:512 xo1:512 xo2:512 xo3:512 mask0:512 mask1:512 gw:512 eqw:512 eqd:512 eqv:512 "
       "tcb:1024 tvf:512 yu:512 hu:512 hn:512 rc:512 eqc:512 z:512 efg:512 sg:512 eat:512 iob:128 cst:416 c2112:512 cneg:512 smb:192")
-_decl("sbuf", "float32", "R:5120 SU:4608 VL:1024 TT:5632 ENC:4096 io:256 cv:1024 gk:128 ow2:144 oneswf:144 idf:384 lw:256 sc0:128 col:32 "
-      "TV:4112 sm:640 ev:64 eD:64 d0:128 d1:128 vs:128 dum3:96 a3:96 sel:512 verf:512 scan:576 expd:256 val:512 vm:512 pg:512 "
+_decl("sbuf", "float32", "R:5120 SU:4608 VL:1024 TT:9248 ENC:4096 io:256 cv:1536 gk:128 ow2:144 oneswf:144 idf:384 lw:256 sc0:128 col:32 "
+      "sm:640 ev:64 eD:64 d0:128 d1:128 vs:128 dum3:96 a3:96 sel:512 verf:512 scan:576 expd:256 val:512 vm:512 pg:512 "
       "nv1:512 nv2:512 keyl:512 tmpf:128")
 _decl("sbuf", "int32", "smi:160 coli:32 ei:1024 sci:512")
-_decl("sbuf", "uint16", "v0u:64 v1u:64 v2u:64 v3u:64 v4u:64 of0:64 of1:64 of2:64 of3:64 og:96 smu:128 veru:512 ofcb:64 ofv:64 ofp:32 exu:16")
-_decl("sbuf", "float16", "dif:1024 idh:512 wselh:2048 key2:64 smh:96 w8:144 v0h:512 verh:512 sch:512")
+_decl("sbuf", "uint16", "v0u:64 v1u:64 v2u:64 v3u:64 v4u:64 of0:64 of1:64 of2:64 of3:64 og:96 smu:128 veru:512 ofcb:128 ofv:64 ofp:32 exu:16")
+_decl("sbuf", "float16", "dif:1024 idh:640 wselh:2048 key2:64 smh:96 w8:144 v0h:512 verh:512 sch:512")
 
 DMASEMS = ["dx", "dv0", "de", "dver", "dr0", "dr1", "dr2", "dr3", "deff", "dsu", "dtt", "dtv", "out"]
-SEMAPHORES = ["pe", "act", "dve", "pool", "sent"] + DMASEMS + ["ax%d" % t for t in range(1, 5)] + ["av%d" % t for t in range(1, 5)]
+SEMAPHORES = ["pe", "act", "dve", "pool", "sent"] + DMASEMS + ["ax%d" % t for t in range(1, 5)] + ["av%d" % t for t in range(1, 5)] + ["aj%d" % t for t in range(1, 4)]
 NSTEP, HOP = 4, 3
 D1, FAR = 262144.0, 524288.0
-GUESS = ((0.00087, 1.56, 3.8, 0.00046, 0.12), (0.00095, 1.15, 2.0, 0.0006, 0.14), (0.00105, 1.95, 5.2, 0.0005, 0.08))
+GUESS = ((0.00087, 1.56, 3.8, 0.00046, 0.12, 150), (0.00095, 1.15, 2.0, 0.00052, 0.15, 150), (0.00105, 1.95, 5.2, 0.00055, 0.08, 200),
+         (0.00093, 1.4, 3.0, 0.00052, 0.13, 160))
 ORDER = {}
-OPT = {"rounds": 3, "tries": 4, "noise": 0.4, "look": 1.0, "gain": 10.0, "slip": 0.05, "parts": ((3, 2), (1,), (0,)),
-       "gp": ((32, 96), (128,), (128,), (64, 64)), "gdve": 0, "ep": (1, 1, 1, 2), "expd": "dve", "tb": "dve", "gw": "dve", "rc": "dve",
-       "vw": "dve", "vl": "dve", "val": "act", "rclone": "act", "nact": 2, "tv": "act", "yu": "dve", "tvinit": "act",
-       "head": ("G.0-5 hn TV.0-3 TT.0-7~TV.4-7", "TV.0-3 G.0-1 hn G.2-5 TT.0-7~TV.4-7"),
-       "body": "TT.8-15~TV.8-15 TT.16-23~TV.16-23 TT.24-27~TV.24-27 hu TT.28-31~TV.28-31 tcb tvf val",
-       "tail": ("efg R.0 sg xo +mask R.1 VL", "R.0 efg sg VL xo")}
+OPT = {"swaps": 1500, "heat": 0.0, "by": (0, 3), "rounds": 3, "tries": 2, "noise": 0.4, "gain": 2.0, "slip": 0.0, "parts": ((3, 2), (1,), (0,)),
+       "gp": ((64, 64), (32, 96), (128,), (128,)), "gdve": 1, "ep": (1, 1, 1, 1), "expd": "dve", "tb": "dve", "gw": "dve", "rc": "dve",
+       "vw": "dve", "vl": "dve", "val": "act", "rclone": "act", "nact": 3, "tv": "act", "yu": "dve", "vmode": "table", "prej": 0, "fill": 0, "early": 1, "rout": (0, 3, 1, 2),
+       "head": ("G.0-4 TV.0-3 TT.0-7~TV.4-7", "G.0-4 TT.0-7~TV.0-7"),
+       "body": "TT.8-31~TV.8-31 tcb val tvf",
+       "tail": ("efg sg R.0 xo +mask R.1", "R.0 efg R.1 sg xo")}
 
 
 def schedule(ops):
@@ -44,12 +45,17 @@ def schedule(ops):
             sync = i in o["need"] and not (p["e"] == "pe" and o["e"] == "pe")
             pred[k].append((i, p["lat"] if sync else 0.0, sync))
             succ[i].append((k, p["lat"] if sync else 0.0, sync))
-    costs = [[c[0] + cy * (c[1] + ga * c[2] + sc * c[3]) + pe * c[4] for c in (o["cost"] for o in ops)] for cy, ga, sc, pe, _ in GUESS]
+    hard = [list(p) for p in pred]
+    for k, o in enumerate(ops):
+        for i in o["soft"]:
+            pred[k].append((i, 0.0, False))
+            succ[i].append((k, 0.0, False))
+    costs = [[c[0] + cy * (c[1] + ga * c[2] + sc * c[3]) + pe * c[4] for c in (o["cost"] for o in ops)] for cy, ga, sc, pe, _, _ in GUESS]
     eng = [o["e"] for o in ops]
     lat = [o["lat"] for o in ops]
 
-    def run(before, after, prio, back):
-        cost, wake = costs[0], GUESS[0][4]
+    def run(before, after, prio, back, m=0):
+        cost, wake = costs[m], GUESS[m][4]
         left = [len(p) for p in before]
         rel = list(lat) if back else [0.0] * n
         ready, free, end, seq = {}, {}, [0.0] * n, []
@@ -82,7 +88,8 @@ def schedule(ops):
             t, e = first
             lst = ready[e]
             i = max((i for i in lst if rel[i] <= t + 1e-9), key=lambda m: prio[m])
-            wait = [m for m in lst if t < rel[m] < t + OPT["look"] * cost[i] and prio[m] > prio[i] + OPT["gain"] * (rel[m] - t)]
+            wait = [m for m in lst if t < rel[m] < t + cost[i] and prio[m] > prio[i]
+                    and max(prio[m], cost[m] + prio[i]) + OPT["gain"] * (rel[m] - t) < cost[i] + prio[m]]
             if wait:
                 m = min(wait, key=lambda m: rel[m])
                 fit = [j for j in lst if max(rel[j], t) + cost[j] <= rel[m] + OPT["slip"]]
@@ -104,6 +111,7 @@ def schedule(ops):
         return max(end[i] + lat[i] for i in range(n))
 
     seq, _ = run(pred, succ, [0.0] * n, False)
+    assert len(seq) == n
     base = [0.0] * n
     for i in reversed(seq):
         base[i] = costs[0][i] + max([base[k] + gp + (GUESS[0][4] if sync else 0.0) for k, gp, sync in succ[i]] + [lat[i]])
@@ -116,14 +124,67 @@ def schedule(ops):
             prio.append(keep[i] + (OPT["noise"] * z / 2147483648 if tr else 0.0))
         for r in range(OPT["rounds"]):
             prio = [1.0e6 - i if load[i] else prio[i] for i in range(n)]
-            seq, end = run(pred, succ, prio, False)
+            by = OPT["by"][tr % len(OPT["by"])]
+            seq, end = run(pred, succ, prio, False, by)
             spans = [span(seq, m) for m in range(len(GUESS))]
-            score = sum(s / GUESS[m][0] for m, s in enumerate(spans))
+            score = sum(s / GUESS[m][5] for m, s in enumerate(spans))
             if best is None or score < best[0]:
                 best, keep = (score, seq, spans), prio
-            prio = run(succ, pred, end, True)[1]
-    ORDER["span"] = [round(s, 1) for s in best[2]]
-    return best[1]
+            prio = run(succ, pred, end, True, by)[1]
+    seq = list(best[1])
+    gaps = [[[(j, gp + (gs[4] if sync else 0.0)) for j, gp, sync in hard[i]] for i in range(n)] for gs in GUESS]
+    names = [set(j for j, _, _ in hard[i]) for i in range(n)]
+
+    def timed(seq, m, a, old):
+        cost, gap, end, why, last = costs[m], gaps[m], list(old[0]), list(old[1]), {}
+        for i in reversed(seq[max(0, a - 400):a]):
+            last.setdefault(eng[i], i)
+        for i in seq[a:]:
+            e = eng[i]
+            w = last.get(e) if e else None
+            t = end[w] if w is not None else 0.0
+            for j, gp in gap[i]:
+                if end[j] + gp > t:
+                    t, w = end[j] + gp, j
+            end[i], why[i], last[e] = t + cost[i], w, i
+        return end, why
+
+    def worth(states):
+        spans = [max(end[i] + lat[i] for i in tail) for end, _ in states]
+        return sum(s / GUESS[m][5] for m, s in enumerate(spans)), spans
+
+    tail = [i for i in range(n) if not succ[i]]
+    states = [timed(seq, m, 0, ([0.0] * n, [None] * n)) for m in range(len(GUESS))]
+    now = top = worth(states)
+    keep = list(seq)
+    for it in range(OPT["swaps"]):
+        z = (z * 1103515245 + 12345) % 2147483648
+        end, why = states[(z >> 8) % len(GUESS)]
+        i, pairs = max(tail, key=lambda q: end[q] + lat[q]), []
+        while why[i] is not None:
+            if eng[why[i]] == eng[i] and why[i] not in names[i] and not load[i]:
+                pairs.append((why[i], i))
+            i = why[i]
+        z = (z * 1103515245 + 12345) % 2147483648
+        x, y = pairs[(z >> 8) % len(pairs)]
+        a, b = seq.index(x), seq.index(y)
+        late, seen = {x}, set()
+        for q in seq[a + 1:b]:
+            if eng[q] in seen or not names[q].isdisjoint(late):
+                late.add(q)
+                if eng[q]:
+                    seen.add(eng[q])
+        if not names[y].isdisjoint(late):
+            continue
+        trial = seq[:a] + [q for q in seq[a:b] if q not in late] + [y] + [q for q in seq[a:b] if q in late] + seq[b + 1:]
+        tried = [timed(trial, m, a, states[m]) for m in range(len(GUESS))]
+        new = worth(tried)
+        if new[0] <= now[0] + OPT["heat"] * (1.0 - it / OPT["swaps"]):
+            seq, states, now = trial, tried, new
+            if now[0] < top[0]:
+                top, keep = now, list(seq)
+    ORDER["span"] = [round(s, 1) for s in best[2]] + [round(s, 1) for s in top[1]]
+    return keep
 
 
 def rank_program(g, core, T, topo):
@@ -131,7 +192,7 @@ def rank_program(g, core, T, topo):
     if rank is None:
         return
     n_r = len(T.cores)
-    ops, tags, step = [], {}, [-1]
+    ops, tags, step, opened = [], {}, [-1], {}
     Q = {"pe": g.tensor, "act": g.scalar, "dve": g.vector, "pool": g, "sp": g.sync}
 
     def A(name, a=None, b=None, s=None, key=None, p=None):
@@ -150,7 +211,10 @@ def rank_program(g, core, T, topo):
         for i in ins:
             if isinstance(i, tuple):
                 rd += i[1] + i[2]
-        ops.append({"e": e, "fn": fn, "rd": rd, "wr": wr, "dma": dma, "ext": ext, "inc": False, "cost": cost, "lat": lat, "after": list(after), "n": 16})
+        for k in rd + wr:
+            if k in opened and e != "pe":
+                opened.pop(k)[1] = True
+        ops.append({"soft": [], "e": e, "fn": fn, "rd": rd, "wr": wr, "dma": dma, "ext": ext, "inc": False, "cost": cost, "lat": lat, "after": list(after), "n": 16})
 
     def est(o, ins, two=False, fast=True, fix=0.0):
         n = max(o[3], ins[0][3]) if ins else o[3]
@@ -204,8 +268,20 @@ def rank_program(g, core, T, topo):
     def mm(o, l, r, start=False):
         c = max(min(64, l[3]), r[3]) * (4 if SCRATCH[l[4]][2] == "float32" else 1)
         flag = [start, False]
+        if start and o[4] in opened:
+            opened.pop(o[4])[1] = True
         op("pe", lambda: g.tensor.matmul(o[0], l[0], r[0], flag[0], flag[1]), [o], [l, r], (0.0, 0, 0, 0, c))
-        ops[-1]["flag"] = flag
+        opened[o[4]] = flag
+
+    def join(k, by=8):
+        run = ops[-k:]
+        del ops[-k:]
+        for a in range(0, k, by):
+            part = run[a:a + by]
+            o = dict(part[0], fn=lambda part=part: [q["fn"]() for q in part][-1], cost=(0.0, 0, 0, 0, sum(q["cost"][4] for q in part)))
+            for side in ("rd", "wr"):
+                o[side] = sorted(set(x for q in part for x in q[side]))
+            ops.append(o)
 
     pool_tail = []
 
@@ -230,26 +306,28 @@ def rank_program(g, core, T, topo):
         op(e, lambda: Q[e].dma_start(o[0], i[0]), [o], [i], (0.1, 0, 0, 0, 0), dma=sem, lat=lat, after=queue_tail.get(e, ()))
         queue_tail[e] = (len(ops) - 1,)
 
-    def send(src, dname, dst, sem, lat):
+    def send(what, where, dst, src, sem, lat):
         rid, pid, _ = topo.addr(dst)
         m = topo.mask(core, dst)
-        op("pool", lambda: g.remote_dma(T[dname][:], src[0], T.sem[sem], T.sem["sent"], pid, rid, m), [], [src], (0.5, 0, 0, 0, 0), ext="send")
+        op("pool", lambda: g.remote_dma(where[0], what[0], T.sem[sem], T.sem["sent"], pid, rid, m), [], [what], (0.5, 0, 0, 0, 0), ext="send")
         ops[-1]["n"] = len(topo.engines(core, dst))
-        return (len(ops) - 1, lat)
-
-    def arrive(name, sem, src, sent):
-        op(None, None, [A(name)], [], (0.0, 0, 0, 0, 0), dma=sem, ext="arr", lat=sent[1], after=(sent[0],))
+        op(None, None, [where], [], (0.0, 0, 0, 0, 0), dma=sem, ext="arr", lat=lat, after=(len(ops) - 1,))
         ops[-1]["n"] = len(topo.engines(src, core))
+        return len(ops) - 2
 
     def f2w(o, wide, src, first=True, p=None):
         for p0 in range(16):
             mm(o, wide(16 - p0, 144 - p0), A(src[0], src[1] + p0, src[1] + 512, 16, key=src[2], p=p), first and p0 == 0)
+        join(16)
 
     def w2f(bank, sel, src, first=False, cols=128):
         for p0 in range(16):
             mm(A(bank, p0, 512, 16, p=slice(0, 8) if cols == 8 else None), A(sel, 128 * p0, 128 * p0 + 128, 128 // cols), src, first and p0 == 0)
+        join(16)
 
     H = lambda name: (T[name][:], [], [])
+    VU = lambda t, a=0, b=32: A("v%du" % t, a, b, key="v")
+    JU = lambda t: A("v%du" % t, 32, 64, key="j")
     C = lambda j, p=None: A("col", j, j + 1, key=j, p=p)
     PARTKEYS = ["p%d" % q for q in range(4)]
     S = lambda j: A("sm", 32 * j, 32 * j + 32, key=j)
@@ -262,17 +340,19 @@ def rank_program(g, core, T, topo):
     IH = lambda j: A("idh", 128 * j, 128 * j + 128, key=j)
     IF = lambda j: A("idf", 128 * j, 128 * j + 128, key=j)
     WD = lambda j: (lambda a, b: A("wide", 144 * j + a, 144 * j + b, key=j))
-    CS = lambda j: A("cst", 32 * j, 32 * j + 32, key=j)
+    CS = lambda j: A("cst", 32 * j, 32 * j + 32, key=[j] + ["%d_%d" % (j, ch) for ch in range(4)])
     RQ = lambda q: A("EQ", 1024 * q, 1024 * q + 1024, key="r%d" % q)
     eq, ne, ge, lt = ALU.is_equal, ALU.not_equal, ALU.is_ge, ALU.is_lt
     add, sub, mul, mx, mn, band, shr = ALU.add, ALU.subtract, ALU.mult, ALU.max, ALU.min, ALU.bitwise_and, ALU.arith_shift_right
-    PART, P16, G16, G16P, TWOF, LIM, PLO, PHI, B256, B1, BSG, B2, B254, B247, B2048, T1, T2, T3, ACNT, MLO, MHI, B256N, T4, DC, DB = range(25)
-    LANE, DUMR, BF_, THR, CAND, MNV, NT, NC, CG, LQ, NG, JN, JD = range(13)
+    PART, P16, G16, G16P, TWOF, LIM, PLO, PHI, T1, T2, T3, ACNT, MLO, MHI, T4, DC, DB, DV, DV2 = range(19)
+    NK = 3 if OPT["vmode"] == "merged" else 2
+    TB = 0 if NK == 3 else 4608
+    LANE, DUMR, BF_, THR, CAND, MNV, NC, CG, LQ, NG, JN, JD, NT = range(13)
     ONE, NEG, TWO, K4, N8K, K256 = range(6)
     ONESW, JW, JW2, ONESN = range(4)
     CK, CW, LIFT, LIFTV, CZ, OWN, OWNH = 0, 1, 2, 3, 4, 5, 12
     CE, CKEY = A("cst", 192, 256, key="e"), A("cst", 256, 384, key="k")
-    NTG, NTN, CL, SW = range(4)
+    NTG, NTN, CL, SW, NTP = range(5)
     KEYV, TGT, JUH = range(3)
     io = lambda n: A("io", 0, n)
     r8 = slice(0, 8)
@@ -287,7 +367,9 @@ def rank_program(g, core, T, topo):
     for q in range(4):
         dma("sp", A("EF", 1024 * q, 1024 * q + 1024, key=q), H("eff"), "deff", 10.0)
     iota(A("coli", 0, 1, key=0), [[0, 1]], 0, 1, flt=False)
-    iota(io(256), [[1, 256]])
+    iota(C(PART), [[0, 1]], 0, 1)
+    iota(io(144), [[1, 144]])
+    iota(C(T1), [[0, 1]], 16, 16)
     iota(A("iob"), [[1, 128]])
     iota(A("MK"), [[0, 49], [1, 16]])
     iota(CE, [[0, 64]], -15 * int(D1))
@@ -298,17 +380,19 @@ def rank_program(g, core, T, topo):
     iota(TM(6), [[0, 8]], 1)
     iota(A("R", 4096, 4608, key=8), [[0, 512]], 200)
     iota(CS(CK), [[0, 32]], 256000)
-    iota(CS(LIFT), [[0, 16], [2560, 2]], 2048)
+    iota(CS(LIFT), [[0, 16], [2048, 2]], 6656 - TB)
     iota(A("tmpf", 0, 16, key=[0, 1]), [[0, 2], [16, 4], [64, 2]], 15)
     iota(A("tmpf", 16, 24, key=2), [[0, 2], [16, 4]], 15)
     iota(A("lw"), [[0, 4], [1, 64]], -48)
     for ch in range(4):
-        iota(A("cv", 256 * ch, 256 * ch + 256, key=ch), [[16 << ch, 8], [0, 2], [1 << ch, 16]], 128 << ch)
+        iota(A("cv", 384 * ch, 384 * ch + 384, key=ch), [[16 << ch, 8], [0, 3], [1 << ch, 16]], 128 << ch)
     iota(CS(LIFTV), [[0, 32]], 2048)
     iota(CS(CZ), [[0, 32]], 20480)
     iota(S(LQ), [[0, 4], [16, 8]], 128)
-    iota(A("c2112"), [[0, 512]], 2112)
-    iota(A("ENC"), [[-1, 8], [256, 512]], 8)
+    iota(C(LIM), [[0, 1]], 3 * int(D1))
+    iota(A("d0"), [[0, 128]])
+    iota(A("TT", 0, 4096, key="v"), [[0, 4096]])
+    asel(A("wsel"), A("TT", 0, 2048, key="v"), [[-1, 16], [-16, 8], [0, 16]], ne, FAR, 0, 1)
 
     def seld(t, chain):
         pat = [[-1001, 16], [-16, 8], [1000, 16]]
@@ -316,27 +400,29 @@ def rank_program(g, core, T, topo):
         if t:
             asel(A("seld"), A("seld"), pat, ne, 0.0, 1000 * (16 - t), 1, chain)
 
+    seld(0, True)
+    if OPT["vw"] == "act":
+        iota(A("c2112"), [[0, 512]], 2112)
+    for h in range(2):
+        iota(A("ENC", 2048 * h, 2048 * h + 2048, key=h), [[-1, 4], [256, 512]], 8 - 4 * h)
     if OPT["rclone"] != "act":
         iota(A("cneg"), [[0, 512]], -int(FAR))
 
-    for j, c in ((B256, 256.0), (B256N, -256.0), (B1, 1.0), (BSG, 252.5), (B2, 2.0), (B254, 254.0), (B247, -247.0), (B2048, 2048.0), (LIM, 3 * D1)):
-        ms(C(j), c)
-    cp(C(PART), A("coli", 0, 1, key=0))
+    lin = lambda o, i, scale, bias: act(o, i, AF.Identity, bias, scale)
     ts(A("coli", 1, 2, key=1), A("coli", 0, 1, key=0), 15, band)
     cp(C(P16), A("coli", 1, 2, key=1))
     tt(C(G16), C(PART), C(P16), sub)
     ts(C(G16P), C(G16), 16.0, add)
     ts(C(TWOF), C(P16), 2.0, mul, 1.0, add)
-    ts(C(T1), C(PART), 16.0, mul, 16.0, add)
     ts(C(T3), C(G16), 24.0, add)
     ts(C(MLO), C(P16), 8.0, lt, -8388608.0, mul)
     ts(C(MHI), C(P16), 8.0, ge)
     ts(ID(ONE), A("iob"), C(PART), eq)
     for j, c in ((NEG, -1.0), (TWO, 2.0), (K4, 4096.0), (N8K, -8192.0), (K256, 256.0)):
-        act(ID(j), ID(ONE), AF.Copy, None, c)
+        act(ID(j), ID(ONE), AF.Silu if j == K4 else AF.Copy, None, c)
     for j, c in ((0, 1.0), (1, -512.0), (2, 131072.0)):
         act(IF(j), ID(ONE), AF.Copy, None, c)
-    for j, c in ((0, 1.0), (1, 2.0 ** -14), (2, 256.0), (3, -16.0)):
+    for j, c in ((0, 1.0), (1, 2.0 ** -14), (2, 256.0), (3, -16.0), (4, -1.0)):
         ts(IH(j), ID(ONE), c, mul)
     ts(WD(JW)(0, 144), io(144), C(G16P), eq, C(TWOF), mul)
     act(WD(JW2)(0, 144), WD(JW)(0, 144), AF.Copy, None, -2.0)
@@ -350,30 +436,30 @@ def rank_program(g, core, T, topo):
     ts(A("cst", 193, 256, 2, key="e"), A("cst", 193, 256, 2, key="e"), C(MLO), add)
     ms(A("eD"), -16777216.0)
     ts(A("eD", 1, 64, 2), A("eD", 1, 64, 2), C(MHI), mul)
-    ms(A("d0"), 0.0)
-    ts(C(DC), C(P16), 4096.0, add)
-    ts(C(DB), C(P16), 5120.0, add)
-    ts(A("x0b"), A("x0r"), -1.0, mul, 256.0, add)
+    for j, c in ((DC, 9216.0 - TB), (DB, 9232.0 - TB), (DV, 4096.0), (DV2, 4112.0)):
+        lin(C(j), C(P16), 1.0, c)
+    lin(A("x0b"), A("x0r"), -1.0, 256.0)
     ts(A("v0h", p=r8), A("sci", p=r8), -2048.0, add)
     f2w(A("B6", 0, 32), lambda a, b: A("w8", a, b, p=r8), ("v0h", 0, None), p=r8)
     ts(SI(0), A("B6", 0, 32), 2048.0, add)
-    cp(A("v0u", 0, 32, key=1), SI(0))
+    cp(VU(0), SI(0))
     ts(SI(1), SI(0), 511, band)
     cp(SUU(3), SI(1))
     f2w(A("B5", 0, 32), WD(JW), ("x0r", 0, None))
-    cp(A("v0u", 32, 64, key=0), A("B5", 0, 32))
+    cp(JU(0), A("B5", 0, 32))
     ts(A("sci"), A("ei", 0, 512, key=[0, 1]), 9, shr)
     ts(A("B7"), A("sci"), -131073.0, mul, 8.0, add)
     ts(A("nv1"), A("ei", 0, 512, key=[0, 1]), 256.0, mul)
     tt(A("SU", 0, 512, key=0), A("nv1"), A("B7"), add)
-    ts(A("VL", 0, 512), A("ei", 512, 1024, key=[2, 3]), 64.0, add)
+    VOFF = 64.0 if OPT["vw"] == "act" else 0.0
+    ts(A("VL", 0, 512), A("ei", 512, 1024, key=[2, 3]), VOFF, add)
     for q in range(8):
         gq = A("G", 512 * q, 512 * q + 512, key="r%d" % q)
         rq = A("EQ", 512 * q, 512 * q + 512, key="r%d" % (q // 2))
         ts(gq, rq, 5.0, ge, -247.0, mul)
         mm(A("B%d" % (q % 4)), ID(NEG), rq, True)
         mm(A("B%d" % (q % 4)), ID(ONE), gq)
-        act(A("R", 512 * q, 512 * q + 512, key=q), A("B%d" % (q % 4)), AF.Identity, C(B256))
+        act(A("R", 512 * q, 512 * q + 512, key=q), A("B%d" % (q % 4)), AF.Identity, 256.0)
     scan(TM(7), TM(5), TM(6), 0.25, mul, mul)
     for j, sh, a in ((PLO, 0.0, 8), (PHI, 8.0, 12)):
         ts(TM(a), io(8), sh, add, C(P16), eq)
@@ -382,17 +468,19 @@ def rank_program(g, core, T, topo):
     ts(A("wexp", 0, 128), A("gk", 0, 128), C(G16), eq, C(PLO), mul)
     ts(A("wexp", 128, 256), A("gk", 0, 128), C(G16), eq, C(PHI), mul)
     ts(A("blk"), A("gk", 0, 128), C(G16), eq)
-    cp(A("wg"), A("blk", 0, 128, 16))
-    ts(A("we", 0, 8), A("wg"), -256.0, mul)
-    ts(A("we", 8, 24), A("wexp", 0, 256, 16), -1.0, mul)
-    ts(S(LANE), S(LANE), C(P16), add)
-    ts(S(DUMR), S(LANE), 4096.0, add)
-    ts(A("dum3", 0, 32), S(LANE), 4608.0, add)
-    ts(A("dum3", 32, 64), S(LANE), 512.0, add)
-    ts(A("dum3", 64, 96), S(LANE), 4608.0, add)
+    act(A("wg"), A("blk", 0, 128, 16), AF.Copy)
+    act(A("we", 0, 8, key=0), A("blk", 0, 128, 16), AF.Copy, None, -256.0)
+    act(A("we", 8, 24, key=1), A("wexp", 0, 256, 16), AF.Copy, None, -1.0)
+    lin(S(LANE), S(LANE), 1.0, C(P16))
+    lin(S(DUMR), S(LANE), 1.0, 4096.0)
+    for q, c in enumerate((4608.0, 512.0, 4608.0)):
+        lin(A("dum3", 32 * q, 32 * q + 32, key=q), S(LANE), 1.0, c)
+    for t in range(NSTEP):
+        lin(S(NT + t), S(LANE), 8.0, 8192.0 + t)
+    lin(S(LQ), S(LQ), 1.0, C(P16))
     for ch in range(4):
-        ts(A("cst", 32 * OWN + 8 * ch, 32 * OWN + 8 * ch + 8, key=OWN), A("sm", 32 * LQ + 8 * ch, 32 * LQ + 8 * ch + 8, key=LQ), C(P16), add, float(4 << ch), mul)
-    ts(CS(OWNH), CS(OWN), 0.5, mul)
+        for j, c in ((OWN, 4), (OWNH, 2)):
+            act(A("cst", 32 * j + 8 * ch, 32 * j + 8 * ch + 8, key="%d_%d" % (j, ch)), A("sm", 32 * LQ + 8 * ch, 32 * LQ + 8 * ch + 8, key=LQ), AF.Copy, None, float(c << ch))
     mm(A("B7", 0, 128), ID(ONE), ID(ONE), True)
     c2, c3 = A("coli", 8, 16, key=2), A("coli", 16, 24, key=3)
     ts(c2, io(8), -1.0, mul, C(P16), add)
@@ -403,14 +491,11 @@ def rank_program(g, core, T, topo):
     ts(c3, c3, 15, band)
     ts(TM(11), c3, C(P16), mx, C(G16), add)
     for d in range(8):
-        ts(A("rc", 128 * (d % 4), 128 * (d % 4) + 128, key="p%d" % (d % 4)), A("iob"), A("tmpf", 80 + d, 81 + d, key=10), eq)
-        tt(A("dif", 128 * d, 128 * d + 128, key=d), A("rc", 128 * (d % 4), 128 * (d % 4) + 128, key="p%d" % (d % 4)), A("B7", 0, 128), sub)
+        ts(A("z", 128 * (d % 4), 128 * (d % 4) + 128, key=d % 4), A("iob"), A("tmpf", 80 + d, 81 + d, key=10), eq)
+        tt(A("dif", 128 * d, 128 * d + 128, key=d), A("z", 128 * (d % 4), 128 * (d % 4) + 128, key=d % 4), A("B7", 0, 128), sub)
         ts(A("bk", 128 * d, 128 * d + 128, key=d), A("iob"), A("tmpf", 88 + d, 89 + d, key=11), eq, 8192.0, mul)
-    ts(A("tmpf", 112, 128, key=[14, 15]), io(16), C(P16), eq)
-    for p0 in range(16):
-        ts(A("wselh", 128 * p0, 128 * p0 + 128, key=p0), A("blk"), A("tmpf", 112 + p0, 113 + p0, key=[14, 15]), mul)
-    ts(A("wsel"), A("wselh"), FAR, mul)
-    seld(0, True)
+    for h in range(4):
+        ts(A("wselh", 512 * h, 512 * h + 512, key=h), A("wsel", 512 * h, 512 * h + 512), 1.0 / FAR, mul)
     ms(A("sc0"), -1.0 / 16)
     ms(A("sc0", 0, 128, 16), 1.0e6)
     for ch in range(4):
@@ -425,13 +510,8 @@ def rank_program(g, core, T, topo):
     ts(C(T2), C(MHI), 144.0, mul, -128.0, add)
     ts(TM(3), TM(0), C(T2), add, C(T4), mul)
     ts(A("exu", 4, 12), TM(3), 128.0, add)
-    for q in range(8):
-        if OPT["tvinit"] == "act":
-            act(A("TV", 512 * q, 512 * q + 512, key=q), A("x0r"), AF.Copy)
-        else:
-            dma("sp", A("TV", 512 * q, 512 * q + 512, key=q), A("VL", 0, 512), "dtv", 8.0)
-    for q in (0, 1, 2, 3, 4, 5, 6, 7, 9):
-        dma("sp", A("TT", 512 * q, 512 * q + 512, key="c" if q < 9 else "b"), A("VL", 0, 512), "dtt", 12.0)
+    for q in range(9, 18):
+        dma("sp", A("TT", 512 * q, 512 * q + 512, key="cb"), A("VL", 0, 512), "dtt", 12.0)
     for q in range(1, 8):
         dma("sp", A("SU", 512 * q, 512 * q + 512, key=q), A("SU", 0, 512, key=0), "dsu", 16.0)
 
@@ -440,14 +520,15 @@ def rank_program(g, core, T, topo):
 
     def edge(t):
         mask = A("mask%d" % (t % 2))
-        act(mask, IN(A("MK"), A("v%du" % t, 32, 64, key=0 if t == 0 else None)), AF.Copy)
+        act(mask, IN(A("MK"), JU(t)), AF.Copy)
         if t == 0:
             tt(A("sel"), IN(A("SU", 0, 512, key=0), SUU(3)), mask, mx)
         else:
-            tt(A("sel"), IN(SUw, A("v%du" % t, 0, 32)), mask, mx)
+            tt(A("sel"), IN(SUw, VU(t)), mask, mx)
         mm(A("B5", 32, 96), ID(ONE), CE, True)
         for p0 in range(8):
             mm(A("B5", 32, 96), A("ow2", 16 - p0, 144 - p0), A("sel", p0, 512, 8))
+        join(8, 2)
         scan(A("ev"), A("eD"), A("B5", 32, 96), 0.0, add, mx)
         ts(SUU(0), E, 1.0 / 256, mul, 0.25, add)
         for a, b in ((3, 4), (0, 3)):
@@ -455,7 +536,7 @@ def rank_program(g, core, T, topo):
             if OPT["vl"] == "act":
                 act(A("verf", 128 * a, 128 * b, key=keys), ver, AF.Copy)
                 ver = A("verf", 128 * a, 128 * b, key=keys)
-            ts(A("veru", 128 * a, 128 * b, key=keys), ver, -63.75, add)
+            ts(A("veru", 128 * a, 128 * b, key=keys), ver, 0.25 - VOFF, add)
         ts(SI(2), E, 1.0 / 256, mul, 10240.0, add)
         ts(S(BF_), SI(2), -10240.0, add)
         mm(A("B5", 96, 128), ID(ONE), CS(CW), True)
@@ -470,7 +551,8 @@ def rank_program(g, core, T, topo):
         first_v(t)
         mm(A("B4"), ID(ONE), A(x), True)
         if not last:
-            ts(SH(JUH), A("v%du" % t, 32, 64), -512.0, add)
+            ts(SH(JUH), JU(t), -512.0, add)
+        if not last and OPT["prej"]:
             next_j(t, "n", lambda a, s: A("EF", t + 8 * a, 4096, 8 * s), "B1", "hn", A("B0", 0, 32))
             cp(S(JN), A("B0", 0, 32))
         gkey = lambda ch, a, b: ["%d_%d" % (ch, m) for m in range(a // 16, b // 16)]
@@ -484,14 +566,13 @@ def rank_program(g, core, T, topo):
         for a, b in ((3, 4), (0, 3)):
             ts(A("verh", 128 * a, 128 * b, key=list(range(a, b))), A("veru", 128 * a, 128 * b, key=list(range(a, b))), -2048.0, add, 1.0 / 16, mul)
         if OPT["vl"] == "dve":
-            ts(A("verf"), A("veru"), 64.0, add)
+            ts(A("verf"), A("veru"), VOFF, add)
         copy(OPT["gw"], A("gw"), IN(A("R", 0, 4608), SUU(1)))
         tt(A("eqw"), A("gw"), A("B4"), eq)
         f2w(A("B7", 0, 32), WD(ONESW), ("gw", 0, None))
         f2w(A("B7", 0, 32), WD(ONESN), ("eqw", 0, None), False)
         ts(S(THR), A("B7", 0, 32), 256.0, ge, 8388608.0, mul)
         tt(S(CAND), S(THR), A("B5", 96, 128), add)
-        ts(S(NT), S(LANE), 8.0, mul, 8192.0 + t, add)
         for ch in (3, 2, 1, 0):
             bank = "B%d" % ch
             olde = ["r%d" % (2 * ch), "r%d" % (2 * ch + 1)] if ch < 2 and t in (0, NSTEP - 1) else []
@@ -513,22 +594,42 @@ def rank_program(g, core, T, topo):
             scan(A("scan", 144 * ch, 144 * ch + 128, key=ch), A("sc0"), sl("keyl"), 0.0, add, mn)
             for k in range(16):
                 mm(A(bank, 128 + k, 384, 16), eqk(k), A("we", 8, 24), k == 0)
+            join(16, 4)
 
     def first_v(t):
-        ts(SH(KEYV), A("v%du" % t, 0, 32), -2048.0, add)
+        ts(SH(KEYV), VU(t), -2048.0, add)
         for d in range(8):
             mm(A("B4", 32 * d, 32 * d + 32), A("dif", 128 * d, 128 * d + 128, key=d), SH(KEYV), True)
-        ts(A("eqv", 0, 256), A("B4", 0, 256), 0.0, eq)
+        join(8)
+        chain = OPT["vmode"] == "chain"
+        if chain:
+            for p0 in range(16):
+                mm(A("B4", 256 + p0, 512, 16), A("wselh", 128 * p0, 128 * p0 + 128), A("smh", 0, 32, 2, key=KEYV), True)
+                mm(A("B4", 256 + p0, 512, 16), IH(4), A("smh", 1, 32, 2, key=KEYV))
+        ts(A("eqv", 0, 512 if chain else 256), A("B4", 0, 512 if chain else 256), 0.0, eq, 2.0, mul)
         mm(A("B4", 256, 288), IH(0), SH(KEYV), True)
         mm(A("B4", 256, 288), ID(ONE), CS(LIFTV))
         for d in range(8):
             mm(A("B4", 256, 288), A("bk", 128 * d, 128 * d + 128, key=d), A("eqv", 32 * d, 32 * d + 32))
-        ts(A("ofv", 0, 64, 2), A("B4", 256, 288), C(DC), mn)
+        join(8)
+        if chain:
+            for p0 in range(16):
+                mm(A("B4", 257, 288, 2), ID(K4), A("eqv", 256 + p0, 512, 16))
+            ts(A("ofv", 0, 32, 2, key=0), A("B4", 256, 288, 2), C(DV), mn)
+            ts(A("ofv", 1, 32, 2, key=1), A("B4", 257, 288, 2), C(DV2), mn)
+            return
+        if OPT["vmode"] == "merged":
+            ts(A("ofcb", 2, 128, 4, key="v"), A("B4", 256, 288), C(DV), mn)
+            return
+        ts(A("ofv", 0, 64, 2), A("B4", 256, 288), C(DV), mn)
         for c in range(31, -1, -1):
-            act(IN(A("TV"), A("ofv", 2 * c, 2 * c + 1)), A("cv", 32 * c, 32 * c + 16, key=c // 8), AF.Silu)
-        copy(OPT["tv"], A("tvf"), IN(A("TV", 0, 4096), A("v%du" % t, 0, 32)))
+            act(IN(A("TT", 0, 4112, key="v"), A("ofv", 2 * c, 2 * c + 1)), A("cv", 48 * c, 48 * c + 16, key=c // 8), AF.Silu)
+            tags.setdefault((t, "TV"), []).append(tags[(t, "TT")].pop())
 
-    def patchers():
+    def patchers(t):
+        if OPT["vmode"] == "chain":
+            return
+        copy(OPT["tv"], A("tvf"), IN(A("TT", 0, 4096, key="v"), VU(t)))
         zv = A("B7", 96, 128)
         mm(zv, IH(0), SH(KEYV), True)
         mm(zv, ID(ONE), CS(LIFTV))
@@ -540,10 +641,11 @@ def rank_program(g, core, T, topo):
     def next_j(t, name, ef, bank, sign, out):
         mm(A(bank), ID(ONE), A("x%db" % t), True)
         mm(A(bank), ID(NEG), ef(0, 1))
-        act(A(sign), A(bank), AF.Sign, C(BSG), -1.0)
+        act(A(sign), A(bank), AF.Sign, 252.5, -1.0)
         mm(out, IH(0), SH(JUH), True)
         for p0 in range(16):
             mm(out, WD(JW)(16 - p0, 144 - p0), ef(p0, 16))
+        join(16)
         f2w(out, WD(JW2), (sign, 0, None), False)
 
     def decide(t):
@@ -570,50 +672,59 @@ def rank_program(g, core, T, topo):
             tt(A("key2", 2 * c0, 2 * c0 + 2 * w, 2, key=["c" + k for k in keys]), cc, sw, sub)
             tt(A("key2", 2 * c0 + 1, 2 * c0 + 2 * w, 2, key=["b" + k for k in keys]), A("smi", 64 + c0, 64 + c0 + w, key=2), sw, sub)
             ts(W_("smu", 2), cc, -8192.0, add)
-            copy(OPT["rc"], A("rc", 16 * c0, 16 * (c0 + w), key=keys), IN(Rw, W_("smu", 2)))
+            st = OPT["fill"] or w
+            for c in range(c0 + w - st, c0 - 1, -st):
+                copy(OPT["rc"], A("rc", 16 * c, 16 * (c + st), key="q%d" % c), IN(Rw, A("smu", 64 + c, 64 + c + st, key=W_("smu", 2)[1][0][4:])))
             k2 = A("key2", 2 * c0, 2 * c0 + 2 * w, key=[y + k for k in keys for y in "cb"])
             for d in range(8):
                 mm(A("B6", 2 * w * d, 2 * w * d + 2 * w), A("dif", 128 * d, 128 * d + 128, key=d), k2, True)
+            join(8)
             ts(A("eqd", 16 * c0, 16 * c0 + 16 * w, key=keys), A("B6", 0, 16 * w), 0.0, eq)
             back = A("B7", 64, 64 + 2 * w)
             mm(back, IH(0), k2, True)
             mm(back, ID(ONE), A("cst", 32 * LIFT, 32 * LIFT + 2 * w, key=LIFT))
             for d in range(8):
                 mm(back, A("bk", 128 * d, 128 * d + 128, key=d), A("eqd", 16 * c0 + 2 * w * d, 16 * c0 + 2 * w * d + 2 * w, key=keys))
+            join(8)
             for y, dum in ((0, DC), (1, DB)):
-                ts(A("ofcb", 2 * c0 + y, 2 * c0 + 2 * w, 2, key=["cb"[y] + k for k in keys]), A("B7", 64 + y, 64 + 2 * w, 2), C(dum), mn)
+                ts(A("ofcb", 4 * c0 + y, 4 * c0 + 4 * w, 4, key=["cb"[y] + k for k in keys]), A("B7", 64 + y, 64 + 2 * w, 2), C(dum), mn)
             for c in range(c0 + w - 1, c0 - 1, -1):
-                act(IN(A("TT"), A("ofcb", 2 * c, 2 * c + 2, key=[y + k for k in keys for y in "cb"])), A("cv", 32 * c, 32 * c + 32, key=c // 8), AF.Silu)
-            if not last:
-                copy(OPT["yu"], A("yu", 16 * c0, 16 * (c0 + w), key=keys), IN(A("EF"), W_("smu", 2)))
+                act(IN(A("TT", TB, None, key="cb" if TB else None), A("ofcb", 4 * c, 4 * c + NK, key=[y + k for k in keys for y in "cb"] + ["v"] * (NK - 2))),
+                    A("cv", 48 * c, 48 * c + 16 * NK, key=c // 8), AF.Silu)
+            if not last and OPT["prej"]:
+                for c in range(c0 + w - st, c0 - 1, -st):
+                    copy(OPT["yu"], A("yu", 16 * c, 16 * (c + st), key="q%d" % c), IN(A("EF"), A("smu", 64 + c, 64 + c + st, key=W_("smu", 2)[1][0][4:])))
         allp = lambda j: ["%d%s" % (j, k) for k in PARTKEYS]
         K = A("smi", 96, 128, key=["3p%d%s" % (ch, h) for ch in range(4) for h in "ab"])
         CC, CU, SWA = A("smi", 128, 160, key=allp(4)), A("smu", 64, 96, key=allp(2)), A("smb", 32 * SW, 32 * SW + 32, key=allp(SW))
         cf, dl, may = A("d1", 1, 64, 2, key=1), A("d0", 1, 64, 2, key=1), A("d1", 0, 64, 2, key=0)
-        if not last:
+        prej = not last and OPT["prej"]
+        if prej:
             ju = A("d1", 65, 128, 2, key=3)
             next_j(t, "u", lambda a, s: A("yu", a, 512, s), "B7", "hu", A("B7", 0, 32))
             cp(ju, A("B7", 0, 32))
             tt(S(JD), S(JN), ju, sub)
-        patchers()
-        act(A("tcb", 0, 512, key=0), IN(A("TT", 0, 4096), CU), AF.Copy)
-        copy(OPT["tb"], A("tcb", 512, 1024, key=1), IN(A("TT", 4608, 5120), SUU(0)))
+        act(A("tcb", 0, 512, key=0), IN(A("TT", 4608, 8704, key="cb"), CU), AF.Copy)
+        copy(OPT["tb"], A("tcb", 512, 1024, key=1), IN(A("TT", 8704, 9216, key="cb"), SUU(0)))
+        patchers(t)
         ts(SB(NTG), K, C(LIM), ge)
-        ts(SB(NTN), K, C(LIM), ge, -8192.0, mul)
+        ts(SB(NTP), K, C(LIM), ge, 8192.0, mul)
+        if OPT["vw"] == "act":
+            ts(SB(NTN), K, C(LIM), ge, -8192.0, mul)
         ts(cf, CC, -8192.0, add)
-        tt(S(NC), S(NT), CC, sub)
+        tt(S(NC), S(NT + t), CC, sub)
         tt(dl, S(NC), SB(NTG), mul)
-        if not last:
+        if prej:
             tt(A("d0", 65, 128, 2, key=3), S(JD), SB(NTG), mul)
         tt(SH(TGT), A("key2", 0, 64, 2, key=["c" + k for k in PARTKEYS]), dl, add)
-        tt(S(CG), cf, SB(NTN), sub)
+        tt(S(CG), cf, SB(NTP), add)
         mm(A("B4"), ID(ONE), A("x%db" % t), True)
         w2f("B4", "wsel", SB(NTG))
         tt(A("eqc"), A("rc"), A("B4"), eq)
         if OPT["val"] == "act":
             mm(A("B4"), ID(ONE), A("x%db" % t), True)
             mm(A("B4"), ID(K256), A("eqc"))
-            act(A("val"), A("B4"), AF.Relu, C(B256N))
+            act(A("val"), A("B4"), AF.Relu, -256.0)
         else:
             tt(A("val"), A("eqc"), A("B4"), mul)
         for ch in range(4):
@@ -639,7 +750,7 @@ def rank_program(g, core, T, topo):
             tt(A("nv2"), A("nv1"), A("B3"), mx)
         else:
             kept("B6", SB(NTG), ID(K4), True)
-            act(A("eat"), A("B6"), AF.Relu, C(B1), -1.0)
+            act(A("eat"), A("B6"), AF.Relu, 1.0, -1.0)
             mm(A("B3"), IH(3), A("verh"), True)
             w2f("B3", "wselh", SH(TGT))
             tt(A("nv2"), A("eat"), A("B3"), mul)
@@ -650,20 +761,19 @@ def rank_program(g, core, T, topo):
         f2w(zn, WD(ONESN), ("tcb", 0, 0), False)
         f2w(zn, WD(ONESN), ("tcb", 512, 1), False)
         ts(may, zn, 4096.0, lt)
-        if last:
+        if not prej:
             scan(A("vs", 0, 64), A("d0", 0, 64, key=[0, 1]), A("d1", 0, 64, key=[0, 1]), 0.0, mul, add)
-            cp(A(of, 32, 64), A("vs", 1, 64, 2))
-            cp(A(of, 0, 32), A("vs", 1, 64, 2))
+            cp(A(of, 0, 32, key=0), A("vs", 1, 64, 2))
         else:
             ts(A("d1", 64, 128, 2, key=2), zn, 4096.0, lt)
             scan(A("vs"), A("d0"), A("d1"), 0.0, mul, add)
             cp(A(of, 0, 64), A("vs", 1, 128, 2))
-        tt(SB(CL), may, SB(NTG), mul)
+        tt(SB(CL), zn, SB(NTP), lt)
         tt(A("a3", 0, 32, key=0), zn, S(CG), add)
         tt(A("a3", 32, 64, key=1), zn, S(BF_), add)
         w = 64
         if OPT["rclone"] == "act":
-            tt(S(NG), S(NT), SB(NTN), add)
+            tt(S(NG), S(NT + t), SB(NTP), sub)
             tt(A("a3", 64, 96, key=2), zn, S(NG), add)
             w = 96
         tt(A("a3", 0, w), A("a3", 0, w), A("dum3", 0, w), mn)
@@ -674,20 +784,30 @@ def rank_program(g, core, T, topo):
         last = t == NSTEP - 1
         hop = HOP if not last else -HOP * t
         dst, src = T.cores[(rank + hop) % n_r], T.cores[(rank - hop) % n_r]
-        vn = A(of, 0, 32)
-        sv = send(A(of), "v%du" % (t + 1), dst, "av%d" % (t + 1), 1.8)
+        vn = A(of, 0, 32, key=0)
+        apart = last or (OPT["early"] and not OPT["prej"])
+        if apart:
+            send(vn, VU(t + 1), dst, src, "av%d" % (t + 1), 1.8)
         act(A("efg"), IN(A("EF"), vn), AF.Copy)
-        mm(A("B7"), ID(ONE), A(x), True)
-        mm(A("B7"), ID(NEG), A("efg"))
-        act(A("sg"), A("B7"), AF.Sign, C(BSG), -1.0)
+        if last or OPT["prej"]:
+            mm(A("B7"), ID(ONE), A(x), True)
+            mm(A("B7"), ID(NEG), A("efg"))
+            act(A("sg"), A("B7"), AF.Sign, 252.5, -1.0)
+        else:
+            next_j(t, "u", lambda a, s: A("efg", a, 512, s), "B7", "sg", A("B5", 288, 320))
+            cp(A(of, 32, 64, key=1), A("B5", 288, 320))
+        if not apart:
+            send(A(of), A("v%du" % (t + 1)), dst, src, "av%d" % (t + 1), 1.8)
+        elif not last:
+            send(A(of, 32, 64, key=1), JU(t + 1), dst, src, "aj%d" % (t + 1), 1.8)
         mm(A("B6"), ID(ONE), A(x), True)
         mm(A("B6"), ID(NEG), A("efg"))
         mm(A("B6"), ID(TWO), A("sg"))
         if last:
-            act(A("xo%d" % t), A("B6"), AF.Identity, C(B254), -1.0)
+            act(A("xo%d" % t), A("B6"), AF.Identity, 254.0, -1.0)
         else:
-            act(A("xo%d" % t), A("B6"), AF.Identity, C(B2))
-        sx = send(A("xo%d" % t), "x%db" % (t + 1), dst, "ax%d" % (t + 1), 2.3)
+            act(A("xo%d" % t), A("B6"), AF.Identity, 2.0)
+        sx = send(A("xo%d" % t), A("x%db" % (t + 1)), dst, src, "ax%d" % (t + 1), 2.3)
         su_t = A("SU", t, 4096, 8)
         mm(A("B1"), IH(2), A("sch"), True)
         w2f("B0", "wsel", SB(CL), True)
@@ -695,8 +815,14 @@ def rank_program(g, core, T, topo):
         w2f("B1", "wsel", SB(CL))
         tt(su_t, su_t, A("B1"), mx)
         tt(A("vm"), IN(A("ENC"), vn), A("mask%d" % (t % 2)), sub)
-        tt(A("pg"), IN(SUw, A("v%du" % t, 0, 32)), A("mask%d" % (t % 2)), mn)
-        tt(IN(A("SU"), A("ofp")), A("pg"), A("vm"), mx)
+        if OPT["vmode"] == "chain":
+            for h in (1, 0):
+                tt(A("pg", 256 * h, 256 * h + 256, key=h), IN(SUw, VU(t, 16 * h, 16 + 16 * h)), A("mask%d" % (t % 2), 256 * h, 256 * h + 256), mn)
+            for q in range(15, -1, -1):
+                tt(IN(A("SU"), A("ofv", 2 * q, 2 * q + 2)), A("pg", 32 * q, 32 * q + 32, key=q // 8), A("vm", 32 * q, 32 * q + 32), mx)
+        else:
+            tt(A("pg"), IN(SUw, VU(t)), A("mask%d" % (t % 2)), mn)
+            tt(IN(A("SU"), A("ofp")), A("pg"), A("vm"), mx)
         act(IN(A("R"), A("og", 0, 32)), A("val"), AF.Silu)
         if OPT["vw"] == "act":
             act(IN(A("VL"), A("og", 32, 64)), A("nv2"), AF.Silu)
@@ -712,12 +838,10 @@ def rank_program(g, core, T, topo):
             w2f("B2", "wsel", SB(CL))
             tt(r_t, r_t, A("B0"), sub)
             tt(r_t, r_t, A("B2"), mx)
-        arrive("v%du" % (t + 1), "av%d" % (t + 1), src, sv)
-        arrive("x%db" % (t + 1), "ax%d" % (t + 1), src, sx)
         if not last:
             seld(t + 1, False)
             for o in ops[-2:]:
-                o["after"].append(sx[0])
+                o["after"].append(sx)
             mm(A("B5", 320, 352), A("blk"), SB(CL), True)
             red(C(ACNT), A("B5", 320, 352))
             cp(A("coli", 2, 3, key=4), C(ACNT))
@@ -748,47 +872,44 @@ def rank_program(g, core, T, topo):
         words = OPT["head"][min(t, 1)] + " " + OPT["body"] + " " + OPT["tail"][t == NSTEP - 1]
         seq += [i for word in words.split() for i in named(t, word)]
     for a, b in zip(seq, seq[1:]):
-        ops[b]["after"].append(a)
-    for ch in range(32):
-        mm(A("B2", ch, 256, 32), A("SU", 128 * ch, 128 * ch + 128), A("oneswf", 16, 144, 16), True)
-    cp(A("nv1", 0, 256, key=0), A("B2", 0, 256))
-    ts(A("ei", 0, 256), A("B2", 0, 256), 1.0 / 256, mul, -0.25, add)
-    cp(A("nv1", 256, 512, key=1), A("ei", 0, 256))
+        ops[b]["soft"].append(a)
+    ops[seq[0]]["soft"] += [i for k, v in tags.items() if k[0] < 0 and k[1] in ("wg", "we", "x0b") for i in v]
     for h in range(2):
-        o = A("B3", 128 * h, 128 * h + 128)
-        mm(o, A("nv1", 128 * h, 128 * h + 128, key=0), IF(1), True)
-        mm(o, A("nv1", 256 + 128 * h, 384 + 128 * h, key=1), IF(2))
-        mm(o, A("nv1", 256 + 128 * h, 384 + 128 * h, key=1), IF(0))
-    ts(A("pg", 0, 256), A("B3", 0, 256), 65536.0, add)
+        sums, out = "B%d" % (4 + h), A("B%d" % (6 + h), 0, 128)
+        for ch in range(16):
+            mm(A(sums, ch, 128, 16), A("SU", 2048 * h + 128 * ch, 2048 * h + 128 * ch + 128), A("oneswf", 16, 144, 16), True)
+        join(16, 4)
+        part = lambda nm, j: A(nm, 256 * h + 128 * j, 256 * h + 128 * j + 128, key=2 * h + j)
+        ts(part("sci", 0), A(sums, 0, 128), 1.0 / 256, mul, -0.25, add)
+        act(part("keyl", 0), A(sums, 0, 128), AF.Copy)
+        cp(part("keyl", 1), part("sci", 0))
+        mm(out, part("keyl", 0), IF(1), True)
+        mm(out, part("keyl", 1), IF(2))
+        mm(out, part("keyl", 1), IF(0))
+        ts(A("pg", 128 * h, 128 * h + 128, key="s%d" % h), out, 65536.0, add)
     for q in range(4):
         if q < OPT["nact"]:
-            act(RQ(q), A("R", 1024 * q, 1024 * q + 1024), AF.Relu, C(B247))
+            act(RQ(q), A("R", 1024 * q, 1024 * q + 1024), AF.Relu, -247.0)
         else:
             ts(RQ(q), A("R", 1024 * q, 1024 * q + 1024), -247.0, add, 0.0, mx)
         ts(RQ(q), RQ(q), -1.0, mul, 9.0, add)
-    ts(A("sci"), A("VL", 0, 512), -64.0, add)
-    cp(A("verf"), A("sci"))
-    ts(SH(KEYV), A("v4u", 0, 32), -2048.0, add)
-    w2f("B4", "wselh", SH(KEYV), True, 8)
-    act(A("sel", p=r8), A("B4", p=r8), AF.Identity, C(B2048, r8))
-    dma("sp", H("yv"), A("sel", p=r8), "out", 2.0)
-    dma("sp", H("yx"), A("x4b"), "out", 2.5)
-    for m, q in enumerate((2, 0, 3, 1)):
-        dma("sp", (T["yr"][:, 1024 * q:1024 * q + 1024], [], []), RQ(q), "out", 5.2 - 0.8 * m)
-    dma("act", H("yl"), A("verf"), "out", 2.8)
+    if VOFF:
+        ts(A("ei", 0, 512), A("VL", 0, 512), -VOFF, add)
+        cp(A("verf"), A("ei", 0, 512))
+    ts(SH(KEYV), VU(NSTEP), -2048.0, add)
+    w2f("B3", "wselh", SH(KEYV), True, 8)
+    act(A("sel", p=r8), A("B3", p=r8), AF.Identity, 2048.0)
+    for m, q in enumerate(OPT["rout"]):
+        dma("sp", (T["yr"][:, 1024 * q:1024 * q + 1024], [], []), RQ(q), "out", 5.6 - 0.8 * m)
+    dma("act", H("yv"), A("sel", p=r8), "out", 2.0)
+    dma("act", H("yx"), A("x4b"), "out", 2.5)
+    dma("sp", H("yl"), A("verf") if VOFF else A("VL", 0, 512), "out", 2.8)
     for h in range(2):
-        dma("act", (T["ys"][4 * h:4 * h + 4, :], [], []), A("pg", 128 * h, 128 * h + 128), "out", 2.2)
+        dma("sp", (T["ys"][:, 2048 * h:2048 * h + 2048], [], []), A("pg", 128 * h, 128 * h + 128, key="s%d" % h), "out", 2.2)
 
     def hit(a, b):
         return a == b or a.split("#")[0] == b or b.split("#")[0] == a
 
-    opened = {}
-    for o in ops:
-        for k in o["rd"] + o["wr"]:
-            if k in opened and (o["e"] != "pe" or o["flag"][0]):
-                opened.pop(k)[1] = True
-        if o["e"] == "pe":
-            opened[o["wr"][0]] = o["flag"]
     lastw, readers, group = {}, {}, {}
     for i, o in enumerate(ops):
         if o["dma"]:

from concourse.mybir import AluOpType as ALU, AxisListType as AX, ActivationFunctionType as AF

SCRATCH = {}


def _decl(where, dtype, spec):
    for item in spec.split():
        name, cols = item.split(":")
        SCRATCH[name] = (where, [128, int(cols)], dtype)


_decl("psum", "float32", "B0:512 B1:512 B2:512 B3:512 B4:512 B5:512 B6:512 B7:512")
_decl("sbuf", "bfloat16", "EF:4096 G:8192 EQ:8192 MK:784 wide:576 bk:1024 idm:768 blk:128 wexp:256 we:24 wg:8 wsel:2048 seld:2048 "
      "x0r:512 x0b:512 x1b:512 x2b:512 x3b:512 x4b:512 xo0:512 xo1:512 xo2:512 xo3:512 mask0:512 mask1:512 gw:512 eqw:512 eqd:512 eqv:512 "
      "tcb:1024 tvf:512 yu:512 hu:512 hn:512 rc:512 eqc:512 z:512 efg:512 sg:512 eat:512 iob:128 cst:416 c2112:512 cneg:512 smb:192")
_decl("sbuf", "float32", "R:5120 SU:4608 VL:1024 TT:9248 ENC:4096 io:256 cv:1536 gk:128 ow2:144 oneswf:144 idf:384 lw:256 sc0:128 col:32 "
      "sm:640 ev:64 eD:64 d0:128 d1:128 vs:128 dum3:96 a3:96 sel:512 verf:512 scan:576 expd:256 val:512 vm:512 pg:512 "
      "nv1:512 nv2:512 keyl:512 tmpf:128")
_decl("sbuf", "int32", "smi:160 coli:32 ei:1024 sci:512")
_decl("sbuf", "uint16", "v0u:64 v1u:64 v2u:64 v3u:64 v4u:64 of0:64 of1:64 of2:64 of3:64 og:96 smu:128 veru:512 ofcb:128 ofv:64 ofp:32 exu:16")
_decl("sbuf", "float16", "dif:1024 idh:640 wselh:2048 key2:64 smh:96 w8:144 v0h:512 verh:512 sch:512")

DMASEMS = ["dx", "dv0", "de", "dver", "dr0", "dr1", "dr2", "dr3", "deff", "dsu", "dtt", "dtv", "out"]
SEMAPHORES = ["pe", "act", "dve", "pool", "sent"] + DMASEMS + ["ax%d" % t for t in range(1, 5)] + ["av%d" % t for t in range(1, 5)] + ["aj%d" % t for t in range(1, 4)]
NSTEP, HOP = 4, 3
D1, FAR = 262144.0, 524288.0
GUESS = ((0.00087, 1.56, 3.8, 0.00046, 0.12, 150), (0.00095, 1.15, 2.0, 0.00052, 0.15, 150), (0.00105, 1.95, 5.2, 0.00055, 0.08, 200),
         (0.00093, 1.4, 3.0, 0.00052, 0.13, 160))
ORDER = {}
OPT = {"swaps": 1500, "heat": 0.0, "by": (0, 3), "rounds": 3, "tries": 2, "noise": 0.4, "gain": 2.0, "slip": 0.0, "parts": ((3, 2), (1,), (0,)),
       "gp": ((64, 64), (32, 96), (128,), (128,)), "gdve": 1, "ep": (1, 1, 1, 1), "expd": "dve", "tb": "dve", "gw": "dve", "rc": "dve",
       "vw": "dve", "vl": "dve", "val": "act", "rclone": "act", "nact": 3, "tv": "act", "yu": "dve", "vmode": "table", "prej": 0, "fill": 0, "early": 1, "rout": (0, 3, 1, 2),
       "head": ("G.0-4 TV.0-3 TT.0-7~TV.4-7", "G.0-4 TT.0-7~TV.0-7"),
       "body": "TT.8-31~TV.8-31 tcb val tvf",
       "tail": ("efg sg R.0 xo +mask R.1", "R.0 efg R.1 sg xo")}


def schedule(ops):
    n = len(ops)
    pred = [[] for _ in range(n)]
    succ = [[] for _ in range(n)]
    for k, o in enumerate(ops):
        for i in o["all"]:
            p = ops[i]
            sync = i in o["need"] and not (p["e"] == "pe" and o["e"] == "pe")
            pred[k].append((i, p["lat"] if sync else 0.0, sync))
            succ[i].append((k, p["lat"] if sync else 0.0, sync))
    hard = [list(p) for p in pred]
    for k, o in enumerate(ops):
        for i in o["soft"]:
            pred[k].append((i, 0.0, False))
            succ[i].append((k, 0.0, False))
    costs = [[c[0] + cy * (c[1] + ga * c[2] + sc * c[3]) + pe * c[4] for c in (o["cost"] for o in ops)] for cy, ga, sc, pe, _, _ in GUESS]
    eng = [o["e"] for o in ops]
    lat = [o["lat"] for o in ops]

    def run(before, after, prio, back, m=0):
        cost, wake = costs[m], GUESS[m][4]
        left = [len(p) for p in before]
        rel = list(lat) if back else [0.0] * n
        ready, free, end, seq = {}, {}, [0.0] * n, []
        todo = [i for i in range(n) if not left[i]]

        def done(i):
            seq.append(i)
            for k, gp, sync in after[i]:
                rel[k] = max(rel[k], end[i] + gp + (wake if sync else 0.0))
                left[k] -= 1
                if not left[k]:
                    todo.append(k)

        while True:
            while todo:
                i = todo.pop()
                if eng[i] is None:
                    end[i] = rel[i]
                    done(i)
                else:
                    ready.setdefault(eng[i], []).append(i)
            first = None
            for e, lst in ready.items():
                if lst:
                    t = max(free.get(e, 0.0), min(rel[i] for i in lst))
                    if first is None or t < first[0]:
                        first = (t, e)
            if first is None:
                return seq, end
            t, e = first
            lst = ready[e]
            i = max((i for i in lst if rel[i] <= t + 1e-9), key=lambda m: prio[m])
            wait = [m for m in lst if t < rel[m] < t + cost[i] and prio[m] > prio[i]
                    and max(prio[m], cost[m] + prio[i]) + OPT["gain"] * (rel[m] - t) < cost[i] + prio[m]]
            if wait:
                m = min(wait, key=lambda m: rel[m])
                fit = [j for j in lst if max(rel[j], t) + cost[j] <= rel[m] + OPT["slip"]]
                i = max(fit, key=lambda j: prio[j]) if fit else m
            lst.remove(i)
            end[i] = max(t, rel[i]) + cost[i]
            free[e] = end[i]
            done(i)

    def span(seq, m):
        cost, wake, end, free = costs[m], GUESS[m][4], [0.0] * n, {}
        for i in seq:
            t = free.get(eng[i], 0.0)
            for j, gp, sync in pred[i]:
                t = max(t, end[j] + gp + (wake if sync else 0.0))
            end[i] = t + cost[i]
            if eng[i] is not None:
                free[eng[i]] = end[i]
        return max(end[i] + lat[i] for i in range(n))

    seq, _ = run(pred, succ, [0.0] * n, False)
    assert len(seq) == n
    base = [0.0] * n
    for i in reversed(seq):
        base[i] = costs[0][i] + max([base[k] + gp + (GUESS[0][4] if sync else 0.0) for k, gp, sync in succ[i]] + [lat[i]])
    load = [bool(o["dma"]) and not o["rd"] and not o["ext"] for o in ops]
    best, z, keep = None, 12345, base
    for tr in range(OPT["tries"]):
        prio = []
        for i in range(n):
            z = (z * 1103515245 + 12345) % 2147483648
            prio.append(keep[i] + (OPT["noise"] * z / 2147483648 if tr else 0.0))
        for r in range(OPT["rounds"]):
            prio = [1.0e6 - i if load[i] else prio[i] for i in range(n)]
            by = OPT["by"][tr % len(OPT["by"])]
            seq, end = run(pred, succ, prio, False, by)
            spans = [span(seq, m) for m in range(len(GUESS))]
            score = sum(s / GUESS[m][5] for m, s in enumerate(spans))
            if best is None or score < best[0]:
                best, keep = (score, seq, spans), prio
            prio = run(succ, pred, end, True, by)[1]
    seq = list(best[1])
    gaps = [[[(j, gp + (gs[4] if sync else 0.0)) for j, gp, sync in hard[i]] for i in range(n)] for gs in GUESS]
    names = [set(j for j, _, _ in hard[i]) for i in range(n)]

    def timed(seq, m, a, old):
        cost, gap, end, why, last = costs[m], gaps[m], list(old[0]), list(old[1]), {}
        for i in reversed(seq[max(0, a - 400):a]):
            last.setdefault(eng[i], i)
        for i in seq[a:]:
            e = eng[i]
            w = last.get(e) if e else None
            t = end[w] if w is not None else 0.0
            for j, gp in gap[i]:
                if end[j] + gp > t:
                    t, w = end[j] + gp, j
            end[i], why[i], last[e] = t + cost[i], w, i
        return end, why

    def worth(states):
        spans = [max(end[i] + lat[i] for i in tail) for end, _ in states]
        return sum(s / GUESS[m][5] for m, s in enumerate(spans)), spans

    tail = [i for i in range(n) if not succ[i]]
    states = [timed(seq, m, 0, ([0.0] * n, [None] * n)) for m in range(len(GUESS))]
    now = top = worth(states)
    keep = list(seq)
    for it in range(OPT["swaps"]):
        z = (z * 1103515245 + 12345) % 2147483648
        end, why = states[(z >> 8) % len(GUESS)]
        i, pairs = max(tail, key=lambda q: end[q] + lat[q]), []
        while why[i] is not None:
            if eng[why[i]] == eng[i] and why[i] not in names[i] and not load[i]:
                pairs.append((why[i], i))
            i = why[i]
        z = (z * 1103515245 + 12345) % 2147483648
        x, y = pairs[(z >> 8) % len(pairs)]
        a, b = seq.index(x), seq.index(y)
        late, seen = {x}, set()
        for q in seq[a + 1:b]:
            if eng[q] in seen or not names[q].isdisjoint(late):
                late.add(q)
                if eng[q]:
                    seen.add(eng[q])
        if not names[y].isdisjoint(late):
            continue
        trial = seq[:a] + [q for q in seq[a:b] if q not in late] + [y] + [q for q in seq[a:b] if q in late] + seq[b + 1:]
        tried = [timed(trial, m, a, states[m]) for m in range(len(GUESS))]
        new = worth(tried)
        if new[0] <= now[0] + OPT["heat"] * (1.0 - it / OPT["swaps"]):
            seq, states, now = trial, tried, new
            if now[0] < top[0]:
                top, keep = now, list(seq)
    ORDER["span"] = [round(s, 1) for s in best[2]] + [round(s, 1) for s in top[1]]
    return keep


def rank_program(g, core, T, topo):
    rank = T.rank_of(core)
    if rank is None:
        return
    n_r = len(T.cores)
    ops, tags, step, opened = [], {}, [-1], {}
    Q = {"pe": g.tensor, "act": g.scalar, "dve": g.vector, "pool": g, "sp": g.sync}

    def A(name, a=None, b=None, s=None, key=None, p=None):
        keys = [name] if key is None else [name + "#" + str(k) for k in (key if isinstance(key, list) else [key])]
        n = len(range(SCRATCH[name][1][1])[slice(a, b, s)])
        return (T[name][slice(None) if p is None else p, slice(a, b, s)], keys, [], n, name, False)

    def IN(win, off):
        return (win[0].indirect(off[0]), win[1], off[1], 16 * off[3], win[4], True)

    def op(e, fn, outs, ins, cost, dma=None, ext=None, lat=0.0, after=()):
        rd, wr = [], []
        for o in outs:
            wr += o[1]
            rd += o[2]
        for i in ins:
            if isinstance(i, tuple):
                rd += i[1] + i[2]
        for k in rd + wr:
            if k in opened and e != "pe":
                opened.pop(k)[1] = True
        ops.append({"soft": [], "e": e, "fn": fn, "rd": rd, "wr": wr, "dma": dma, "ext": ext, "inc": False, "cost": cost, "lat": lat, "after": list(after), "n": 16})

    def est(o, ins, two=False, fast=True, fix=0.0):
        n = max(o[3], ins[0][3]) if ins else o[3]
        if o[5]:
            return (fix + 0.05, 0, 0, n, 0)
        if ins and ins[0][5]:
            return (fix + 0.05, 0, n, 0, 0)
        r = 2 if two else 0.5 if fast and all(SCRATCH[x[4]][2].endswith("16") for x in [o] + ins) else 1
        return (fix + 0.012, max(64, n * r), 0, 0, 0)

    def u(x):
        return x[0] if isinstance(x, tuple) else x

    def cp(o, i):
        op("dve", lambda: g.vector.tensor_copy(o[0], i[0]), [o], [i], est(o, [i]))

    def tt(o, a, b, alu):
        two = SCRATCH[a[4]][0] == SCRATCH[b[4]][0]
        op("dve", lambda: g.vector.tensor_tensor(o[0], a[0], b[0], alu), [o], [a, b], est(o, [a, b], two, False))

    def ts(o, a, s1, op0, s2=None, op1=None):
        if op1 is None:
            op("dve", lambda: g.vector.tensor_scalar(o[0], a[0], u(s1), None, op0), [o], [a, s1], est(o, [a]))
        else:
            op("dve", lambda: g.vector.tensor_scalar(o[0], a[0], u(s1), u(s2), op0, op1), [o], [a, s1, s2], est(o, [a]))

    def ms(o, c):
        op("dve", lambda: g.vector.memset(o[0], c), [o], [], est(o, []))

    def scan(o, a, b, init, op0, op1):
        op("dve", lambda: g.vector.tensor_tensor_scan(o[0], a[0], b[0], init, op0, op1), [o], [a, b], est(o, [a]))

    def red(o, a):
        op("dve", lambda: g.vector.tensor_reduce(o[0], a[0], AX.X, ALU.add), [o], [a], est(o, [a]))

    def act(o, i, f, bias=None, scale=None):
        kw = {}
        if bias is not None:
            kw["bias"] = u(bias)
        if scale is not None:
            kw["scale"] = scale
        op("act", lambda: g.scalar.activation(o[0], i[0], f, **kw), [o], [i, bias], est(o, [i], fast=False, fix=0.015))
        tags.setdefault((step[0], o[4].rstrip("0123")), []).append(len(ops) - 1)

    def copy(e, o, i):
        if e == "act":
            act(o, i, AF.Copy)
        else:
            cp(o, i)

    def mm(o, l, r, start=False):
        c = max(min(64, l[3]), r[3]) * (4 if SCRATCH[l[4]][2] == "float32" else 1)
        flag = [start, False]
        if start and o[4] in opened:
            opened.pop(o[4])[1] = True
        op("pe", lambda: g.tensor.matmul(o[0], l[0], r[0], flag[0], flag[1]), [o], [l, r], (0.0, 0, 0, 0, c))
        opened[o[4]] = flag

    def join(k, by=8):
        run = ops[-k:]
        del ops[-k:]
        for a in range(0, k, by):
            part = run[a:a + by]
            o = dict(part[0], fn=lambda part=part: [q["fn"]() for q in part][-1], cost=(0.0, 0, 0, 0, sum(q["cost"][4] for q in part)))
            for side in ("rd", "wr"):
                o[side] = sorted(set(x for q in part for x in q[side]))
            ops.append(o)

    pool_tail = []

    def pool(fn, outs, ins, cost, chain):
        op("pool", fn, outs, ins, cost, after=pool_tail[-1:] if chain else ())
        if chain:
            pool_tail.append(len(ops) - 1)

    def iota(o, pat, base=0, cm=0, flt=True, chain=True):
        c = (0.13, 2 * o[3], 0, 0, 0)
        if flt:
            pool(lambda: g.iota(o[0], pat, base, cm, allow_small_or_imprecise_dtypes=True), [o], [], c, chain)
        else:
            pool(lambda: g.iota(o[0], pat, base, cm), [o], [], c, chain)

    def asel(o, i, pat, cmp, fill, base, cm, chain=True):
        pool(lambda: g.affine_select(o[0], i[0], pat, cmp, fill, base, cm), [o], [i], (0.17, 2 * o[3], 0, 0, 0), chain)

    queue_tail = {}

    def dma(e, o, i, sem, lat=3.0):
        op(e, lambda: Q[e].dma_start(o[0], i[0]), [o], [i], (0.1, 0, 0, 0, 0), dma=sem, lat=lat, after=queue_tail.get(e, ()))
        queue_tail[e] = (len(ops) - 1,)

    def send(what, where, dst, src, sem, lat):
        rid, pid, _ = topo.addr(dst)
        m = topo.mask(core, dst)
        op("pool", lambda: g.remote_dma(where[0], what[0], T.sem[sem], T.sem["sent"], pid, rid, m), [], [what], (0.5, 0, 0, 0, 0), ext="send")
        ops[-1]["n"] = len(topo.engines(core, dst))
        op(None, None, [where], [], (0.0, 0, 0, 0, 0), dma=sem, ext="arr", lat=lat, after=(len(ops) - 1,))
        ops[-1]["n"] = len(topo.engines(src, core))
        return len(ops) - 2

    def f2w(o, wide, src, first=True, p=None):
        for p0 in range(16):
            mm(o, wide(16 - p0, 144 - p0), A(src[0], src[1] + p0, src[1] + 512, 16, key=src[2], p=p), first and p0 == 0)
        join(16)

    def w2f(bank, sel, src, first=False, cols=128):
        for p0 in range(16):
            mm(A(bank, p0, 512, 16, p=slice(0, 8) if cols == 8 else None), A(sel, 128 * p0, 128 * p0 + 128, 128 // cols), src, first and p0 == 0)
        join(16)

    H = lambda name: (T[name][:], [], [])
    VU = lambda t, a=0, b=32: A("v%du" % t, a, b, key="v")
    JU = lambda t: A("v%du" % t, 32, 64, key="j")
    C = lambda j, p=None: A("col", j, j + 1, key=j, p=p)
    PARTKEYS = ["p%d" % q for q in range(4)]
    S = lambda j: A("sm", 32 * j, 32 * j + 32, key=j)
    SI = lambda j: A("smi", 32 * j, 32 * j + 32, key=j)
    SB = lambda j: A("smb", 32 * j, 32 * j + 32, key=j)
    SH = lambda j: A("smh", 32 * j, 32 * j + 32, key=j)
    SUU = lambda j: A("smu", 32 * j, 32 * j + 32, key=j)
    TM = lambda j: A("tmpf", 8 * j, 8 * j + 8, key=j)
    ID = lambda j: A("idm", 128 * j, 128 * j + 128, key=j)
    IH = lambda j: A("idh", 128 * j, 128 * j + 128, key=j)
    IF = lambda j: A("idf", 128 * j, 128 * j + 128, key=j)
    WD = lambda j: (lambda a, b: A("wide", 144 * j + a, 144 * j + b, key=j))
    CS = lambda j: A("cst", 32 * j, 32 * j + 32, key=[j] + ["%d_%d" % (j, ch) for ch in range(4)])
    RQ = lambda q: A("EQ", 1024 * q, 1024 * q + 1024, key="r%d" % q)
    eq, ne, ge, lt = ALU.is_equal, ALU.not_equal, ALU.is_ge, ALU.is_lt
    add, sub, mul, mx, mn, band, shr = ALU.add, ALU.subtract, ALU.mult, ALU.max, ALU.min, ALU.bitwise_and, ALU.arith_shift_right
    PART, P16, G16, G16P, TWOF, LIM, PLO, PHI, T1, T2, T3, ACNT, MLO, MHI, T4, DC, DB, DV, DV2 = range(19)
    NK = 3 if OPT["vmode"] == "merged" else 2
    TB = 0 if NK == 3 else 4608
    LANE, DUMR, BF_, THR, CAND, MNV, NC, CG, LQ, NG, JN, JD, NT = range(13)
    ONE, NEG, TWO, K4, N8K, K256 = range(6)
    ONESW, JW, JW2, ONESN = range(4)
    CK, CW, LIFT, LIFTV, CZ, OWN, OWNH = 0, 1, 2, 3, 4, 5, 12
    CE, CKEY = A("cst", 192, 256, key="e"), A("cst", 256, 384, key="k")
    NTG, NTN, CL, SW, NTP = range(5)
    KEYV, TGT, JUH = range(3)
    io = lambda n: A("io", 0, n)
    r8 = slice(0, 8)

    dma("sp", A("x0r"), H("x0"), "dx", 2.5)
    dma("act", A("sci", p=r8), H("v0"), "dv0", 2.5)
    for q in range(4):
        dma("sp", RQ(q), (T["rec0"][:, 1024 * q:1024 * q + 1024], [], []), "dr%d" % q, 3.5 + q)
        if q == 0:
            dma("act", A("ei", 0, 512, key=[0, 1]), H("edge0"), "de")
            dma("act", A("ei", 512, 1024, key=[2, 3]), H("ver0"), "dver", 3.5)
    for q in range(4):
        dma("sp", A("EF", 1024 * q, 1024 * q + 1024, key=q), H("eff"), "deff", 10.0)
    iota(A("coli", 0, 1, key=0), [[0, 1]], 0, 1, flt=False)
    iota(C(PART), [[0, 1]], 0, 1)
    iota(io(144), [[1, 144]])
    iota(C(T1), [[0, 1]], 16, 16)
    iota(A("iob"), [[1, 128]])
    iota(A("MK"), [[0, 49], [1, 16]])
    iota(CE, [[0, 64]], -15 * int(D1))
    iota(S(LANE), [[16, 32]])
    iota(A("gk"), [[16, 8], [0, 16]])
    iota(CS(CW), [[0, 32]], -4096)
    iota(TM(5), [[0, 8]], 4)
    iota(TM(6), [[0, 8]], 1)
    iota(A("R", 4096, 4608, key=8), [[0, 512]], 200)
    iota(CS(CK), [[0, 32]], 256000)
    iota(CS(LIFT), [[0, 16], [2048, 2]], 6656 - TB)
    iota(A("tmpf", 0, 16, key=[0, 1]), [[0, 2], [16, 4], [64, 2]], 15)
    iota(A("tmpf", 16, 24, key=2), [[0, 2], [16, 4]], 15)
    iota(A("lw"), [[0, 4], [1, 64]], -48)
    for ch in range(4):
        iota(A("cv", 384 * ch, 384 * ch + 384, key=ch), [[16 << ch, 8], [0, 3], [1 << ch, 16]], 128 << ch)
    iota(CS(LIFTV), [[0, 32]], 2048)
    iota(CS(CZ), [[0, 32]], 20480)
    iota(S(LQ), [[0, 4], [16, 8]], 128)
    iota(C(LIM), [[0, 1]], 3 * int(D1))
    iota(A("d0"), [[0, 128]])
    iota(A("TT", 0, 4096, key="v"), [[0, 4096]])
    asel(A("wsel"), A("TT", 0, 2048, key="v"), [[-1, 16], [-16, 8], [0, 16]], ne, FAR, 0, 1)

    def seld(t, chain):
        pat = [[-1001, 16], [-16, 8], [1000, 16]]
        asel(A("seld"), A("wsel"), pat, ne, 0.0, -1000 * t, 1, chain)
        if t:
            asel(A("seld"), A("seld"), pat, ne, 0.0, 1000 * (16 - t), 1, chain)

    seld(0, True)
    if OPT["vw"] == "act":
        iota(A("c2112"), [[0, 512]], 2112)
    for h in range(2):
        iota(A("ENC", 2048 * h, 2048 * h + 2048, key=h), [[-1, 4], [256, 512]], 8 - 4 * h)
    if OPT["rclone"] != "act":
        iota(A("cneg"), [[0, 512]], -int(FAR))

    lin = lambda o, i, scale, bias: act(o, i, AF.Identity, bias, scale)
    ts(A("coli", 1, 2, key=1), A("coli", 0, 1, key=0), 15, band)
    cp(C(P16), A("coli", 1, 2, key=1))
    tt(C(G16), C(PART), C(P16), sub)
    ts(C(G16P), C(G16), 16.0, add)
    ts(C(TWOF), C(P16), 2.0, mul, 1.0, add)
    ts(C(T3), C(G16), 24.0, add)
    ts(C(MLO), C(P16), 8.0, lt, -8388608.0, mul)
    ts(C(MHI), C(P16), 8.0, ge)
    ts(ID(ONE), A("iob"), C(PART), eq)
    for j, c in ((NEG, -1.0), (TWO, 2.0), (K4, 4096.0), (N8K, -8192.0), (K256, 256.0)):
        act(ID(j), ID(ONE), AF.Silu if j == K4 else AF.Copy, None, c)
    for j, c in ((0, 1.0), (1, -512.0), (2, 131072.0)):
        act(IF(j), ID(ONE), AF.Copy, None, c)
    for j, c in ((0, 1.0), (1, 2.0 ** -14), (2, 256.0), (3, -16.0), (4, -1.0)):
        ts(IH(j), ID(ONE), c, mul)
    ts(WD(JW)(0, 144), io(144), C(G16P), eq, C(TWOF), mul)
    act(WD(JW2)(0, 144), WD(JW)(0, 144), AF.Copy, None, -2.0)
    ts(A("w8"), io(144), C(T1), eq)
    ts(A("oneswf"), io(144), C(G16P), eq)
    ts(A("ow2"), io(144), C(T3), eq)
    tt(A("ow2"), A("ow2"), A("oneswf"), add)
    act(WD(ONESW)(0, 144), A("oneswf"), AF.Copy, None, 2.0)
    act(WD(ONESN)(0, 144), A("oneswf"), AF.Copy, None, -512.0)
    ts(A("MK"), A("MK"), C(P16), ne, D1, mul)
    ts(A("cst", 193, 256, 2, key="e"), A("cst", 193, 256, 2, key="e"), C(MLO), add)
    ms(A("eD"), -16777216.0)
    ts(A("eD", 1, 64, 2), A("eD", 1, 64, 2), C(MHI), mul)
    for j, c in ((DC, 9216.0 - TB), (DB, 9232.0 - TB), (DV, 4096.0), (DV2, 4112.0)):
        lin(C(j), C(P16), 1.0, c)
    lin(A("x0b"), A("x0r"), -1.0, 256.0)
    ts(A("v0h", p=r8), A("sci", p=r8), -2048.0, add)
    f2w(A("B6", 0, 32), lambda a, b: A("w8", a, b, p=r8), ("v0h", 0, None), p=r8)
    ts(SI(0), A("B6", 0, 32), 2048.0, add)
    cp(VU(0), SI(0))
    ts(SI(1), SI(0), 511, band)
    cp(SUU(3), SI(1))
    f2w(A("B5", 0, 32), WD(JW), ("x0r", 0, None))
    cp(JU(0), A("B5", 0, 32))
    ts(A("sci"), A("ei", 0, 512, key=[0, 1]), 9, shr)
    ts(A("B7"), A("sci"), -131073.0, mul, 8.0, add)
    ts(A("nv1"), A("ei", 0, 512, key=[0, 1]), 256.0, mul)
    tt(A("SU", 0, 512, key=0), A("nv1"), A("B7"), add)
    VOFF = 64.0 if OPT["vw"] == "act" else 0.0
    ts(A("VL", 0, 512), A("ei", 512, 1024, key=[2, 3]), VOFF, add)
    for q in range(8):
        gq = A("G", 512 * q, 512 * q + 512, key="r%d" % q)
        rq = A("EQ", 512 * q, 512 * q + 512, key="r%d" % (q // 2))
        ts(gq, rq, 5.0, ge, -247.0, mul)
        mm(A("B%d" % (q % 4)), ID(NEG), rq, True)
        mm(A("B%d" % (q % 4)), ID(ONE), gq)
        act(A("R", 512 * q, 512 * q + 512, key=q), A("B%d" % (q % 4)), AF.Identity, 256.0)
    scan(TM(7), TM(5), TM(6), 0.25, mul, mul)
    for j, sh, a in ((PLO, 0.0, 8), (PHI, 8.0, 12)):
        ts(TM(a), io(8), sh, add, C(P16), eq)
        tt(TM(a + 1), TM(a), TM(7), mul)
        red(C(j), TM(a + 1))
    ts(A("wexp", 0, 128), A("gk", 0, 128), C(G16), eq, C(PLO), mul)
    ts(A("wexp", 128, 256), A("gk", 0, 128), C(G16), eq, C(PHI), mul)
    ts(A("blk"), A("gk", 0, 128), C(G16), eq)
    act(A("wg"), A("blk", 0, 128, 16), AF.Copy)
    act(A("we", 0, 8, key=0), A("blk", 0, 128, 16), AF.Copy, None, -256.0)
    act(A("we", 8, 24, key=1), A("wexp", 0, 256, 16), AF.Copy, None, -1.0)
    lin(S(LANE), S(LANE), 1.0, C(P16))
    lin(S(DUMR), S(LANE), 1.0, 4096.0)
    for q, c in enumerate((4608.0, 512.0, 4608.0)):
        lin(A("dum3", 32 * q, 32 * q + 32, key=q), S(LANE), 1.0, c)
    for t in range(NSTEP):
        lin(S(NT + t), S(LANE), 8.0, 8192.0 + t)
    lin(S(LQ), S(LQ), 1.0, C(P16))
    for ch in range(4):
        for j, c in ((OWN, 4), (OWNH, 2)):
            act(A("cst", 32 * j + 8 * ch, 32 * j + 8 * ch + 8, key="%d_%d" % (j, ch)), A("sm", 32 * LQ + 8 * ch, 32 * LQ + 8 * ch + 8, key=LQ), AF.Copy, None, float(c << ch))
    mm(A("B7", 0, 128), ID(ONE), ID(ONE), True)
    c2, c3 = A("coli", 8, 16, key=2), A("coli", 16, 24, key=3)
    ts(c2, io(8), -1.0, mul, C(P16), add)
    ts(c2, c2, 15.0, add)
    ts(c2, c2, 15, band)
    ts(TM(10), c2, C(G16), add)
    ts(c3, io(8), 1.0, add, C(P16), add)
    ts(c3, c3, 15, band)
    ts(TM(11), c3, C(P16), mx, C(G16), add)
    for d in range(8):
        ts(A("z", 128 * (d % 4), 128 * (d % 4) + 128, key=d % 4), A("iob"), A("tmpf", 80 + d, 81 + d, key=10), eq)
        tt(A("dif", 128 * d, 128 * d + 128, key=d), A("z", 128 * (d % 4), 128 * (d % 4) + 128, key=d % 4), A("B7", 0, 128), sub)
        ts(A("bk", 128 * d, 128 * d + 128, key=d), A("iob"), A("tmpf", 88 + d, 89 + d, key=11), eq, 8192.0, mul)
    for h in range(4):
        ts(A("wselh", 512 * h, 512 * h + 512, key=h), A("wsel", 512 * h, 512 * h + 512), 1.0 / FAR, mul)
    ms(A("sc0"), -1.0 / 16)
    ms(A("sc0", 0, 128, 16), 1.0e6)
    for ch in range(4):
        iota(A("scan", 144 * ch + 128, 144 * ch + 144, key=ch), [[0, 16]], 0, chain=False)
    ts(A("lw"), A("lw"), C(P16), eq, D1, mul)
    ts(A("coli", 24, 25, key=6), A("coli", 0, 1, key=0), 7, band)
    ts(A("coli", 25, 26, key=7), A("coli", 0, 1, key=0), 4, shr)
    tt(C(T4), A("coli", 24, 25, key=6), A("coli", 25, 26, key=7), eq)
    ts(C(T2), C(MHI), 64.0, mul, -128.0, add)
    ts(A("tmpf", 24, 28, key=3), A("tmpf", 16, 20, key=2), C(T2), add, C(T4), mul)
    ts(A("exu", 0, 4), A("tmpf", 24, 28, key=3), 128.0, add)
    ts(C(T2), C(MHI), 144.0, mul, -128.0, add)
    ts(TM(3), TM(0), C(T2), add, C(T4), mul)
    ts(A("exu", 4, 12), TM(3), 128.0, add)
    for q in range(9, 18):
        dma("sp", A("TT", 512 * q, 512 * q + 512, key="cb"), A("VL", 0, 512), "dtt", 12.0)
    for q in range(1, 8):
        dma("sp", A("SU", 512 * q, 512 * q + 512, key=q), A("SU", 0, 512, key=0), "dsu", 16.0)

    Rw, SUw = A("R", 0, 4096), A("SU", 0, 4096)
    E = A("ev", 1, 64, 2)

    def edge(t):
        mask = A("mask%d" % (t % 2))
        act(mask, IN(A("MK"), JU(t)), AF.Copy)
        if t == 0:
            tt(A("sel"), IN(A("SU", 0, 512, key=0), SUU(3)), mask, mx)
        else:
            tt(A("sel"), IN(SUw, VU(t)), mask, mx)
        mm(A("B5", 32, 96), ID(ONE), CE, True)
        for p0 in range(8):
            mm(A("B5", 32, 96), A("ow2", 16 - p0, 144 - p0), A("sel", p0, 512, 8))
        join(8, 2)
        scan(A("ev"), A("eD"), A("B5", 32, 96), 0.0, add, mx)
        ts(SUU(0), E, 1.0 / 256, mul, 0.25, add)
        for a, b in ((3, 4), (0, 3)):
            ver, keys = IN(A("VL", 0, 512), A("smu", 8 * a, 8 * b, key=0)), list(range(a, b))
            if OPT["vl"] == "act":
                act(A("verf", 128 * a, 128 * b, key=keys), ver, AF.Copy)
                ver = A("verf", 128 * a, 128 * b, key=keys)
            ts(A("veru", 128 * a, 128 * b, key=keys), ver, 0.25 - VOFF, add)
        ts(SI(2), E, 1.0 / 256, mul, 10240.0, add)
        ts(S(BF_), SI(2), -10240.0, add)
        mm(A("B5", 96, 128), ID(ONE), CS(CW), True)
        mm(A("B5", 96, 128), IF(1), E)
        mm(A("B5", 96, 128), IF(2), S(BF_))
        mm(A("B5", 96, 128), IF(0), S(BF_))
        ts(SUU(1), A("B5", 96, 128), 8192.25, add)

    def main(t):
        x = "x%db" % t
        last = t == NSTEP - 1
        first_v(t)
        mm(A("B4"), ID(ONE), A(x), True)
        if not last:
            ts(SH(JUH), JU(t), -512.0, add)
        if not last and OPT["prej"]:
            next_j(t, "n", lambda a, s: A("EF", t + 8 * a, 4096, 8 * s), "B1", "hn", A("B0", 0, 32))
            cp(S(JN), A("B0", 0, 32))
        gkey = lambda ch, a, b: ["%d_%d" % (ch, m) for m in range(a // 16, b // 16)]
        old = ["r%d" % q for q in range(8)] if t == 0 else []
        for ch in (3, 2, 1, 0):
            b = 128
            for m, ln in enumerate(OPT["gp"][3 - ch]):
                copy("dve" if ch == 2 and m < OPT["gdve"] else "act", A("G", 2048 * ch + 16 * (b - ln), 2048 * ch + 16 * b, key=gkey(ch, b - ln, b) + (old if ch < 2 else [])),
                     IN(Rw, A("veru", 128 * ch + b - ln, 128 * ch + b, key=ch)))
                b -= ln
        for a, b in ((3, 4), (0, 3)):
            ts(A("verh", 128 * a, 128 * b, key=list(range(a, b))), A("veru", 128 * a, 128 * b, key=list(range(a, b))), -2048.0, add, 1.0 / 16, mul)
        if OPT["vl"] == "dve":
            ts(A("verf"), A("veru"), VOFF, add)
        copy(OPT["gw"], A("gw"), IN(A("R", 0, 4608), SUU(1)))
        tt(A("eqw"), A("gw"), A("B4"), eq)
        f2w(A("B7", 0, 32), WD(ONESW), ("gw", 0, None))
        f2w(A("B7", 0, 32), WD(ONESN), ("eqw", 0, None), False)
        ts(S(THR), A("B7", 0, 32), 256.0, ge, 8388608.0, mul)
        tt(S(CAND), S(THR), A("B5", 96, 128), add)
        for ch in (3, 2, 1, 0):
            bank = "B%d" % ch
            olde = ["r%d" % (2 * ch), "r%d" % (2 * ch + 1)] if ch < 2 and t in (0, NSTEP - 1) else []
            ne_ = OPT["ep"][3 - ch]
            pieces = [(128 * m // ne_, 128 * (m + 1) // ne_) for m in range(ne_)]
            eqk = lambda k: A("EQ", 2048 * ch + 128 * k, 2048 * ch + 128 * k + 128, key=["%d_%d_%d" % (ch, k, a) for a, _ in pieces] + (olde if last else []))
            for k in range(16):
                base = 2048 * ch + 128 * k
                for a, b in reversed(pieces):
                    tt(A("EQ", base + a, base + b, key=["%d_%d_%d" % (ch, k, a)] + ([olde[k // 8]] if olde and t == 0 and k % 8 == 0 else [])),
                       A("G", 2048 * ch + 16 * a + k, 2048 * ch + 16 * b, 16, key=gkey(ch, a, b)), A("B4", 128 * ch + a, 128 * ch + b), eq)
                mm(A(bank, k, 128, 16), A("G", 2048 * ch + k, 2048 * ch + 2048, 16, key=gkey(ch, 0, 128)), A("wg"), k == 0)
                if k == 1:
                    mm(A(bank, 128, 256), A("verh", 128 * ch, 128 * ch + 128, key=ch), IH(1))
                mm(A(bank, k, 128, 16), eqk(k), A("we", 0, 8))
            sl = lambda nm: A(nm, 128 * ch, 128 * ch + 128, key=ch)
            ts(sl("sci"), A(bank, 0, 128), 1.0 / 256, mul, 0.09, add)
            tt(sl("keyl"), sl("sci"), A(bank, 128, 256), add)
            scan(A("scan", 144 * ch, 144 * ch + 128, key=ch), A("sc0"), sl("keyl"), 0.0, add, mn)
            for k in range(16):
                mm(A(bank, 128 + k, 384, 16), eqk(k), A("we", 8, 24), k == 0)
            join(16, 4)

    def first_v(t):
        ts(SH(KEYV), VU(t), -2048.0, add)
        for d in range(8):
            mm(A("B4", 32 * d, 32 * d + 32), A("dif", 128 * d, 128 * d + 128, key=d), SH(KEYV), True)
        join(8)
        chain = OPT["vmode"] == "chain"
        if chain:
            for p0 in range(16):
                mm(A("B4", 256 + p0, 512, 16), A("wselh", 128 * p0, 128 * p0 + 128), A("smh", 0, 32, 2, key=KEYV), True)
                mm(A("B4", 256 + p0, 512, 16), IH(4), A("smh", 1, 32, 2, key=KEYV))
        ts(A("eqv", 0, 512 if chain else 256), A("B4", 0, 512 if chain else 256), 0.0, eq, 2.0, mul)
        mm(A("B4", 256, 288), IH(0), SH(KEYV), True)
        mm(A("B4", 256, 288), ID(ONE), CS(LIFTV))
        for d in range(8):
            mm(A("B4", 256, 288), A("bk", 128 * d, 128 * d + 128, key=d), A("eqv", 32 * d, 32 * d + 32))
        join(8)
        if chain:
            for p0 in range(16):
                mm(A("B4", 257, 288, 2), ID(K4), A("eqv", 256 + p0, 512, 16))
            ts(A("ofv", 0, 32, 2, key=0), A("B4", 256, 288, 2), C(DV), mn)
            ts(A("ofv", 1, 32, 2, key=1), A("B4", 257, 288, 2), C(DV2), mn)
            return
        if OPT["vmode"] == "merged":
            ts(A("ofcb", 2, 128, 4, key="v"), A("B4", 256, 288), C(DV), mn)
            return
        ts(A("ofv", 0, 64, 2), A("B4", 256, 288), C(DV), mn)
        for c in range(31, -1, -1):
            act(IN(A("TT", 0, 4112, key="v"), A("ofv", 2 * c, 2 * c + 1)), A("cv", 48 * c, 48 * c + 16, key=c // 8), AF.Silu)
            tags.setdefault((t, "TV"), []).append(tags[(t, "TT")].pop())

    def patchers(t):
        if OPT["vmode"] == "chain":
            return
        copy(OPT["tv"], A("tvf"), IN(A("TT", 0, 4096, key="v"), VU(t)))
        zv = A("B7", 96, 128)
        mm(zv, IH(0), SH(KEYV), True)
        mm(zv, ID(ONE), CS(LIFTV))
        mm(zv, ID(K4), CS(OWNH))
        f2w(zv, WD(ONESN), ("tvf", 0, None), False)
        tt(S(MNV), zv, S(DUMR), mn)
        cp(A("ofp"), S(MNV))

    def next_j(t, name, ef, bank, sign, out):
        mm(A(bank), ID(ONE), A("x%db" % t), True)
        mm(A(bank), ID(NEG), ef(0, 1))
        act(A(sign), A(bank), AF.Sign, 252.5, -1.0)
        mm(out, IH(0), SH(JUH), True)
        for p0 in range(16):
            mm(out, WD(JW)(16 - p0, 144 - p0), ef(p0, 16))
        join(16)
        f2w(out, WD(JW2), (sign, 0, None), False)

    def decide(t):
        of, last = "of%d" % t, t == NSTEP - 1
        for part in OPT["parts"]:
            nch, lo = len(part), min(part)
            c0, w = 8 * lo, 8 * nch
            keys = ["p%d" % q for q in part]
            W_ = lambda nm, j: A(nm, 32 * j + c0, 32 * j + c0 + w, key=["%d%s" % (j, k) for k in keys])
            ex = lambda a, b: A("expd", 64 * lo + a, 64 * lo + b, key=list(part))
            copy(OPT["expd"], ex(0, 64 * nch), IN(A("scan", 144 * lo, 144 * (lo + nch), key=list(part)), A("exu", 4 * nch - 4, 8 * nch - 4)))
            kb = A("B5", 128, 128 + 2 * w)
            mm(kb, ID(ONE), A("cst", 32 * CK, 32 * CK + 2 * w, key=CK), True)
            for gg in range(4):
                mm(kb, A("lw", 112 - 16 * gg, 240 - 16 * gg), ex(2 * w * gg, 2 * w * gg + 2 * w))
            for h in range(2):
                rows = slice(64 * h, 64 * h + 64)
                tt(A("smi", 96 + c0, 96 + c0 + w, key=["3p%d%s" % (ch, "ab"[h]) for ch in part], p=rows), A("B5", 128 + w * h, 128 + w * h + w, p=rows),
                   A("sm", 32 * CAND + c0, 32 * CAND + c0 + w, key=CAND, p=rows), mn)
            kp = A("smi", 96 + c0, 96 + c0 + w, key=["3p%d%s" % (ch, h) for ch in part for h in "ab"])
            cc, sw = W_("smi", 4), W_("smb", SW)
            ts(cc, kp, 0x2FFF, band)
            ts(sw, kp, D1, ge, 10240.0, mul)
            tt(A("key2", 2 * c0, 2 * c0 + 2 * w, 2, key=["c" + k for k in keys]), cc, sw, sub)
            tt(A("key2", 2 * c0 + 1, 2 * c0 + 2 * w, 2, key=["b" + k for k in keys]), A("smi", 64 + c0, 64 + c0 + w, key=2), sw, sub)
            ts(W_("smu", 2), cc, -8192.0, add)
            st = OPT["fill"] or w
            for c in range(c0 + w - st, c0 - 1, -st):
                copy(OPT["rc"], A("rc", 16 * c, 16 * (c + st), key="q%d" % c), IN(Rw, A("smu", 64 + c, 64 + c + st, key=W_("smu", 2)[1][0][4:])))
            k2 = A("key2", 2 * c0, 2 * c0 + 2 * w, key=[y + k for k in keys for y in "cb"])
            for d in range(8):
                mm(A("B6", 2 * w * d, 2 * w * d + 2 * w), A("dif", 128 * d, 128 * d + 128, key=d), k2, True)
            join(8)
            ts(A("eqd", 16 * c0, 16 * c0 + 16 * w, key=keys), A("B6", 0, 16 * w), 0.0, eq)
            back = A("B7", 64, 64 + 2 * w)
            mm(back, IH(0), k2, True)
            mm(back, ID(ONE), A("cst", 32 * LIFT, 32 * LIFT + 2 * w, key=LIFT))
            for d in range(8):
                mm(back, A("bk", 128 * d, 128 * d + 128, key=d), A("eqd", 16 * c0 + 2 * w * d, 16 * c0 + 2 * w * d + 2 * w, key=keys))
            join(8)
            for y, dum in ((0, DC), (1, DB)):
                ts(A("ofcb", 4 * c0 + y, 4 * c0 + 4 * w, 4, key=["cb"[y] + k for k in keys]), A("B7", 64 + y, 64 + 2 * w, 2), C(dum), mn)
            for c in range(c0 + w - 1, c0 - 1, -1):
                act(IN(A("TT", TB, None, key="cb" if TB else None), A("ofcb", 4 * c, 4 * c + NK, key=[y + k for k in keys for y in "cb"] + ["v"] * (NK - 2))),
                    A("cv", 48 * c, 48 * c + 16 * NK, key=c // 8), AF.Silu)
            if not last and OPT["prej"]:
                for c in range(c0 + w - st, c0 - 1, -st):
                    copy(OPT["yu"], A("yu", 16 * c, 16 * (c + st), key="q%d" % c), IN(A("EF"), A("smu", 64 + c, 64 + c + st, key=W_("smu", 2)[1][0][4:])))
        allp = lambda j: ["%d%s" % (j, k) for k in PARTKEYS]
        K = A("smi", 96, 128, key=["3p%d%s" % (ch, h) for ch in range(4) for h in "ab"])
        CC, CU, SWA = A("smi", 128, 160, key=allp(4)), A("smu", 64, 96, key=allp(2)), A("smb", 32 * SW, 32 * SW + 32, key=allp(SW))
        cf, dl, may = A("d1", 1, 64, 2, key=1), A("d0", 1, 64, 2, key=1), A("d1", 0, 64, 2, key=0)
        prej = not last and OPT["prej"]
        if prej:
            ju = A("d1", 65, 128, 2, key=3)
            next_j(t, "u", lambda a, s: A("yu", a, 512, s), "B7", "hu", A("B7", 0, 32))
            cp(ju, A("B7", 0, 32))
            tt(S(JD), S(JN), ju, sub)
        act(A("tcb", 0, 512, key=0), IN(A("TT", 4608, 8704, key="cb"), CU), AF.Copy)
        copy(OPT["tb"], A("tcb", 512, 1024, key=1), IN(A("TT", 8704, 9216, key="cb"), SUU(0)))
        patchers(t)
        ts(SB(NTG), K, C(LIM), ge)
        ts(SB(NTP), K, C(LIM), ge, 8192.0, mul)
        if OPT["vw"] == "act":
            ts(SB(NTN), K, C(LIM), ge, -8192.0, mul)
        ts(cf, CC, -8192.0, add)
        tt(S(NC), S(NT + t), CC, sub)
        tt(dl, S(NC), SB(NTG), mul)
        if prej:
            tt(A("d0", 65, 128, 2, key=3), S(JD), SB(NTG), mul)
        tt(SH(TGT), A("key2", 0, 64, 2, key=["c" + k for k in PARTKEYS]), dl, add)
        tt(S(CG), cf, SB(NTP), add)
        mm(A("B4"), ID(ONE), A("x%db" % t), True)
        w2f("B4", "wsel", SB(NTG))
        tt(A("eqc"), A("rc"), A("B4"), eq)
        if OPT["val"] == "act":
            mm(A("B4"), ID(ONE), A("x%db" % t), True)
            mm(A("B4"), ID(K256), A("eqc"))
            act(A("val"), A("B4"), AF.Relu, -256.0)
        else:
            tt(A("val"), A("eqc"), A("B4"), mul)
        for ch in range(4):
            mm(A("B%d" % ch, 128, 384), A("eqc", 128 * ch, 128 * ch + 128), A("wexp"))
        ts(A("sch"), IN(SUw, CU), 1.0 / 256, mul, -2048.0, add)
        for ch in range(4):
            ek = A("ei", 256 * ch, 256 * ch + 256, key=ch)
            ts(ek, A("B%d" % ch, 128, 384), 21845.0, add)
            ts(ek, ek, 0xAAAA, band)
            tt(A("z", 128 * ch, 128 * ch + 128, key=ch), A("ei", 256 * ch, 256 * ch + 128, key=ch), A("ei", 256 * ch + 128, 256 * ch + 256, key=ch), add)

        def kept(bank, flag, ident, first):
            w2f(bank, "seld", flag, first)
            for ch in range(4):
                mm(A(bank, 128 * ch, 128 * ch + 128), A("z", 128 * ch, 128 * ch + 128, key=ch), ident)

        if OPT["vw"] == "act":
            for bank, flag, ident in (("B6", SB(NTG), ID(K4)), ("B3", SB(NTN), ID(N8K))):
                mm(A(bank), ID(ONE), A("c2112"), True)
                w2f(bank, "wselh", SH(TGT))
                kept(bank, flag, ident, False)
            tt(A("nv1"), A("verf"), A("B6"), mn)
            tt(A("nv2"), A("nv1"), A("B3"), mx)
        else:
            kept("B6", SB(NTG), ID(K4), True)
            act(A("eat"), A("B6"), AF.Relu, 1.0, -1.0)
            mm(A("B3"), IH(3), A("verh"), True)
            w2f("B3", "wselh", SH(TGT))
            tt(A("nv2"), A("eat"), A("B3"), mul)
        zn = A("B5", 256, 288)
        mm(zn, ID(K4), CS(CZ), True)
        mm(zn, ID(N8K), SWA)
        mm(zn, ID(K4), CS(OWN))
        f2w(zn, WD(ONESN), ("tcb", 0, 0), False)
        f2w(zn, WD(ONESN), ("tcb", 512, 1), False)
        ts(may, zn, 4096.0, lt)
        if not prej:
            scan(A("vs", 0, 64), A("d0", 0, 64, key=[0, 1]), A("d1", 0, 64, key=[0, 1]), 0.0, mul, add)
            cp(A(of, 0, 32, key=0), A("vs", 1, 64, 2))
        else:
            ts(A("d1", 64, 128, 2, key=2), zn, 4096.0, lt)
            scan(A("vs"), A("d0"), A("d1"), 0.0, mul, add)
            cp(A(of, 0, 64), A("vs", 1, 128, 2))
        tt(SB(CL), zn, SB(NTP), lt)
        tt(A("a3", 0, 32, key=0), zn, S(CG), add)
        tt(A("a3", 32, 64, key=1), zn, S(BF_), add)
        w = 64
        if OPT["rclone"] == "act":
            tt(S(NG), S(NT + t), SB(NTP), sub)
            tt(A("a3", 64, 96, key=2), zn, S(NG), add)
            w = 96
        tt(A("a3", 0, w), A("a3", 0, w), A("dum3", 0, w), mn)
        cp(A("og", 0, w), A("a3", 0, w))

    def writes(t):
        x, of = "x%db" % t, "of%d" % t
        last = t == NSTEP - 1
        hop = HOP if not last else -HOP * t
        dst, src = T.cores[(rank + hop) % n_r], T.cores[(rank - hop) % n_r]
        vn = A(of, 0, 32, key=0)
        apart = last or (OPT["early"] and not OPT["prej"])
        if apart:
            send(vn, VU(t + 1), dst, src, "av%d" % (t + 1), 1.8)
        act(A("efg"), IN(A("EF"), vn), AF.Copy)
        if last or OPT["prej"]:
            mm(A("B7"), ID(ONE), A(x), True)
            mm(A("B7"), ID(NEG), A("efg"))
            act(A("sg"), A("B7"), AF.Sign, 252.5, -1.0)
        else:
            next_j(t, "u", lambda a, s: A("efg", a, 512, s), "B7", "sg", A("B5", 288, 320))
            cp(A(of, 32, 64, key=1), A("B5", 288, 320))
        if not apart:
            send(A(of), A("v%du" % (t + 1)), dst, src, "av%d" % (t + 1), 1.8)
        elif not last:
            send(A(of, 32, 64, key=1), JU(t + 1), dst, src, "aj%d" % (t + 1), 1.8)
        mm(A("B6"), ID(ONE), A(x), True)
        mm(A("B6"), ID(NEG), A("efg"))
        mm(A("B6"), ID(TWO), A("sg"))
        if last:
            act(A("xo%d" % t), A("B6"), AF.Identity, 254.0, -1.0)
        else:
            act(A("xo%d" % t), A("B6"), AF.Identity, 2.0)
        sx = send(A("xo%d" % t), A("x%db" % (t + 1)), dst, src, "ax%d" % (t + 1), 2.3)
        su_t = A("SU", t, 4096, 8)
        mm(A("B1"), IH(2), A("sch"), True)
        w2f("B0", "wsel", SB(CL), True)
        tt(su_t, su_t, A("B0"), sub)
        w2f("B1", "wsel", SB(CL))
        tt(su_t, su_t, A("B1"), mx)
        tt(A("vm"), IN(A("ENC"), vn), A("mask%d" % (t % 2)), sub)
        if OPT["vmode"] == "chain":
            for h in (1, 0):
                tt(A("pg", 256 * h, 256 * h + 256, key=h), IN(SUw, VU(t, 16 * h, 16 + 16 * h)), A("mask%d" % (t % 2), 256 * h, 256 * h + 256), mn)
            for q in range(15, -1, -1):
                tt(IN(A("SU"), A("ofv", 2 * q, 2 * q + 2)), A("pg", 32 * q, 32 * q + 32, key=q // 8), A("vm", 32 * q, 32 * q + 32), mx)
        else:
            tt(A("pg"), IN(SUw, VU(t)), A("mask%d" % (t % 2)), mn)
            tt(IN(A("SU"), A("ofp")), A("pg"), A("vm"), mx)
        act(IN(A("R"), A("og", 0, 32)), A("val"), AF.Silu)
        if OPT["vw"] == "act":
            act(IN(A("VL"), A("og", 32, 64)), A("nv2"), AF.Silu)
        else:
            tt(IN(A("VL"), A("og", 32, 64)), A("verf"), A("nv2"), add)
        if OPT["rclone"] == "act":
            act(A("keyl"), A(x), AF.Copy)
            act(IN(A("R"), A("og", 64, 96)), A("keyl"), AF.Silu)
        else:
            r_t = A("R", t, 4096, 8)
            mm(A("B2"), ID(ONE), A(x), True)
            mm(A("B2"), ID(ONE), A("cneg"))
            w2f("B2", "wsel", SB(CL))
            tt(r_t, r_t, A("B0"), sub)
            tt(r_t, r_t, A("B2"), mx)
        if not last:
            seld(t + 1, False)
            for o in ops[-2:]:
                o["after"].append(sx)
            mm(A("B5", 320, 352), A("blk"), SB(CL), True)
            red(C(ACNT), A("B5", 320, 352))
            cp(A("coli", 2, 3, key=4), C(ACNT))
            ts(A("coli", 3, 4, key=5), A("coli", 2, 3, key=4), 1, band)
            ts(C(LIM), A("coli", 3, 4, key=5), D1, mul, 3 * D1, add)

    for t in range(NSTEP):
        step[0] = t
        edge(t)
        main(t)
        decide(t)
        writes(t)
    step[0] = NSTEP

    def named(t, word):
        if "~" in word:
            lists = [named(t, w) for w in word.split("~")]
            return [l[m] for m in range(max(len(l) for l in lists)) for l in lists if m < len(l)]
        if "," in word:
            return [i for w in word.split(",") for i in named(t, w)]
        name, _, rng = word.partition(".")
        calls = tags.get((t + name.startswith("+"), name.lstrip("+")), [])
        a, _, b = rng.partition("-")
        return calls[int(a):int(b or a) + 1] if rng else calls

    seq = []
    for t in range(NSTEP):
        words = OPT["head"][min(t, 1)] + " " + OPT["body"] + " " + OPT["tail"][t == NSTEP - 1]
        seq += [i for word in words.split() for i in named(t, word)]
    for a, b in zip(seq, seq[1:]):
        ops[b]["soft"].append(a)
    ops[seq[0]]["soft"] += [i for k, v in tags.items() if k[0] < 0 and k[1] in ("wg", "we", "x0b") for i in v]
    for h in range(2):
        sums, out = "B%d" % (4 + h), A("B%d" % (6 + h), 0, 128)
        for ch in range(16):
            mm(A(sums, ch, 128, 16), A("SU", 2048 * h + 128 * ch, 2048 * h + 128 * ch + 128), A("oneswf", 16, 144, 16), True)
        join(16, 4)
        part = lambda nm, j: A(nm, 256 * h + 128 * j, 256 * h + 128 * j + 128, key=2 * h + j)
        ts(part("sci", 0), A(sums, 0, 128), 1.0 / 256, mul, -0.25, add)
        act(part("keyl", 0), A(sums, 0, 128), AF.Copy)
        cp(part("keyl", 1), part("sci", 0))
        mm(out, part("keyl", 0), IF(1), True)
        mm(out, part("keyl", 1), IF(2))
        mm(out, part("keyl", 1), IF(0))
        ts(A("pg", 128 * h, 128 * h + 128, key="s%d" % h), out, 65536.0, add)
    for q in range(4):
        if q < OPT["nact"]:
            act(RQ(q), A("R", 1024 * q, 1024 * q + 1024), AF.Relu, -247.0)
        else:
            ts(RQ(q), A("R", 1024 * q, 1024 * q + 1024), -247.0, add, 0.0, mx)
        ts(RQ(q), RQ(q), -1.0, mul, 9.0, add)
    if VOFF:
        ts(A("ei", 0, 512), A("VL", 0, 512), -VOFF, add)
        cp(A("verf"), A("ei", 0, 512))
    ts(SH(KEYV), VU(NSTEP), -2048.0, add)
    w2f("B3", "wselh", SH(KEYV), True, 8)
    act(A("sel", p=r8), A("B3", p=r8), AF.Identity, 2048.0)
    for m, q in enumerate(OPT["rout"]):
        dma("sp", (T["yr"][:, 1024 * q:1024 * q + 1024], [], []), RQ(q), "out", 5.6 - 0.8 * m)
    dma("act", H("yv"), A("sel", p=r8), "out", 2.0)
    dma("act", H("yx"), A("x4b"), "out", 2.5)
    dma("sp", H("yl"), A("verf") if VOFF else A("VL", 0, 512), "out", 2.8)
    for h in range(2):
        dma("sp", (T["ys"][:, 2048 * h:2048 * h + 2048], [], []), A("pg", 128 * h, 128 * h + 128, key="s%d" % h), "out", 2.2)

    def hit(a, b):
        return a == b or a.split("#")[0] == b or b.split("#")[0] == a

    lastw, readers, group = {}, {}, {}
    for i, o in enumerate(ops):
        if o["dma"]:
            group.setdefault(o["dma"], []).append(i)
    for i, o in enumerate(ops):
        deps = set()
        for k in o["rd"]:
            base = k.split("#")[0]
            deps.update(j for k2, j in lastw.get(base, {}).items() if hit(k, k2))
            if SCRATCH[base][0] == "psum":
                deps.update(j for j in readers.get(base, {}).get(base, []) if ops[j]["e"] != o["e"])
        for k in o["wr"]:
            base = k.split("#")[0]
            deps.update(j for k2, j in lastw.get(base, {}).items() if hit(k, k2))
            for k2, js in readers.get(base, {}).items():
                if hit(k, k2):
                    deps.update(js)
        if o["ext"] == "arr" or (o["dma"] and o["dma"] == "dtt"):
            deps = set(j for j in deps if o["ext"] is None and ops[j]["dma"] != o["dma"])
        deps.discard(i)
        for j in list(deps):
            if ops[j]["dma"]:
                deps.update(group[ops[j]["dma"]])
        o["sync"] = [j for j in deps if ops[j]["ext"] != "send" and not (ops[j]["e"] == "pe" and o["e"] == "pe")]
        o["need"] = deps
        o["all"] = sorted(deps.union(o["after"]))
        for k in o["wr"]:
            base = k.split("#")[0]
            d = lastw.setdefault(base, {})
            r = readers.setdefault(base, {})
            if k == base:
                d.clear()
                r.clear()
            r.pop(k, None)
            d[k] = i
        for k in o["rd"]:
            readers.setdefault(k.split("#")[0], {}).setdefault(k, []).append(i)
    if "order" not in ORDER:
        ORDER["order"] = schedule(ops)
    order = ORDER["order"]
    pos = {i: n for n, i in enumerate(order)}
    seen = {e: {} for e in Q}
    for i in order:
        o = ops[i]
        if o["e"] is None:
            continue
        keep = {}
        for j in o["sync"]:
            s = ops[j]["dma"] or ops[j]["e"]
            if s not in keep or pos[j] > pos[keep[s]]:
                keep[s] = j
        sn = seen[o["e"]]
        o["deps"] = {s: j for s, j in keep.items() if sn.get(s, -1) < pos[j]}
        for s, j in o["deps"].items():
            sn[s] = len(ops) if ops[j]["dma"] else pos[j]
            ops[j]["inc"] = True
    total = {}
    for i in order:
        o = ops[i]
        if o["dma"]:
            total[o["dma"]] = total.get(o["dma"], 0) + o["n"]
        elif o["ext"] == "send":
            total["sent"] = total.get("sent", 0) + o["n"]
        elif o["inc"]:
            total[o["e"]] = total.get(o["e"], 0) + 1
            o["cnt"] = total[o["e"]]
    for i in order:
        o = ops[i]
        if o["e"] is None:
            continue
        for s, j in o["deps"].items():
            Q[o["e"]].wait_ge(T.sem[s], total[s] if ops[j]["dma"] else ops[j]["cnt"])
        ins = o["fn"]()
        if o["dma"]:
            ins.then_inc(T.sem[o["dma"]], 16)
        elif o["inc"]:
            ins.then_inc(T.sem[o["e"]], 1)
    for s, n in total.items():
        g.wait_ge(T.sem[s], n)
